import numpy as np, ml_dtypes
CORES = [48,51,52,55]
N = 4
BF = ml_dtypes.bfloat16
def gentries(a):
    return np.ascontiguousarray(a.reshape(8, 16, -1).transpose(0, 2, 1)).reshape(8, -1)
def gtable(e):
    e = np.asarray(e); return np.ascontiguousarray(e.reshape(8, -1, 16).transpose(0, 2, 1)).reshape(128, -1).astype(np.int32)
B, J, CAP, RO, Q = 3328, 4096, 64, 3, 4096
LN, LJ = 2, 12
M = N * CAP; W = B + RO * M
WT = (14 * np.arange(16) + 9)[:, None]
def decode(n):
    C = np.add.accumulate((n * n[..., ::-1]) >> 12, axis=-1)
    x = (C[..., -1:] * np.arange(J)) >> LJ
    return np.add.reduce((C[..., None] <= x[..., None, :]).astype(np.int64), axis=-2)
def combine(x, y, z):
    q = x.shape[-1] // 4
    k = np.concatenate([np.minimum(x[..., :q], y[..., :q]), np.maximum(x[..., q:2 * q], y[..., q:2 * q]), np.abs(x[..., 2 * q:3 * q] - y[..., 2 * q:3 * q]), x[..., 3 * q:] + y[..., 3 * q:]], axis=-1)
    return np.minimum(k, z)
def sizes(c):
    c = np.sort(c, axis=-1); z = np.zeros(c.shape[:-1] + (1,), np.int64)
    return np.diff(np.concatenate([z, c, z + B - 256], axis=-1), axis=-1) + 64
def span(rng, v, share):
    o = rng.integers(0, B, (3, N, 8, 1, 2048)); x, y, z = [np.take_along_axis(v, i, 3) for i in o]
    s = np.sort(np.add.reduce(combine(x, y, z), axis=2), axis=-1)
    m = np.minimum(np.maximum((2048 * share).astype(np.int64), 1), 2048); k = (rng.random((N, 8)) * (2048 - m)).astype(np.int64)
    return np.concatenate([np.take_along_axis(s, k[..., None], 2), np.take_along_axis(s, (k + m - 1)[..., None], 2)], axis=2)
def shares(rng):
    return CAP * N * 2.0 ** -LJ * rng.choice(np.array([0.4, 0.8, 1.0, 1.5]), (N, 8))
def parts(rng):
    e = rng.choice(np.array([0.5, 1.0, 1.0, 2.0]), (N, 8, 16, 1))
    v = np.minimum((256 * rng.random((N, 8, 16, B)) ** e).astype(np.int64), 255)
    n = sizes(rng.integers(0, B - 255, (N, 8, 3))); r = rng.integers(0, 4096, (3, N, 8, RO, J))
    u = (rng.random((N, 8, Q)) < rng.choice(np.array([0.05, 0.2, 0.5]), (N, 8, 1))).astype(np.int64)
    return v, n, span(rng, v, shares(rng)), r, u
def pack(v, n, lim, r, u):
    t = [np.stack([gtable(a.reshape(8, -1)) for a in b]) for b in r]
    return {"bank": np.ascontiguousarray(v.reshape(N, 128, B)).astype(np.float32).astype(BF), "ncl": n.astype(np.int32), "lim": lim.astype(np.int32),
            "ra": t[0], "rb": t[1], "rc": t[2], "used": u.astype(np.int32)}
def goals(rng, k):
    return np.stack([rng.permutation(Q - 1)[:k] + 1 for p in range(N)]) * N + np.arange(N)[:, None]
def keyed(rng, d):
    c = rng.integers(1, 256, (16, d.size)); c[[0, 1, 15]] = rng.integers(40, 101, (3, d.size))
    e = (d - np.add.reduce(c * WT, axis=0)) & (N * Q - 1)
    c[15] += e // 219; e = e % 219; c[0] += e // 9 - 5 * (e % 9); c[1] += 2 * (e % 9)
    return c
def put(rng, v, n, q, g, d):
    s = np.add.accumulate(n[q, g]) - n[q, g]; v[q, g][:, s] = 255; v[q, g][:, s + 1] = 0
    w = rng.permutation(np.setdiff1d(np.arange(B), np.concatenate([s, s + 1])))[:d.size]
    v[q, g][:, w] = keyed(rng, d.reshape(-1)); return w.reshape(d.shape)
def deal(rng, col, at, w):
    o = rng.permutation(np.repeat(np.arange(N), CAP)); at = np.sort(rng.permutation(at)[:M])
    for p in range(N): col[at[o == p]] = w[p]
def play(r, n, q, g, t, col):
    h = J // 4; k = B + t * M; r[:2, q, g, t] = 0; r[2, q, g, t] = (col * 4096 + k - 1) // k
    if t == 0:
        m = n[q, g][3 - decode(n[q, g])[2 * h:3 * h]]; r[1, q, g, 0, 2 * h:3 * h] = (4096 + m - 1) // m
def setup_inputs(rng):
    return pack(*parts(rng))
def setup_inputs_room(rng):
    v, n, lim, r, u = parts(rng); lim[:] = (1500, 2600)
    for q in range(N):
        for g in range(8):
            m = n[q, g]; p = np.concatenate([np.arange(k) for k in m]); live = p >= np.repeat(m // 2, m)
            c = np.where(live, rng.integers(110, 150, (16, B)), rng.integers(0, 90, (16, B)))
            c[0] += (p - np.add.reduce(c * WT, axis=0)) & (N - 1)
            c[:, p == 0] = 0; c[:, p == 1] = 255; v[q, g] = c
            t = rng.choice(np.array([0, 1, CAP - 1, CAP, CAP + 1, 2 * CAP]), N)
            if q == 0: t[1] = (CAP, CAP + 1, CAP - 1, CAP, 0, 1, 2 * CAP, CAP)[g]
            if g == 6: t[2] = 0
            own = np.full(J, -1); own[rng.permutation(J)[:int(np.sum(t))]] = rng.permutation(np.repeat(np.arange(N), t))
            a = decode(m); na = m[a]; nb = m[3 - a]; h = na // 2
            dead = 2 + (rng.random(J) * (h - 2)).astype(np.int64)
            good = h + (own - h) % N + N * (rng.random(J) * ((na - h - N) // N + 1)).astype(np.int64)
            i = np.where(own < 0, dead, good); y = (np.arange(J) < J // 4).astype(np.int64)
            r[0, q, g, 0] = (i * 4096 + na - 1) // na; r[1, q, g, 0] = (y * 4096 + nb - 1) // nb; r[2, q, g, 0] = (4096 + B - 1) // B
    return pack(v, n, lim, r, u)
def setup_inputs_ends(rng):
    v, n, lim, r, u = parts(rng); v[..., 0] = 0; v[..., B - 1] = 255
    for g in range(4):
        n[:, g] = 64; n[:, g, g] = B - 192
    n[:, 5] = n[:, 2]; lim[0, 5] = (1, 4080)
    for g in (0, 2, 4): r[:, :, g] = rng.choice(np.array([0, 1, 4094, 4095]), (3, N, RO, J))
    lim[:, 0] = (0, 4080); lim[:, 2] = (4080, 4080); lim[:, 4] = (0, 0); lim[:, 6, 0] = lim[:, 6, 1]
    r[:, :, 2, 0, J - 1] = 4095; r[2, :, 4, 0, :8] = 0; u[:, 2] = 0; u[:, 4] = 0
    r[2, :, 0, 0, :8] = 0; u[:, 0] = 0
    lim[:, 1] = (1, 4080); lim[:, 3] = (1, 4080); lim[:, 7] = (0, 4079); u[:, 1] = 0; u[:, 3] = 0; u[:, 7] = 0
    full = goals(rng, RO * M).reshape(N, RO, N, CAP)
    grid = goals(rng, M).reshape(N, N, CAP); grid[1:, N - 1, CAP - 1] = grid[1:, 0, 0]
    many = goals(rng, 2 * CAP); at = np.concatenate([np.arange(J // 4, J // 2), np.arange(3 * J // 4, J)])
    for q in range(N):
        w = put(rng, v, n, q, 3, full[:, :, q])
        for t in range(RO):
            col = np.full(J, 1); deal(rng, col, at, w[:, t]); play(r, n, q, 3, t, col)
        i = J // 8 + rng.permutation(J // 8)[:4]; r[0, q, 3, RO - 1, i] = rng.integers(1000, 4096, 4); r[2, q, 3, RO - 1, i] = 0
        w = put(rng, v, n, q, 7, grid[:, q])
        if q == N - 1: w[0, CAP - 1] = 1
        col = np.zeros(J, np.int64); deal(rng, col, np.arange(J), w); play(r, n, q, 7, 0, col)
        w = put(rng, v, n, q, 1, many[(q + 1) % N]); col = np.full(J, 1); k = J // 4
        if q > 0: k += int(rng.integers(0, CAP))
        i = np.sort(rng.permutation(J // 2)[:k]); col[i] = w[rng.integers(0, CAP, k)]; col[i[:CAP]] = w[:CAP]
        col[J // 2 + rng.permutation(J // 2)[:2 * CAP]] = np.tile(w[CAP:], 2); play(r, n, q, 1, 0, col)
    return pack(v, n, lim, r, u)
def setup_inputs_alike(rng):
    v, n, lim, r, u = parts(rng)
    a = rng.integers(1, 255, (8, 16, 3)); tw = np.zeros((16, 1), np.int64); tw[:4, 0] = (1, -1, -1, 1)
    pool = np.concatenate([a, a + tw], axis=2)
    for g in range(1, 8, 2):
        v[:, g] = pool[g][:, rng.integers(0, 6, (N, B))].transpose(1, 0, 2)
        for q in range(N):
            e = np.add.accumulate(n[q, g]); v[q, g][:, e - n[q, g]] = pool[g][:, :1]; v[q, g][:, e - 1] = pool[g][:, 3:4]
    lim[:, 1::2] = (0, 4080); u[:, 1::2] = 0; r[:, :, 1::2, 0, 0] = 0; r[:, :, 1::2, 0, 1] = 4095
    v[:, 2] = v[0, 2]; n[:, 2] = n[0, 2]; lim[:, 2] = lim[0, 2]; r[:, :, 2] = r[:, :1, 2]
    return pack(v, n, lim, r, u)
def setup_inputs_cold(rng):
    v, n, lim, r, u = parts(rng); o = rng.permutation(N); g = int(rng.integers(0, 8))
    lim[o[0]] = (1, 0); lim[o[0], 1::2] = (1600, 1000); lim[o[1]] = (0, 4080)
    lim[:, g] = (1700, 1100); lim[o[0], g] = (2000, 1999); lim[o[1], g] = (4080, 0); u[:, (g + 1) % 8] = 1; u[:, (g + 2) % 8] = 0
    u[o[2], (g + 3) % 8] = 1
    return pack(v, n, lim, r, u)
def setup_inputs_spread(rng):
    v, n, lim, r, u = parts(rng)
    v = np.minimum((np.exp2(8 * rng.random((N, 8, 1, B))) * rng.random((N, 8, 16, B))).astype(np.int64), 255)
    n = sizes(((B - 256) * rng.random((N, 8, 3)) ** 4).astype(np.int64))
    e = rng.choice(np.array([0.5, 1.0, 2.0, 3.0]), (3, N, 8, RO, 1)); r = np.minimum((4096 * rng.random((3, N, 8, RO, J)) ** e).astype(np.int64), 4095)
    u = (rng.random((N, 8, Q)) < 0.8 * rng.random((N, 8, 1))).astype(np.int64)
    return pack(v, n, span(rng, v, shares(rng)), r, u)
def check_inputs(d):
    bad = []; b = np.asarray(d["bank"]).astype(np.float32)
    if not np.all((b >= 0) & (b <= 255) & (b == np.floor(b))): bad.append("bank: whole numbers from 0 to 255")
    for k, lo, hi in (("ncl", 64, B), ("lim", 0, 4080), ("ra", 0, 4095), ("rb", 0, 4095), ("rc", 0, 4095), ("used", 0, 1)):
        if np.min(d[k]) < lo or np.max(d[k]) > hi: bad.append("range of " + k)
    if np.any(np.sum(np.asarray(d["ncl"]).astype(np.int64), axis=-1) != B): bad.append("sums of ncl")
    return bad
def reference(bank, ncl, lim, ra, rb, rc, used):
    v = np.zeros((N, 8, 16, W), np.int32); v[..., :B] = bank.astype(np.float32).astype(np.int32).reshape(N, 8, 16, B)
    n = np.zeros((N, 8, 4 + RO), np.int64); n[:, :, :4] = ncl
    la, lb, lc = [np.stack([gentries(a) for a in b]).astype(np.int64).reshape(N, 8, RO, J) for b in (ra, rb, rc)]
    free = used == 0; lo = lim[:, :, :1]; hi = lim[:, :, 1:]; take = np.take_along_axis
    for t in range(RO):
        s = 4 + t; m = n[:, :, :s].copy(); start = np.add.accumulate(m, axis=2) - m; tot = np.add.reduce(m, axis=2)
        a = decode(m); b = s - 1 - a
        ix = take(start, a, 2) + ((take(m, a, 2) * la[:, :, t]) >> 12)
        iy = take(start, b, 2) + ((take(m, b, 2) * lb[:, :, t]) >> 12)
        iz = (tot[:, :, None] * lc[:, :, t]) >> 12
        x, y, z = [take(v, i[:, :, None, :], 3) for i in (ix, iy, iz)]
        k = combine(x, y, z)
        total = np.add.reduce(k, axis=2); key = np.add.reduce(k * WT, axis=2)
        alive = (total >= lo) & (total <= hi); owner = key & (N - 1); bucket = (key >> LN) & (Q - 1)
        for p in range(N):
            for g in range(8):
                got = [np.flatnonzero(alive[q, g] & (owner[q, g] == p))[:CAP] for q in range(N)]
                c = np.concatenate([k[q, g][:, got[q]] for q in range(N)], axis=1); bu = np.concatenate([bucket[q, g, got[q]] for q in range(N)])
                first = np.sort(np.unique(bu, return_index=True)[1])
                keep = first[free[p, g, bu[first]]]; e = int(tot[p, g])
                v[p, g][:, e:e + len(keep)] = c[:, keep]; free[p, g, bu[keep]] = False; n[p, g, s] = len(keep)
    return {"y": np.ascontiguousarray(v[..., B:]).reshape(N, 128, RO * M).astype(np.float32).astype(BF)}

@@ -1,0 +1,550 @@
+import numpy as np
+from concourse.bass import DstId, RemoteDMATransfer
+from concourse.mybir import dt, AluOpType as A, AxisListType, ActivationFunctionType as F
+
+B, J, CAP, RO, Q, N = 3328, 4096, 64, 3, 4096, 4
+TR = 4096
+DUM = 288
+M23 = 8388608.0
+M27 = 201326592.0
+EPS = 2.0 ** -13
+
+SCRATCH = {}
+
+
+def _sb(dtype, **kw):
+    for n, w in kw.items():
+        SCRATCH[n] = ("sbuf", [128, w], dtype)
+
+
+_sb("bfloat16", BANK=TR + 256, CAND=J + DUM, TX=J, TY=J, TZ=J, USED=TR + 256, ONE256=256, FM=1024, SC=1024, I1=256, I2=256,
+    UG=256, E=2048, XP=256, XS=272, SEND0=256, SEND1=256, SEND2=256, LAND0=256, LAND1=256, LAND2=256, BO=128, BO16=128,
+    BO256=128, NBO=128, IDN=128, NID=128, ID4=128, UP=128, NU=128, SU=128, WB=128, LS=2048, WKF=2048, WT=16, KP=256, MK2=256,
+    rowg=128, rowl=128, rowk=128, rowh=128, R256=256, sB=64, IOC=258, JLC=128, AL=258, GM=128, LT=1024, X1=256, X2=256, OB=256)
+_sb("float32", sR=256, IC0=256, cols=64, RN=8, ra8=8, AS=8, M0=8, M1=8, AA=8, AB=8, T8=32, T9=32, PRE=16, HL=16, DD=16, I16=16, TB=16,
+    TI=16, NK=16, C16=16, C256=16, W1T=64, W2S=72, W3S=1040, PK1=256, SEL8=128, NF=8, LX=256, LOT=128, HIT=128,
+    TRI=128, TRIS=128, ONE=128, ONES=128, rk6=128, F1=128, F1b=128, ZT=256, RCF=256, XT=256, YT=256, BC=16, NV=16, PO=16)
+_sb("int32", RA=768, RB=768, RC=768, ip=8, NI=8, WI=4, KI=256, OW=256, KRI=256, BRI=256, KBI=16, BBI=16)
+_sb("uint16", XO=256, YO=256, ZO=256, O1=16, O2=16, O3=16, UO=16, SO=16, UO2=16, BR=256)
+SCRATCH["UD"] = ("dram", [8, 4096], "bfloat16")
+for _b in range(8):
+    SCRATCH["P%d" % _b] = ("psum", [128, 512], "float32")
+
+SEMAPHORES = ["cV", "cS", "cP", "cG"] + ["d%d" % i for i in range(12)] + ["dU", "arr0", "arr1", "arr2", "snt0", "snt1", "snt2"]
+
+
+def rank_program(g, core, T, topo):
+    rank = T.rank_of(core)
+    if rank is None:
+        return
+    queue = {"V": g.vector, "S": g.scalar, "P": g.tensor, "G": g, "Y": g.sync}
+    count, snap, recs, names, nd = {}, {}, {}, {}, [0]
+    known = {q: {} for q in queue}
+
+    def psum(b):
+        return b[0] == "P" and b[1:].isdigit()
+
+    def deps(q, reads, writes):
+        need = {}
+        for lst, w in ((reads, False), (writes, True)):
+            for b, lo, hi in lst:
+                for r in recs.get(b, []):
+                    if psum(b):
+                        if r[4] == q and (q == "P" or r[0] >= hi or r[1] <= lo or not (w or r[2])):
+                            continue
+                    elif r[0] >= hi or r[1] <= lo or not (w or r[2]):
+                        continue
+                    need[r[3][0]] = max(need.get(r[3][0], 0), r[3][1])
+        for s, v in need.items():
+            if known[q].get(s, 0) < v:
+                queue[q].wait_ge(T.sem[s], v)
+                known[q][s] = v
+        for s, v in need.items():
+            for s2, v2 in snap.get((s, v), {}).items():
+                known[q][s2] = max(known[q].get(s2, 0), v2)
+
+    def note(q, reads, writes, tok, remote=False):
+        snap[tok] = {} if remote else dict(known[q])
+        for b, lo, hi in writes:
+            recs[b] = [r for r in recs.get(b, []) if not (r[0] >= lo and r[1] <= hi)] + [(lo, hi, True, tok, q)]
+        for b, lo, hi in reads:
+            keep = [r for r in recs.get(b, []) if r[2] or r[4] != q or not (r[0] >= lo and r[1] <= hi)]
+            recs[b] = keep + [(lo, hi, False, tok, q)]
+
+    def do(q, fn, reads, writes):
+        deps(q, reads, writes)
+        s = "c" + q
+        count[s] = count.get(s, 0) + 1
+        fn().then_inc(T.sem[s], 1)
+        note(q, reads, writes, (s, count[s]))
+
+    def mm(lst):
+        reads = [x[3][:3] for x in lst] + [x[4][:3] for x in lst]
+        writes = [x[:3] for x in lst]
+        deps("P", reads, writes)
+        last = None
+        for x in lst:
+            o, c0, c1, lh, rh, st, sp = x[:7]
+            kp = rh[4] if len(rh) > 4 else 128
+            lv = T[lh[0]][0:kp, lh[1]:lh[2]:lh[3] if len(lh) > 3 else 1]
+            rv = T[rh[0]][0:kp, rh[1]:rh[2]:rh[3] if len(rh) > 3 else 1]
+            last = g.tensor.matmul(T[o][:, c0:c1:x[7] if len(x) > 7 else 1], lv, rv, st, sp)
+        count["cP"] = count.get("cP", 0) + 1
+        last.then_inc(T.sem["cP"], 1)
+        note("P", reads, writes, ("cP", count["cP"]))
+
+    def dma(q, out, in_, reads, writes, sem=None):
+        deps(q, reads, writes)
+        if sem is None:
+            sem = "d%d" % nd[0]
+            nd[0] += 1
+        queue[q].dma_start(out, in_).then_inc(T.sem[sem], 16)
+        count[sem] = count.get(sem, 0) + 16
+        note(q, reads, writes, (sem, count[sem]))
+
+    def ap(r):
+        return T[r[0]][:, r[1]:r[2]:r[3]] if len(r) > 3 else T[r[0]][:, r[1]:r[2]]
+
+    def pair(x):
+        return isinstance(x, tuple) and isinstance(x[0], tuple)
+
+    def regs(*xs):
+        out = []
+        for x in xs:
+            if pair(x):
+                out += [x[0][:3], x[1][:3]]
+            elif isinstance(x, tuple):
+                out.append(x[:3])
+        return out
+
+    def view(x):
+        return ap(x[0]).indirect(ap(x[1])) if pair(x) else ap(x) if isinstance(x, tuple) else x
+
+    def ts(out, in0, s1, op0, s2=None, op1=None):
+        if op1 is None:
+            do("V", lambda: g.vector.tensor_scalar(ap(out), view(in0), view(s1), None, op0), regs(in0, s1), regs(out))
+        else:
+            do("V", lambda: g.vector.tensor_scalar(ap(out), view(in0), view(s1), view(s2), op0, op1), regs(in0, s1, s2), regs(out))
+
+    def tt(out, in0, in1, op):
+        do("V", lambda: g.vector.tensor_tensor(ap(out), view(in0), view(in1), op), regs(in0, in1), regs(out))
+
+    def cp(out, in0):
+        if pair(out):
+            do("V", lambda: g.vector.tensor_copy(view(out), ap(in0)), regs(in0) + [out[1][:3]], [out[0][:3]])
+        else:
+            do("V", lambda: g.vector.tensor_copy(ap(out), view(in0)), regs(in0), regs(out))
+
+    def scan(out, d0, d1, init, op0, op1):
+        do("V", lambda: g.vector.tensor_tensor_scan(ap(out), ap(d0), ap(d1), view(init), op0, op1), regs(d0, d1, init), regs(out))
+
+    def red(out, in0):
+        do("V", lambda: g.vector.tensor_reduce(ap(out), ap(in0), AxisListType.X, A.add), regs(in0), regs(out))
+
+    def fill(r, c):
+        do("V", lambda: g.vector.memset(ap(r), c), [], regs(r))
+
+    def act(out, in0, func=F.Copy, scale=1.0, acc=None):
+        do("S", lambda: g.scalar.activation(ap(out), view(in0), func, bias=0.0, scale=view(scale), accum_out=view(acc)), regs(in0, scale), regs(out, acc))
+
+    def lin(out, in0, scale, bias):
+        do("S", lambda: g.scalar.activation(ap(out), view(in0), F.Identity, bias=view(bias), scale=view(scale)), regs(in0, scale, bias), regs(out))
+
+    def iota(r, pattern, base=0, cm=0):
+        if SCRATCH[r[0]][2] == "int32":
+            do("G", lambda: g.iota(ap(r), pattern, base, cm), [], regs(r))
+        else:
+            do("G", lambda: g.iota(ap(r), pattern, base, cm, allow_small_or_imprecise_dtypes=True), [], regs(r))
+
+    def sel(out, in0, pattern, op, fl, base, cm):
+        do("G", lambda: g.affine_select(ap(out), ap(in0), pattern, op, fl, base, cm), regs(in0), regs(out))
+
+    def R(b, lo=0, hi=None, *step):
+        return (b, lo, SCRATCH[b][1][1] if hi is None else hi) + step
+
+    def C(name):
+        if name not in names:
+            names[name] = len(names)
+        return ("cols", names[name], names[name] + 1)
+
+    def lists_z(t):
+        if t == 0:
+            ts(R("ZT"), R("RC", 0, 256), B / 4096.0, A.mult, -1920.5 + EPS, A.add)
+        ts(R("ZO"), R("ZT"), M23 + 1920.0, A.add, M23, A.subtract)
+
+    dma("Y", T.NI[0:8, 0:4], T.ncl[:, :], [], [("NI", 0, 4)])
+    dma("S", T.NI[0:8, 4:6], T.lim[:, :], [], [("NI", 4, 6)])
+    dma("Y", T.RC[:, 0:256], T.rc[:, 0:256], [], [R("RC", 0, 256)])
+    dma("S", T.BANK[:, 0:B], T.bank[:, :], [], [("BANK", 0, B)])
+    dma("Y", T.RA[:, 0:256], T.ra[:, 0:256], [], [R("RA", 0, 256)])
+    dma("Y", T.RB[:, 0:256], T.rb[:, 0:256], [], [R("RB", 0, 256)])
+    dma("Y", T.KRI[:, 0:256], T.used[:, :], [], [R("KRI")])
+    dma("Y", T.RC[:, 256:768], T.rc[:, 256:768], [], [R("RC", 256)])
+    dma("Y", T.RA[:, 256:768], T.ra[:, 256:768], [], [R("RA", 256)])
+    dma("Y", T.RB[:, 256:768], T.rb[:, 256:768], [], [R("RB", 256)])
+
+    ip = ("ip", 0, 1)
+    iota(ip, [[0, 1]], 0, 1)
+    iota(R("rowg"), [[1, 8], [0, 16]])
+    iota(R("SEL8"), [[1, 8], [0, 16]])
+    iota(R("rowk"), [[0, 16], [1, 8]])
+    sel(R("rk6"), R("rowk"), [[0, 16], [-1, 8]], A.is_ge, -100.0, 5, 0)
+    iota(R("ra8"), [[1, 8]])
+    iota(R("rowl"), [[0, 8], [1, 16]])
+    iota(R("rowh"), [[0, 8], [2, 2], [0, 8]], -1)
+    iota(R("IC0"), [[1, 256]])
+    iota(R("BANK", B, TR + 256), [[0, 1024]])
+    iota(R("GM"), [[0, 128]], 1)
+    sel(R("IDN"), R("GM"), [[-1, 128]], A.is_equal, 0.0, 0, 1)
+    iota(R("R256"), [[0, 16], [1, 16]])
+    iota(R("CAND", J, J + DUM), [[0, DUM]], -512)
+    iota(R("W2S", 64, 72), [[0, 8]], 1000000)
+    iota(R("W3S", 1024, 1040), [[0, 16]], 1000000)
+    iota(R("LS"), [[0, 2048]])
+    iota(R("sB"), [[1, 64]])
+    iota(R("sR"), [[0, 4], [1, 64]])
+    iota(R("C16"), [[16, 4], [0, 4]])
+    iota(R("C256"), [[256, 4], [0, 4]])
+    iota(R("I16"), [[16, 16]])
+    iota(R("ONE256"), [[0, 256]], 1)
+    iota(("XS", 0, 16), [[0, 16]])
+    iota(R("USED", TR, TR + 256), [[0, 256]], 1)
+
+    ts(("ip", 1, 2), ip, 15, A.bitwise_and)
+    ts(("ip", 2, 3), ip, 7, A.bitwise_and)
+    ts(("ip", 3, 4), ip, 3, A.logical_shift_right, 1, A.bitwise_and)
+    ts(("ip", 4, 5), ip, 4, A.logical_shift_right)
+    ts(("ip", 5, 6), ip, 1, A.bitwise_and)
+    for c in "plkhgq":
+        C(c)
+    cp(("cols", 0, 6), ("ip", 0, 6))
+    ts(R("BO"), R("rowg"), C("g"), A.is_equal)
+    ts(R("SEL8"), R("SEL8"), C("p"), A.is_equal)
+    lin(C("h0"), C("h"), -1.0, 1.0)
+    act(R("BO256"), R("BO"), scale=256.0)
+    lin(C("sg16"), C("h"), 0.125, -0.0625)
+    ts(R("F1"), R("rk6"), C("k"), A.is_gt, C("h0"), A.mult)
+    tt(R("TRI"), R("F1"), R("BO256"), A.mult)
+    act(R("ONE"), R("BO"), scale=C("h0"))
+    lin(R("F1b"), R("rowl"), C("sg16"), 1024.0)
+    lin(R("IOC", 0, 256), R("IC0"), 1.0, C("h"))
+    lin(R("IOC", 256, 257), C("h"), -256.0, 256.0)
+    ts(R("M0"), R("ra8"), C("k"), A.is_equal)
+    ts(R("M1"), R("ra8"), C("k"), A.subtract, -1.0, A.is_equal)
+    ts(C("k6"), C("k"), 6.0, A.is_ge, 100.0, A.mult)
+    tt(C("kk"), C("k"), C("k6"), A.add)
+    ts(R("AS"), R("ra8"), C("kk"), A.add)
+    m0 = ("M0", 0, 1)
+    tt(C("m01"), m0, ("M0", 1, 2), A.subtract)
+    lin(C("zc"), C("h"), 0.0, -1920.5 + EPS)
+    act(C("c7"), ("M0", 7, 8), scale=C("h0"))
+    act(C("c6"), ("M0", 6, 7), scale=C("h0"))
+    act(C("chi"), C("c7"), scale=-1920.0)
+    act(C("c6"), C("c6"), scale=EPS)
+    lin(C("clo"), C("c7"), -0.5, C("c6"))
+    fill(R("RN"), 0.0)
+    tt(R("TRIS"), R("TRI"), R("rowh"), A.mult)
+    tt(R("ONES"), R("ONE"), R("rowh"), A.mult)
+    tt(R("F1"), R("F1b"), R("BO"), A.mult)
+    lin(R("JLC"), R("F1"), 1.0, -1024.0)
+    do("V", lambda: g.vector.tensor_copy(T.NF[0:8, 0:6], T.NI[0:8, 0:6]), [("NI", 0, 6)], [("NF", 0, 6)])
+    mm([("P0", 8, 14, ("SEL8", 0, 128), ("NF", 0, 6, 1, 8), True, True)])
+    for i in (4, 5):
+        li, o = ("LX", 128 * (i - 4), 128 * (i - 4) + 128), 128 * (i - 3)
+        do("S", lambda: g.scalar.activation(T.LX[0:8, li[1]:li[2]], T.SEL8[0:8, 0:128], F.Identity, bias=T.NF[0:8, i:i + 1], scale=0.0),
+           [R("SEL8"), ("NF", i, i + 1)], [li])
+        mm([("P6", o, o + 128, li, ("SEL8", 0, 128, 1, 8), True, True)])
+    act(("RN", 0, 3), ("P0", 8, 11))
+    act(C("e0"), ("P0", 11, 12))
+    lin(C("Told"), C("e0"), -1.0, float(B))
+    act(R("LOT"), ("P6", 128, 256))
+    act(R("HIT"), ("P6", 256, 384))
+    lists_z(0)
+
+    def anti(t):
+        ts(R("AA"), R("AS"), float(3 + t), A.is_equal)
+        ts(R("AB"), R("AS"), float(4 + t), A.is_equal)
+
+    def prepare(t):
+        for i, (m, c) in enumerate((("M0", "PNL"), ("AA", "PNR"), ("M1", "dS"), ("AB", "Qc"))):
+            tt(R("T8", 8 * i, 8 * i + 8), R("RN"), R(m), A.mult)
+            act(R("T9", 8 * i, 8 * i + 8), R("T8", 8 * i, 8 * i + 8), acc=C(c))
+        lin(C("ml"), ("M0", 3 + t, 4 + t), 1.0, m0)
+        act(C("mc"), C("ml"), scale=16.0)
+
+    def prepare2(t):
+        lin(("PRE", 0, 1), C("dS"), -1.0, C("PNL"))
+        lin(("PRE", 1, 2), C("Qc"), -1.0, C("PNR"))
+        act(C("tm"), m0, scale=C("Told"))
+        lin(C("dSb"), C("PNR"), -1.0, C("tm"))
+        for c, i in (("dS", 2), ("dSb", 6)):
+            hi, lo = ("HL", i, i + 1), ("HL", i + 1, i + 2)
+            if t == 0 and i == 6:
+                ts(hi, C(c), M27, A.add, M27, A.subtract)
+                tt(lo, C(c), hi, A.subtract)
+                tt(hi, hi, C("chi"), A.add)
+                tt(lo, lo, C("clo"), A.add)
+                continue
+            lin(lo, C(c), 1.0, M27)
+            lin(hi, lo, 1.0, -M27)
+            lin(lo, hi, -1.0, C(c))
+            lin(lo, lo, 1.0, C("clo"))
+            lin(hi, hi, 1.0, C("chi"))
+
+    def shares(t):
+        tt(("WI", 0, 1), C("PNL"), C("PNR"), A.mult)
+        ts(("WI", 1, 2), ("WI", 0, 1), 12, A.arith_shift_right)
+        ts(C("Wp"), ("WI", 1, 2), 16.0, A.mult)
+
+    def newest(t):
+        e = C("e%d" % t)
+        for i, m in enumerate((("M0", 3 + t, 4 + t), C("m01"))):
+            lin(("DD", i, i + 1), m, e, ("PRE", i, i + 1))
+        lin(("DD", 6, 8), ("DD", 0, 2), 1.0, M27)
+        lin(("DD", 2, 4), ("DD", 6, 8), 1.0, -M27)
+        for i in range(2):
+            lin(("DD", 4 + i, 5 + i), ("DD", 2 + i, 3 + i), -1.0, ("DD", i, i + 1))
+
+    def gath(o, c0, c1):
+        return (("BANK", 0, TR), (o, c0 // 16, c1 // 16))
+
+    def sg(b, o, c, n):
+        act(R(b, c, c + n), gath(o, c, c + n))
+
+    def decode(t):
+        if t == 0:
+            ts(("WI", 2, 3), C("e0"), ("RN", 0, 1), A.mult)
+        else:
+            ts(("WI", 2, 3), ("P4", 16, 17), 256.0, A.add, ("RN", 0, 1), A.mult)
+            lin(C("e%d" % t), ("P4", 16, 17), 1.0, 256.0)
+            lin(C("Tq"), C("e%d" % t), 2.0 ** -12, C("TqO"))
+            lin(R("ZT"), R("RCF"), C("Tq"), C("zc"))
+        ts(("WI", 3, 4), ("WI", 2, 3), 12, A.arith_shift_right)
+        ts(C("w"), ("WI", 3, 4), C("mc"), A.mult, C("Wp"), A.add)
+        mm([("P0", 0, 1, R("TRI"), C("w"), True, True), ("P0", 1, 2, R("ONE"), C("w"), True, True)])
+        mm([("P7", 0, 1, R("TRIS"), C("w"), True, True), ("P7", 1, 2, R("ONES"), C("w"), True, True)])
+        if t:
+            newest(t)
+            cp((("BANK", 0, TR + 256), R("SO")), R("LAND%d" % (t - 1)))
+            lists_z(t)
+        else:
+            ts(("DD", 0, 1), ("M0", 3, 4), C("e0"), A.mult, ("PRE", 0, 1), A.add)
+            ts(("DD", 1, 2), C("m01"), C("e0"), A.mult, ("PRE", 1, 2), A.add)
+            ts(("DD", 2, 4), ("DD", 0, 2), M27, A.add, M27, A.subtract)
+            tt(("DD", 4, 6), ("DD", 0, 2), ("DD", 2, 4), A.subtract)
+        sg("TZ", "ZO", 0, 1024)
+        sg("TZ", "ZO", 3072, 512)
+        ts(R("AL", 0, 257), R("IOC", 0, 257), ("P0", 1, 2), A.mult, ("P0", 0, 1), A.is_ge)
+        red(C("cnt"), R("AL", 0, 257))
+        ts(C("th"), C("cnt"), -256.0, A.add, ("P7", 1, 2), A.mult)
+        ts(C("th2"), C("th"), ("P7", 0, 1), A.add, C("h0"), A.add)
+        ts(R("GM"), R("JLC"), ("P0", 1, 2), A.mult, C("th2"), A.is_ge)
+        for i, c in enumerate((("DD", 2, 3), ("DD", 4, 5), ("HL", 2, 3), ("HL", 3, 4), ("DD", 3, 4), ("DD", 5, 6), ("HL", 6, 7), ("HL", 7, 8))):
+            lt = ("LT", 128 * i, 128 * i + 128)
+            if c[0] == "DD":
+                ts(lt, R("GM"), c, A.mult, 2.0 ** -12, A.mult)
+            else:
+                ts(lt, R("GM"), c, A.mult)
+            if i % 2:
+                pb, al = ("P1", "P3", "P2", "P4")[i // 2], ("AL", 0, 256)
+                mm([(pb, 0, 256, ("LT", 128 * (i - 1), 128 * i), al, True, False), (pb, 0, 256, lt, al, False, True)])
+        for pn, ps, r, x, o in (("P1", "P3", "RA", "XT", "XO"), ("P2", "P4", "RB", "YT", "YO")):
+            tt(R(x), (pn, 0, 256), R(r, 256 * t, 256 * t + 256), A.mult)
+            tt(R(x), (ps, 0, 256), R(x), A.add)
+            ts(R(o), R(x), M23 + 1920.0, A.add, M23, A.subtract)
+
+    def add2(pb, c, n, w):
+        mm([(pb, 0, n, R("IDN"), ("TX", c, c + n), True, False), (pb, 0, n, R(w), ("TY", c, c + n), False, True)])
+
+    def sumkey(h):
+        mm([("P%d" % (1 + h), l, 256, ("CAND", 2048 * h + l, 2048 * h + 2048, 16), R("WT"), True, True, 16) for l in range(16)])
+
+    def codes(h):
+        pb, a = "P%d" % (1 + h), (128 * h, 128 * h + 128)
+        cp(R("KI", *a), (pb, 128, 256))
+        tt(R("X1", *a), (pb, 0, 128), R("LOT"), A.is_lt)
+        tt(R("X2", *a), (pb, 0, 128), R("HIT"), A.is_gt)
+        ts(R("OW", *a), R("KI", *a), 3, A.bitwise_and)
+        cp(R("OB", *a), R("OW", *a))
+        pc = "P%d" % (3 + h)
+        mm([(pc, 0, 128, R("X1", *a), R("ID4"), True, False), (pc, 0, 128, R("X2", *a), R("ID4"), False, False),
+            (pc, 0, 128, R("OB", *a), R("IDN"), False, True)])
+
+    def part(h):
+        return [(256 * p + 128 * h, 256 * p + 128 * h + 128) for p in range(N)]
+
+    def masks(h):
+        for p, f in enumerate(part(h)):
+            ts(("FM",) + f, ("P%d" % (3 + h), 0, 128), float(p), A.is_equal)
+
+    def scans(h, ps):
+        for f in [part(h)[p] for p in ps]:
+            scan(("SC",) + f, ("FM",) + f, ("FM",) + f, ("SC", f[0] - 1, f[0]) if h else 0.0, A.add, A.max)
+
+    def counts(h, ps):
+        q = [("P%d" % (5 + p // 2), 256 * (p % 2) + 128 * h, 256 * p + 128 * h) for p in ps]
+        for pb, o, c in q:
+            mm([(pb, o, o + 128, R("BO"), ("SC", c, c + 128), True, False), (pb, o, o + 128, R("NU"), ("FM", c, c + 128), False, True)])
+        for pb, o, c in q:
+            act(R("W3S", c, c + 128), (pb, o, o + 128))
+
+    for t in range(RO):
+        land, send = "LAND%d" % t, "SEND%d" % t
+        if t == 0:
+            anti(0)
+            prepare(0)
+            prepare2(0)
+            shares(0)
+        decode(t)
+        if t == 0:
+            cp(R("UG"), R("KRI"))
+            dma("Y", T.UD[:, :], T.UG[:, 0:256], [R("UG")], [("UD", 0, 4096)])
+            for l in range(16):
+                dma("Y", T.USED[l::16, 0:Q], T.UD[:, :], [("UD", 0, 4096)], [("USED", 0, Q)] if l == 15 else [], "dU")
+            act(R("NID"), R("IDN"), scale=-1.0)
+        sg("TX", "XO", 1024, 1024)
+        tt(R("TX", 0, 1024), gath("XO", 0, 1024), R("TZ", 0, 1024), A.min)
+        tt(R("CAND", 0, 1024), gath("YO", 0, 1024), R("TX", 0, 1024), A.min)
+        for i in range(2):
+            c = 2048 + 512 * i
+            sg("TX", "XO", c, 512)
+            sg("TY", "YO", c, 512)
+            add2("P%d" % (5 + i), c, 512, "NID")
+        sg("TX", "XO", 3072, 512)
+        for i in range(2):
+            act(R("TZ", 2048 + 512 * i, 2560 + 512 * i), ("P%d" % (5 + i), 0, 512), F.Abs)
+        tt(R("TY", 1024, 2048), gath("YO", 1024, 2048), R("TX", 1024, 2048), A.max)
+        tt(R("CAND", 1024, 2048), gath("ZO", 1024, 2048), R("TY", 1024, 2048), A.min)
+        if t == 0:
+            cp(R("WT", 0, 8), ("BO", 0, 128, 16))
+            ts(C("s4"), C("q"), -2.0, A.mult, 1.0, A.add)
+            ts(R("WT", 8, 16), R("WT", 0, 8), C("s4"), A.mult)
+        sumkey(0)
+        tt(R("CAND", 2048, 3072), gath("ZO", 2048, 3072), R("TZ", 2048, 3072), A.min)
+        sg("TY", "YO", 3072, 512)
+        for c in (3584, 3840):
+            sg("TX", "XO", c, 256)
+            sg("TY", "YO", c, 256)
+        if t == 0:
+            act(R("ID4"), R("IDN"), scale=4.0)
+        sg("TZ", "ZO", 3584, 512)
+        for c, n, pb in ((3072, 512, "P7"), (3584, 256, "P5"), (3840, 256, "P6")):
+            add2(pb, c, n, "IDN")
+            if c == 3072:
+                codes(0)
+            tt(R("CAND", c, c + n), (pb, 0, n), R("TZ", c, c + n), A.min)
+        sumkey(1)
+        if t == 0:
+            sel(R("UP"), R("BO"), [[-1, 128]], A.is_gt, 0.0, 0, 1)
+            sel(R("SU"), R("BO"), [[1, 128]], A.is_gt, 0.0, 0, -1)
+            act(R("NU"), R("UP"), scale=-1.0)
+            act(R("BO16"), R("BO"), scale=16.0)
+            for l in range(16):
+                act(("LS", 128 * l + l, 128 * l + 128, 16), ("BO", 0, 128, 16))
+            ts(R("KP"), R("R256"), C("l"), A.is_equal, 32768.0, A.mult)
+        masks(0)
+        scans(0, (0, 1))
+        codes(1)
+        scans(0, (2, 3))
+        counts(0, range(N))
+        masks(1)
+        scans(1, range(N))
+        mm([("P0", 64, 128, R("BO"), ("SC", 15, 1024, 16), True, True)])
+        mm([("P7", 0, 64, ("LS", 128 * b, 128 * b + 128), ("SC", b, 1024, 16), b == 0, False) for b in range(11)])
+        scan(R("W1T"), R("KP", 0, 64), ("P0", 64, 128), 0.0, A.max, A.min)
+        for p in range(N):
+            ts(("I1", 64 * p, 64 * p + 64), R("sB"), ("W1T", 16 * p + 15, 16 * p + 16), A.is_ge)
+        mm([("P1", 0, 256, R("BO"), R("I1"), True, True)])
+        mm([("P7", 0, 64, ("LS", 128 * b, 128 * b + 128), ("SC", b, 1024, 16), False, b == 15) for b in range(11, 16)])
+        act(R("W2S", 0, 64), ("P7", 0, 64))
+        mm([("P2", 0, 256, R("BO16"), R("I1"), True, False)])
+        counts(1, (0, 1))
+        if t < RO - 1:
+            anti(t + 1)
+        scan(R("PK1"), R("KP"), ("P1", 0, 256), 0.0, A.max, A.min)
+        tt(R("O1"), ("PK1", 15, 256, 16), R("C16"), A.add)
+        tt(R("I2"), (("W2S", 0, 72), R("O1")), R("sR"), A.is_le)
+        mm([("P2", 0, 256, R("BO"), R("I2"), False, True)])
+        counts(1, (2, 3))
+        mm([("P3", 0, 256, R("BO256"), R("I1"), True, False)])
+        mm([("P3", 0, 256, R("BO16"), R("I2"), False, False)])
+        if t == 0:
+            ts(C("wi"), C("l"), 14.0, A.mult, 9.0, A.add)
+            act(R("WB"), R("BO"), scale=C("wi"))
+            act(R("WKF"), R("LS"), scale=C("wi"))
+            act(R("NBO"), R("BO"), scale=-1.0)
+        if t < RO - 1:
+            cp(R("RCF"), R("RC", 256 * (t + 1), 256 * (t + 1) + 256))
+        scan(R("PK1"), R("KP"), ("P2", 0, 256), 0.0, A.max, A.min)
+        tt(R("O2"), ("PK1", 15, 256, 16), R("C256"), A.add)
+        tt(R("XP"), (("W3S", 0, 1040), R("O2")), R("sR"), A.is_le)
+        mm([("P3", 0, 256, R("BO"), R("XP"), False, True)])
+        scan(R("PK1"), R("KP"), ("P3", 0, 256), 0.0, A.max, A.min)
+        cp(R("O3"), ("PK1", 15, 256, 16))
+        cp(R(send), (("CAND", 0, J + DUM), R("O3")))
+        deps("G", [R(send)], [])
+        tr, lo = [], 0
+        for d, ne in ((1, 4), (2, 4), (3, 4)):
+            p = (rank + d) % N
+            rid, pid = topo.addr(T.cores[p])[:2]
+            mask = sum(1 << x for x in topo.engines(core, T.cores[p])[lo:lo + ne])
+            lo += ne
+            tr.append(RemoteDMATransfer(dst_ids=[DstId(rid=rid, pnc=pid)], dma_engine_mask=mask, remote_sem=T.sem["arr%d" % t],
+                                        src=T[send][:, 64 * p:64 * p + 64], dst=T[land][:, 64 * rank:64 * rank + 64]))
+        g.remote_dma_fused(tr, local_sem=T.sem["snt%d" % t])
+        count["snt%d" % t] = 12
+        count["arr%d" % t] = 12
+        note("G", [], [(land, 64 * p, 64 * p + 64) for p in range(N) if p != rank], ("arr%d" % t, 12), True)
+        act((land, 64 * rank, 64 * rank + 64), (send, 64 * rank, 64 * rank + 64))
+        if t == 0:
+            ts(R("MK2"), R("R256"), C("l"), A.not_equal, 9984.0, A.mult)
+            ts(R("I16"), R("I16"), C("l"), A.add)
+            ts(R("TB"), R("I16"), float(TR), A.add)
+        else:
+            tt(R("UO2"), R("BC"), R("NK"), A.max)
+            cp((("USED", 0, TR + 256), R("UO2")), R("ONE256"))
+        lin(C("Told"), C("Told"), 1.0, C("e%d" % t))
+        lin(R("TI"), R("I16"), 1.0, C("Told"))
+        if t < RO - 1:
+            act(("RN", 3 + t, 4 + t), C("e%d" % t))
+            prepare(t + 1)
+            shares(t + 1)
+            act(C("TqO"), C("Told"), scale=2.0 ** -12)
+        mm([("P1", 0, 256, R("WB"), R(land), True, True)])
+        mm([("P2", 0, 16, ("WKF", 128 * l, 128 * l + 128), (land, l, 256, 16), l == 0, l == 15) for l in range(16)])
+        cp(R("KRI"), ("P1", 0, 256))
+        ts(R("BRI"), R("KRI"), 2, A.arith_shift_right, 4095, A.bitwise_and)
+        cp(R("BR"), R("BRI"))
+        cp(R("KBI"), ("P2", 0, 16))
+        ts(R("NV"), ("P2", 0, 16), 0.0, A.is_lt, 4096.0, A.mult)
+        ts(R("BBI"), R("KBI"), 2, A.arith_shift_right, 4095, A.bitwise_and)
+        tt(R("BC"), R("BBI"), R("NV"), A.add)
+        cp(R("UO"), R("BC"))
+        act(R("UG"), (("USED", 0, TR + 256), R("UO")))
+        if t < RO - 1:
+            prepare2(t + 1)
+        for n in range(16):
+            c = 4 * (n % 4) + n // 4
+            o = 512 * (c // 4) + 16 * (c % 4)
+            ts(("E", o, o + 256 - 16 * c), ("BR", 16 * c, 256), ("BC", c, c + 1), A.is_equal)
+            if c == 0:
+                mm([("P3", 0, 256, R("BO"), R("E", 0, 256), True, False), ("P3", 0, 16, R("NBO"), ("E", 0, 16), False, False)])
+            elif c < 15:
+                mm([("P3", 16 * c + 16, 256, R("BO"), ("E", o + 16, o + 256 - 16 * c), False, False)])
+            if n == 6:
+                mm([("P3", 0, 256, R("BO"), R("UG"), False, False)])
+        mm([("P3", 64 * k, 64 * k + 64, R("SU"), ("E", 512 * k, 512 * k + 64), False, k == 3) for k in range(4)])
+        tt(R("XP"), ("P3", 0, 256), R("MK2"), A.is_gt)
+        scan(("XS", 16, 272), R("XP"), R("XP"), 0.0, A.add, A.max)
+        sk = ("XS", 31, 272, 16)
+        mm([("P4", 0, 16, R("NBO"), sk, True, False), ("P4", 0, 16, R("UP"), sk, False, False), ("P4", 1, 16, R("NU"), ("XS", 31, 256, 16), False, True),
+            ("P4", 16, 17, R("NBO"), ("XS", 271, 272), True, True)])
+        tt(R("NK"), sk, ("XS", 15, 256, 16), A.subtract)
+        tt(R("NK"), R("NK"), R("TB"), A.mult)
+        tt(R("PO"), ("P4", 0, 16), R("TI"), A.add)
+        tt(R("SO"), R("PO"), R("NK"), A.max)
+
+    cp((("BANK", 0, TR + 256), R("SO")), R("LAND%d" % (RO - 1)))
+    dma("Y", T.y[:, :], T.BANK[:, B:TR], [("BANK", B, TR)], [])
+    for s in sorted(count):
+        g.wait_ge(T.sem[s], count[s])

@@ -6,8 +6,12 @@ B, J, CAP, RO, Q, N = 3328, 4096, 64, 3, 4096, 4
 TR = 4096
 DUM = 288
 M23 = 8388608.0
+M24 = 16777218.0
 M27 = 201326592.0
+M35 = 1.5 * 2.0 ** 35
 EPS = 2.0 ** -13
+NONE = 4096
+ZK = 2.0 ** 20 - 2047.625
 
 SCRATCH = {}
 
@@ -19,12 +23,12 @@ def _sb(dtype, **kw):
 
 _sb("bfloat16", BANK=TR + 256, CAND=J + DUM, TX=J, TY=J, TZ=J, USED=TR + 256, ONE256=256, FM=1024, SC=1024, I1=256, I2=256,
     UG=256, E=2048, XP=256, XS=272, SEND0=256, SEND1=256, SEND2=256, LAND0=256, LAND1=256, LAND2=256, BO=128, BO16=128,
-    BO256=128, NBO=128, IDN=128, NID=128, ID4=128, UP=128, NU=128, SU=128, WB=128, LS=2048, WKF=2048, WT=16, KP=256, MK2=256,
-    rowg=128, rowl=128, rowk=128, rowh=128, R256=256, sB=64, IOC=258, JLC=128, AL=258, GM=128, LT=1024, X1=256, X2=256, OB=256)
-_sb("float32", sR=256, IC0=256, cols=64, RN=8, ra8=8, AS=8, M0=8, M1=8, AA=8, AB=8, T8=32, T9=32, PRE=16, HL=16, DD=16, I16=16, TB=16,
-    TI=16, NK=16, C16=16, C256=16, W1T=64, W2S=72, W3S=1040, PK1=256, SEL8=128, NF=8, LX=256, LOT=128, HIT=128,
-    TRI=128, TRIS=128, ONE=128, ONES=128, rk6=128, F1=128, F1b=128, ZT=256, RCF=256, XT=256, YT=256, BC=16, NV=16, PO=16)
-_sb("int32", RA=768, RB=768, RC=768, ip=8, NI=8, WI=4, KI=256, OW=256, KRI=256, BRI=256, KBI=16, BBI=16)
+    BO256=128, NBO=128, IDN=128, NID=128, ID4=128, UP=128, NU=128, SU=128, WB=128, LS=2048, WT=16, KP=256, MK2=256, MKB=256, CR=256,
+    rowg=128, rowl=128, rowk=128, R256=256, sB=64, IOC=256, AL=256, SG=256, GM=128, LT=1024, X1=256, X2=256, OB=256, AC=8)
+_sb("float32", sR=256, IC0=256, NIC=256, cols=64, RN=8, ra8=8, AS=8, M0=8, M1=8, AA=8, AB=8, T8=32, T9=32, PRE=4, HL=16, I16=16, TB=16,
+    TI=16, NK=16, C16=16, C256=16, W1T=64, W2S=72, W3S=1040, PK1=256, SEL8=128, NF=8, LX=256, LOT=128, HIT=128, IN2=2, CC=2,
+    TRI=128, ONE=128, F1=128, F1b=128, JL=128, ZT=256, RCF=256, XT=256, YT=256, BC=16, BD=16, NV=16, PO=16, KZ=256, T16=16, BIA=4)
+_sb("int32", RA=768, RB=768, RC=768, ip=8, NI=8, WI=4, KI=256, KRI=256)
 _sb("uint16", XO=256, YO=256, ZO=256, O1=16, O2=16, O3=16, UO=16, SO=16, UO2=16, BR=256)
 SCRATCH["UD"] = ("dram", [8, 4096], "bfloat16")
 for _b in range(8):
@@ -78,7 +82,7 @@ def rank_program(g, core, T, topo):
         fn().then_inc(T.sem[s], 1)
         note(q, reads, writes, (s, count[s]))
 
-    def mm(lst):
+    def mm(lst, rows=(0, 128)):
         reads = [x[3][:3] for x in lst] + [x[4][:3] for x in lst]
         writes = [x[:3] for x in lst]
         deps("P", reads, writes)
@@ -88,7 +92,7 @@ def rank_program(g, core, T, topo):
             kp = rh[4] if len(rh) > 4 else 128
             lv = T[lh[0]][0:kp, lh[1]:lh[2]:lh[3] if len(lh) > 3 else 1]
             rv = T[rh[0]][0:kp, rh[1]:rh[2]:rh[3] if len(rh) > 3 else 1]
-            last = g.tensor.matmul(T[o][:, c0:c1:x[7] if len(x) > 7 else 1], lv, rv, st, sp)
+            last = g.tensor.matmul(T[o][rows[0]:rows[1], c0:c1:x[7] if len(x) > 7 else 1], lv, rv, st, sp)
         count["cP"] = count.get("cP", 0) + 1
         last.then_inc(T.sem["cP"], 1)
         note("P", reads, writes, ("cP", count["cP"]))
@@ -138,17 +142,15 @@ def rank_program(g, core, T, topo):
     def scan(out, d0, d1, init, op0, op1):
         do("V", lambda: g.vector.tensor_tensor_scan(ap(out), ap(d0), ap(d1), view(init), op0, op1), regs(d0, d1, init), regs(out))
 
-    def red(out, in0):
-        do("V", lambda: g.vector.tensor_reduce(ap(out), ap(in0), AxisListType.X, A.add), regs(in0), regs(out))
-
     def fill(r, c):
         do("V", lambda: g.vector.memset(ap(r), c), [], regs(r))
 
-    def act(out, in0, func=F.Copy, scale=1.0, acc=None):
-        do("S", lambda: g.scalar.activation(ap(out), view(in0), func, bias=0.0, scale=view(scale), accum_out=view(acc)), regs(in0, scale), regs(out, acc))
+    def act(out, in0, func=F.Copy, scale=1.0, acc=None, bias=0.0):
+        do("S", lambda: g.scalar.activation(ap(out), view(in0), func, bias=view(bias), scale=view(scale), accum_out=view(acc)),
+           regs(in0, scale, bias), regs(out, acc))
 
     def lin(out, in0, scale, bias):
-        do("S", lambda: g.scalar.activation(ap(out), view(in0), F.Identity, bias=view(bias), scale=view(scale)), regs(in0, scale, bias), regs(out))
+        act(out, in0, F.Identity, scale, None, bias)
 
     def iota(r, pattern, base=0, cm=0):
         if SCRATCH[r[0]][2] == "int32":
@@ -162,15 +164,13 @@ def rank_program(g, core, T, topo):
     def R(b, lo=0, hi=None, *step):
         return (b, lo, SCRATCH[b][1][1] if hi is None else hi) + step
 
+    def K(b, i):
+        return (b, i, i + 1)
+
     def C(name):
         if name not in names:
             names[name] = len(names)
-        return ("cols", names[name], names[name] + 1)
-
-    def lists_z(t):
-        if t == 0:
-            ts(R("ZT"), R("RC", 0, 256), B / 4096.0, A.mult, -1920.5 + EPS, A.add)
-        ts(R("ZO"), R("ZT"), M23 + 1920.0, A.add, M23, A.subtract)
+        return K("cols", names[name])
 
     dma("Y", T.NI[0:8, 0:4], T.ncl[:, :], [], [("NI", 0, 4)])
     dma("S", T.NI[0:8, 4:6], T.lim[:, :], [], [("NI", 4, 6)])
@@ -183,21 +183,16 @@ def rank_program(g, core, T, topo):
     dma("Y", T.RA[:, 256:768], T.ra[:, 256:768], [], [R("RA", 256)])
     dma("Y", T.RB[:, 256:768], T.rb[:, 256:768], [], [R("RB", 256)])
 
-    ip = ("ip", 0, 1)
+    ip = K("ip", 0)
     iota(ip, [[0, 1]], 0, 1)
-    iota(R("rowg"), [[1, 8], [0, 16]])
-    iota(R("SEL8"), [[1, 8], [0, 16]])
-    iota(R("rowk"), [[0, 16], [1, 8]])
-    sel(R("rk6"), R("rowk"), [[0, 16], [-1, 8]], A.is_ge, -100.0, 5, 0)
     iota(R("ra8"), [[1, 8]])
-    iota(R("rowl"), [[0, 8], [1, 16]])
-    iota(R("rowh"), [[0, 8], [2, 2], [0, 8]], -1)
+    iota(R("rowg"), [[1, 8], [0, 16]])
+    iota(R("rowk"), [[0, 16], [1, 8]])
     iota(R("IC0"), [[1, 256]])
-    iota(R("BANK", B, TR + 256), [[0, 1024]])
-    iota(R("GM"), [[0, 128]], 1)
-    sel(R("IDN"), R("GM"), [[-1, 128]], A.is_equal, 0.0, 0, 1)
+    iota(R("rowl"), [[0, 8], [1, 16]])
+    iota(R("F1"), [[1, 128]], 0, -1)
     iota(R("R256"), [[0, 16], [1, 16]])
-    iota(R("CAND", J, J + DUM), [[0, DUM]], -512)
+    iota(R("CAND", J, J + DUM), [[0, DUM]], NONE)
     iota(R("W2S", 64, 72), [[0, 8]], 1000000)
     iota(R("W3S", 1024, 1040), [[0, 16]], 1000000)
     iota(R("LS"), [[0, 2048]])
@@ -210,100 +205,89 @@ def rank_program(g, core, T, topo):
     iota(("XS", 0, 16), [[0, 16]])
     iota(R("USED", TR, TR + 256), [[0, 256]], 1)
 
-    ts(("ip", 1, 2), ip, 15, A.bitwise_and)
-    ts(("ip", 2, 3), ip, 7, A.bitwise_and)
-    ts(("ip", 3, 4), ip, 3, A.logical_shift_right, 1, A.bitwise_and)
-    ts(("ip", 4, 5), ip, 4, A.logical_shift_right)
-    ts(("ip", 5, 6), ip, 1, A.bitwise_and)
+    fill(R("BANK", B, TR + 256), 0.0)
+    fill(R("RN"), 0.0)
+    fill(R("BIA", 0, 1), 7.5)
+    fill(R("BIA", 1, 2), -7.5)
+    fill(R("BIA", 2, 4), 0.0)
+    fill(R("AB"), 0.0)
+    ts(K("ip", 1), ip, 15, A.bitwise_and)
+    ts(K("ip", 2), ip, 7, A.bitwise_and)
+    ts(K("ip", 3), ip, 3, A.logical_shift_right, 1, A.bitwise_and)
+    ts(K("ip", 4), ip, 4, A.logical_shift_right)
+    ts(K("ip", 5), ip, 1, A.bitwise_and)
     for c in "plkhgq":
         C(c)
     cp(("cols", 0, 6), ("ip", 0, 6))
-    ts(R("BO"), R("rowg"), C("g"), A.is_equal)
-    ts(R("SEL8"), R("SEL8"), C("p"), A.is_equal)
-    lin(C("h0"), C("h"), -1.0, 1.0)
-    act(R("BO256"), R("BO"), scale=256.0)
-    lin(C("sg16"), C("h"), 0.125, -0.0625)
-    ts(R("F1"), R("rk6"), C("k"), A.is_gt, C("h0"), A.mult)
-    tt(R("TRI"), R("F1"), R("BO256"), A.mult)
-    act(R("ONE"), R("BO"), scale=C("h0"))
-    lin(R("F1b"), R("rowl"), C("sg16"), 1024.0)
-    lin(R("IOC", 0, 256), R("IC0"), 1.0, C("h"))
-    lin(R("IOC", 256, 257), C("h"), -256.0, 256.0)
+    m0 = K("M0", 0)
     ts(R("M0"), R("ra8"), C("k"), A.is_equal)
     ts(R("M1"), R("ra8"), C("k"), A.subtract, -1.0, A.is_equal)
-    ts(C("k6"), C("k"), 6.0, A.is_ge, 100.0, A.mult)
-    tt(C("kk"), C("k"), C("k6"), A.add)
-    ts(R("AS"), R("ra8"), C("kk"), A.add)
-    m0 = ("M0", 0, 1)
-    tt(C("m01"), m0, ("M0", 1, 2), A.subtract)
-    lin(C("zc"), C("h"), 0.0, -1920.5 + EPS)
-    act(C("c7"), ("M0", 7, 8), scale=C("h0"))
-    act(C("c6"), ("M0", 6, 7), scale=C("h0"))
+    ts(C("k6"), C("k"), 6.0, A.is_ge)
+    ts(R("SEL8"), R("rowg"), C("p"), A.is_equal)
+    ts(R("BO"), R("rowg"), C("g"), A.is_equal)
+    lin(C("h0"), C("h"), -1.0, 1.0)
+    lin(C("sg"), C("h"), 2.0, -1.0)
+    lin(C("kk"), C("k6"), 100.0, C("k"))
+    lin(C("on"), C("k6"), 1.0, m0)
+    act(C("hc"), C("h"), scale=1.0 / 128)
+    lin(C("jb"), C("sg"), 2032.0, 6500.0)
+    act(C("sg8"), C("sg"), scale=-8.0)
+    lin(R("AS"), R("ra8"), 1.0, C("kk"))
+    act(R("ONE"), R("BO"), scale=C("h0"))
+    lin(C("gm"), C("on"), -2048.0, 2048.0)
+    lin(C("b1"), C("on"), -10000.0, 4.0 - M24)
+    act(C("c7"), K("M0", 7), scale=C("h0"))
+    act(C("c6"), K("M0", 6), scale=C("h0"))
+    act(C("gm"), C("gm"), scale=C("sg"))
     act(C("chi"), C("c7"), scale=-1920.0)
     act(C("c6"), C("c6"), scale=EPS)
+    lin(C("zc"), C("h"), 0.0, -1920.5 + EPS)
     lin(C("clo"), C("c7"), -0.5, C("c6"))
-    fill(R("RN"), 0.0)
-    tt(R("TRIS"), R("TRI"), R("rowh"), A.mult)
-    tt(R("ONES"), R("ONE"), R("rowh"), A.mult)
-    tt(R("F1"), R("F1b"), R("BO"), A.mult)
-    lin(R("JLC"), R("F1"), 1.0, -1024.0)
+    tt(C("m01"), m0, K("M0", 1), A.subtract)
+    ts(R("TRI"), R("rowk"), C("k"), A.is_gt, 2.0, A.mult)
     do("V", lambda: g.vector.tensor_copy(T.NF[0:8, 0:6], T.NI[0:8, 0:6]), [("NI", 0, 6)], [("NF", 0, 6)])
     mm([("P0", 8, 14, ("SEL8", 0, 128), ("NF", 0, 6, 1, 8), True, True)])
-    for i in (4, 5):
-        li, o = ("LX", 128 * (i - 4), 128 * (i - 4) + 128), 128 * (i - 3)
-        do("S", lambda: g.scalar.activation(T.LX[0:8, li[1]:li[2]], T.SEL8[0:8, 0:128], F.Identity, bias=T.NF[0:8, i:i + 1], scale=0.0),
-           [R("SEL8"), ("NF", i, i + 1)], [li])
-        mm([("P6", o, o + 128, li, ("SEL8", 0, 128, 1, 8), True, True)])
-    act(("RN", 0, 3), ("P0", 8, 11))
-    act(C("e0"), ("P0", 11, 12))
-    lin(C("Told"), C("e0"), -1.0, float(B))
-    act(R("LOT"), ("P6", 128, 256))
-    act(R("HIT"), ("P6", 256, 384))
-    lists_z(0)
+    tt(R("TRI"), R("TRI"), R("ONE"), A.mult)
+    cp(("RN", 0, 3), ("P0", 8, 11))
+    cp(C("e0"), ("P0", 11, 12))
+    lin(R("IOC"), R("IC0"), 1.0 / 128, C("hc"))
+    lin(R("NIC"), R("IC0"), -1.0 / 128, -2.0 ** -19)
+    lin(R("F1b"), R("rowl"), C("sg"), C("jb"))
 
     def anti(t):
         ts(R("AA"), R("AS"), float(3 + t), A.is_equal)
-        ts(R("AB"), R("AS"), float(4 + t), A.is_equal)
+        ts(R("AB", 1), R("AS", 1), float(4 + t), A.is_equal)
 
     def prepare(t):
         for i, (m, c) in enumerate((("M0", "PNL"), ("AA", "PNR"), ("M1", "dS"), ("AB", "Qc"))):
             tt(R("T8", 8 * i, 8 * i + 8), R("RN"), R(m), A.mult)
             act(R("T9", 8 * i, 8 * i + 8), R("T8", 8 * i, 8 * i + 8), acc=C(c))
-        lin(C("ml"), ("M0", 3 + t, 4 + t), 1.0, m0)
-        act(C("mc"), C("ml"), scale=16.0)
-
-    def prepare2(t):
-        lin(("PRE", 0, 1), C("dS"), -1.0, C("PNL"))
-        lin(("PRE", 1, 2), C("Qc"), -1.0, C("PNR"))
-        act(C("tm"), m0, scale=C("Told"))
-        lin(C("dSb"), C("PNR"), -1.0, C("tm"))
-        for c, i in (("dS", 2), ("dSb", 6)):
-            hi, lo = ("HL", i, i + 1), ("HL", i + 1, i + 2)
-            if t == 0 and i == 6:
-                ts(hi, C(c), M27, A.add, M27, A.subtract)
-                tt(lo, C(c), hi, A.subtract)
-                tt(hi, hi, C("chi"), A.add)
-                tt(lo, lo, C("clo"), A.add)
-                continue
-            lin(lo, C(c), 1.0, M27)
-            lin(hi, lo, 1.0, -M27)
-            lin(lo, hi, -1.0, C(c))
-            lin(lo, lo, 1.0, C("clo"))
-            lin(hi, hi, 1.0, C("chi"))
 
     def shares(t):
-        tt(("WI", 0, 1), C("PNL"), C("PNR"), A.mult)
-        ts(("WI", 1, 2), ("WI", 0, 1), 12, A.arith_shift_right)
-        ts(C("Wp"), ("WI", 1, 2), 16.0, A.mult)
+        tt(K("WI", 0), C("PNL"), C("PNR"), A.mult)
+        ts(K("WI", 1), K("WI", 0), 12, A.arith_shift_right)
+        cp(C("Wp"), K("WI", 1))
+        mm([("P6", 0, 1, R("ONE"), C("Wp"), True, True), ("P6", 1, 2, R("TRI"), C("Wp"), True, True)])
 
-    def newest(t):
-        e = C("e%d" % t)
-        for i, m in enumerate((("M0", 3 + t, 4 + t), C("m01"))):
-            lin(("DD", i, i + 1), m, e, ("PRE", i, i + 1))
-        lin(("DD", 6, 8), ("DD", 0, 2), 1.0, M27)
-        lin(("DD", 2, 4), ("DD", 6, 8), 1.0, -M27)
-        for i in range(2):
-            lin(("DD", 4 + i, 5 + i), ("DD", 2 + i, 3 + i), -1.0, ("DD", i, i + 1))
+    def sums(t):
+        ts(K("IN2", 0), ("P6", 0, 1), 4.0 - M24, A.add)
+        ts(K("IN2", 1), ("P6", 1, 2), C("b1"), A.add)
+
+    def steps(t):
+        lin(K("PRE", 0), C("dS"), -1.0, C("PNL"))
+        lin(K("PRE", 1), C("Qc"), -1.0, C("PNR"))
+        act(C("tm"), m0, scale=C("Told"))
+        act(K("PRE", 2), C("dS"))
+        lin(K("PRE", 3), C("PNR"), -1.0, C("tm"))
+        if t == 0:
+            lin(K("PRE", 0), K("M0", 3), C("e0"), K("PRE", 0))
+            lin(K("PRE", 1), C("m01"), C("e0"), K("PRE", 1))
+        hi, lo = ("HL", 0, 4), ("HL", 4, 8)
+        tt(lo, R("PRE"), R("BIA"), A.add)
+        ts(hi, lo, M27, A.add, M27, A.subtract)
+        tt(lo, R("PRE"), hi, A.subtract)
+        ts(("HL", 2, 4), ("HL", 2, 4), C("chi"), A.add)
+        ts(("HL", 6, 8), ("HL", 6, 8), C("clo"), A.add)
 
     def gath(o, c0, c1):
         return (("BANK", 0, TR), (o, c0 // 16, c1 // 16))
@@ -311,71 +295,75 @@ def rank_program(g, core, T, topo):
     def sg(b, o, c, n):
         act(R(b, c, c + n), gath(o, c, c + n))
 
+    def list_z():
+        ts(R("ZO"), R("ZT"), M23 + 1920.0, A.add, M23, A.subtract)
+
+    def places():
+        tt(R("PO"), ("P5", 0, 16), R("TI"), A.add)
+        tt(R("SO"), R("PO"), R("NK"), A.max)
+
     def decode(t):
-        if t == 0:
-            ts(("WI", 2, 3), C("e0"), ("RN", 0, 1), A.mult)
-        else:
-            ts(("WI", 2, 3), ("P4", 16, 17), 256.0, A.add, ("RN", 0, 1), A.mult)
-            lin(C("e%d" % t), ("P4", 16, 17), 1.0, 256.0)
-            lin(C("Tq"), C("e%d" % t), 2.0 ** -12, C("TqO"))
-            lin(R("ZT"), R("RCF"), C("Tq"), C("zc"))
-        ts(("WI", 3, 4), ("WI", 2, 3), 12, A.arith_shift_right)
-        ts(C("w"), ("WI", 3, 4), C("mc"), A.mult, C("Wp"), A.add)
-        mm([("P0", 0, 1, R("TRI"), C("w"), True, True), ("P0", 1, 2, R("ONE"), C("w"), True, True)])
-        mm([("P7", 0, 1, R("TRIS"), C("w"), True, True), ("P7", 1, 2, R("ONES"), C("w"), True, True)])
+        ct, c2, e = K("CC", 0), K("CC", 1), C("e%d" % t)
         if t:
-            newest(t)
+            act(e, ("P0", 0, 1))
+            lin(C("Tq"), ("P0", 0, 1), 2.0 ** -12, C("TqO"))
+            lin(R("ZT"), R("RCF"), C("Tq"), C("zc"))
+            ts(C("w2"), ("P4", 0, 1), C("s2"), A.mult, M24, A.add)
+            tt(R("NK"), R("NK"), R("TB"), A.mult)
+        ts(R("CC"), R("IN2"), C("w2"), A.add, 4.0, A.subtract)
+        if t:
+            places()
+        act(R("SG"), R("NIC"), F.Sign, ct, C("cnt"), c2)
+        lo = [K("HL", 4 + i) for i in range(4)]
+        if t:
+            lo[0], lo[1] = K("HL", 8), K("HL", 9)
+            lin(lo[0], K("M0", 3 + t), e, K("HL", 4))
+            lin(lo[1], C("m01"), e, K("HL", 5))
+        ts(C("al"), ct, C("sg8"), A.mult)
+        ts(C("ga"), c2, C("gm"), A.mult, C("h0"), A.add)
+        ts(R("AL"), R("IOC"), ct, A.mult, c2, A.is_ge)
+        if t:
+            list_z()
+        ts(C("th"), C("cnt"), C("al"), A.mult, C("ga"), A.add)
+        ts(R("GM"), R("JL"), ct, A.mult, C("th"), A.is_ge)
+        for n, (i, pb) in enumerate(((0, "P1"), (2, "P3"), (1, "P2"), (3, "P4"))):
+            for u, c in enumerate((K("HL", i), lo[i])):
+                lt = ("LT", 256 * n + 128 * u, 256 * n + 128 * u + 128)
+                ts(lt, R("GM"), c, A.mult, 1.0 if i > 1 else 2.0 ** -12, A.mult)
+            mm([(pb, 0, 256, ("LT", 256 * n, 256 * n + 128), R("AL"), True, False), (pb, 0, 256, lt, R("AL"), False, True)])
+        if t:
             cp((("BANK", 0, TR + 256), R("SO")), R("LAND%d" % (t - 1)))
-            lists_z(t)
-        else:
-            ts(("DD", 0, 1), ("M0", 3, 4), C("e0"), A.mult, ("PRE", 0, 1), A.add)
-            ts(("DD", 1, 2), C("m01"), C("e0"), A.mult, ("PRE", 1, 2), A.add)
-            ts(("DD", 2, 4), ("DD", 0, 2), M27, A.add, M27, A.subtract)
-            tt(("DD", 4, 6), ("DD", 0, 2), ("DD", 2, 4), A.subtract)
         sg("TZ", "ZO", 0, 1024)
-        sg("TZ", "ZO", 3072, 512)
-        ts(R("AL", 0, 257), R("IOC", 0, 257), ("P0", 1, 2), A.mult, ("P0", 0, 1), A.is_ge)
-        red(C("cnt"), R("AL", 0, 257))
-        ts(C("th"), C("cnt"), -256.0, A.add, ("P7", 1, 2), A.mult)
-        ts(C("th2"), C("th"), ("P7", 0, 1), A.add, C("h0"), A.add)
-        ts(R("GM"), R("JLC"), ("P0", 1, 2), A.mult, C("th2"), A.is_ge)
-        for i, c in enumerate((("DD", 2, 3), ("DD", 4, 5), ("HL", 2, 3), ("HL", 3, 4), ("DD", 3, 4), ("DD", 5, 6), ("HL", 6, 7), ("HL", 7, 8))):
-            lt = ("LT", 128 * i, 128 * i + 128)
-            if c[0] == "DD":
-                ts(lt, R("GM"), c, A.mult, 2.0 ** -12, A.mult)
-            else:
-                ts(lt, R("GM"), c, A.mult)
-            if i % 2:
-                pb, al = ("P1", "P3", "P2", "P4")[i // 2], ("AL", 0, 256)
-                mm([(pb, 0, 256, ("LT", 128 * (i - 1), 128 * i), al, True, False), (pb, 0, 256, lt, al, False, True)])
-        for pn, ps, r, x, o in (("P1", "P3", "RA", "XT", "XO"), ("P2", "P4", "RB", "YT", "YO")):
-            tt(R(x), (pn, 0, 256), R(r, 256 * t, 256 * t + 256), A.mult)
-            tt(R(x), (ps, 0, 256), R(x), A.add)
-            ts(R(o), R(x), M23 + 1920.0, A.add, M23, A.subtract)
+        ra, rb = R("RA", 256 * t, 256 * t + 256), R("RB", 256 * t, 256 * t + 256)
+        tt(R("XT"), ("P1", 0, 256), ra, A.mult)
+        tt(R("YT"), ("P2", 0, 256), rb, A.mult)
+        tt(R("XT"), ("P3", 0, 256), R("XT"), A.add)
+        tt(R("YT"), ("P4", 0, 256), R("YT"), A.add)
+        ts(R("XO"), R("XT"), M23 + 1920.0, A.add, M23, A.subtract)
+        ts(R("YO"), R("YT"), M23 + 1920.0, A.add, M23, A.subtract)
 
     def add2(pb, c, n, w):
         mm([(pb, 0, n, R("IDN"), ("TX", c, c + n), True, False), (pb, 0, n, R(w), ("TY", c, c + n), False, True)])
 
-    def sumkey(h):
-        mm([("P%d" % (1 + h), l, 256, ("CAND", 2048 * h + l, 2048 * h + 2048, 16), R("WT"), True, True, 16) for l in range(16)])
+    def sumkey(h, r0, r1):
+        c = 2048 * h
+        mm([("P%d" % (1 + h), l, 256, ("CAND", c + 16 * r0 + l, c + 16 * r1, 16), R("WT"), True, True, 16) for l in range(16)], (r0, r1))
 
     def codes(h):
-        pb, a = "P%d" % (1 + h), (128 * h, 128 * h + 128)
-        cp(R("KI", *a), (pb, 128, 256))
+        pb, pc, a = "P%d" % (1 + h), "P%d" % (3 + h), (128 * h, 128 * h + 128)
+        ts(R("KI", *a), (pb, 128, 256), 0.125, A.add)
         tt(R("X1", *a), (pb, 0, 128), R("LOT"), A.is_lt)
         tt(R("X2", *a), (pb, 0, 128), R("HIT"), A.is_gt)
-        ts(R("OW", *a), R("KI", *a), 3, A.bitwise_and)
-        cp(R("OB", *a), R("OW", *a))
-        pc = "P%d" % (3 + h)
-        mm([(pc, 0, 128, R("X1", *a), R("ID4"), True, False), (pc, 0, 128, R("X2", *a), R("ID4"), False, False),
-            (pc, 0, 128, R("OB", *a), R("IDN"), False, True)])
+        mm([(pc, 0, 128, R("X1", *a), R("ID4"), True, False), (pc, 0, 128, R("X2", *a), R("ID4"), False, False)])
+        tt(R("OB", *a), (pb, 128, 256), R("KI", *a), A.subtract)
+        mm([(pc, 0, 128, R("OB", *a), R("IDN"), False, True)])
 
     def part(h):
         return [(256 * p + 128 * h, 256 * p + 128 * h + 128) for p in range(N)]
 
     def masks(h):
         for p, f in enumerate(part(h)):
-            ts(("FM",) + f, ("P%d" % (3 + h), 0, 128), float(p), A.is_equal)
+            ts(("FM",) + f, ("P%d" % (3 + h), 0, 128), (0.0, 0.25, -0.5, -0.25)[p], A.is_equal)
 
     def scans(h, ps):
         for f in [part(h)[p] for p in ps]:
@@ -388,20 +376,36 @@ def rank_program(g, core, T, topo):
         for pb, o, c in q:
             act(R("W3S", c, c + 128), (pb, o, o + 128))
 
+    anti(0)
+    prepare(0)
+    ts(K("WI", 2), C("e0"), K("RN", 0), A.mult)
+    tt(R("F1b"), R("F1b"), R("BO"), A.mult)
+    ts(K("WI", 3), K("WI", 2), 12, A.arith_shift_right)
+    lin(C("Told"), C("e0"), -1.0, float(B))
+    shares(0)
+    ts(C("w2"), K("WI", 3), 2.0, A.mult, M24, A.add)
+    ts(R("ZT"), R("RC", 0, 256), B / 4096.0, A.mult, -1920.5 + EPS, A.add)
+    sums(0)
+    lin(R("JL"), R("F1b"), 1.0, -6500.0)
+    steps(0)
+    list_z()
+
     for t in range(RO):
         land, send = "LAND%d" % t, "SEND%d" % t
-        if t == 0:
-            anti(0)
-            prepare(0)
-            prepare2(0)
-            shares(0)
         decode(t)
         if t == 0:
+            ts(R("IDN"), R("F1"), 0.0, A.is_equal)
+            ts(R("NID"), R("F1"), 0.0, A.is_equal, -1.0, A.mult)
+            ts(R("ID4"), R("F1"), 0.0, A.is_equal, 4.0, A.mult)
             cp(R("UG"), R("KRI"))
             dma("Y", T.UD[:, :], T.UG[:, 0:256], [R("UG")], [("UD", 0, 4096)])
             for l in range(16):
                 dma("Y", T.USED[l::16, 0:Q], T.UD[:, :], [("UD", 0, 4096)], [("USED", 0, Q)] if l == 15 else [], "dU")
-            act(R("NID"), R("IDN"), scale=-1.0)
+            for i in (4, 5):
+                li, o = ("LX", 128 * (i - 4), 128 * (i - 4) + 128), 128 * (i - 3)
+                do("S", lambda: g.scalar.activation(T.LX[0:8, li[1]:li[2]], T.SEL8[0:8, 0:128], F.Identity, bias=T.NF[0:8, i:i + 1], scale=0.0),
+                   [R("SEL8"), ("NF", i, i + 1)], [li])
+                mm([("P0", o, o + 128, li, ("SEL8", 0, 128, 1, 8), True, True)])
         sg("TX", "XO", 1024, 1024)
         tt(R("TX", 0, 1024), gath("XO", 0, 1024), R("TZ", 0, 1024), A.min)
         tt(R("CAND", 0, 1024), gath("YO", 0, 1024), R("TX", 0, 1024), A.min)
@@ -417,35 +421,39 @@ def rank_program(g, core, T, topo):
         tt(R("CAND", 1024, 2048), gath("ZO", 1024, 2048), R("TY", 1024, 2048), A.min)
         if t == 0:
             cp(R("WT", 0, 8), ("BO", 0, 128, 16))
-            ts(C("s4"), C("q"), -2.0, A.mult, 1.0, A.add)
+            ts(C("s4"), C("q"), -0.5, A.mult, 0.25, A.add)
+            cp(R("LOT"), ("P0", 128, 256))
+            cp(R("HIT"), ("P0", 256, 384))
             ts(R("WT", 8, 16), R("WT", 0, 8), C("s4"), A.mult)
-        sumkey(0)
+        sumkey(0, 0, 128)
         tt(R("CAND", 2048, 3072), gath("ZO", 2048, 3072), R("TZ", 2048, 3072), A.min)
         sg("TY", "YO", 3072, 512)
-        for c in (3584, 3840):
-            sg("TX", "XO", c, 256)
-            sg("TY", "YO", c, 256)
-        if t == 0:
-            act(R("ID4"), R("IDN"), scale=4.0)
-        sg("TZ", "ZO", 3584, 512)
-        for c, n, pb in ((3072, 512, "P7"), (3584, 256, "P5"), (3840, 256, "P6")):
-            add2(pb, c, n, "IDN")
-            if c == 3072:
-                codes(0)
-            tt(R("CAND", c, c + n), (pb, 0, n), R("TZ", c, c + n), A.min)
-        sumkey(1)
+        add2("P7", 3072, 512, "IDN")
+        sg("TX", "XO", 3584, 512)
+        sg("TY", "YO", 3584, 512)
+        sg("TZ", "ZO", 3072, 512)
+        codes(0)
+        add2("P5", 3584, 512, "IDN")
+        sg("TZ", "ZO", 3584, 256)
+        sg("TZ", "ZO", 3840, 256)
+        masks(0)
+        tt(R("CAND", 3072, 3584), ("P7", 0, 512), R("TZ", 3072, 3584), A.min)
+        sumkey(1, 0, 96)
+        scans(0, (0, 1))
+        tt(R("CAND", 3584, 3840), ("P5", 0, 256), R("TZ", 3584, 3840), A.min)
+        tt(R("CAND", 3840, 4096), ("P5", 256, 512), R("TZ", 3840, 4096), A.min)
+        sumkey(1, 96, 128)
         if t == 0:
             sel(R("UP"), R("BO"), [[-1, 128]], A.is_gt, 0.0, 0, 1)
             sel(R("SU"), R("BO"), [[1, 128]], A.is_gt, 0.0, 0, -1)
             act(R("NU"), R("UP"), scale=-1.0)
             act(R("BO16"), R("BO"), scale=16.0)
+            act(R("BO256"), R("BO"), scale=256.0)
             for l in range(16):
                 act(("LS", 128 * l + l, 128 * l + 128, 16), ("BO", 0, 128, 16))
             ts(R("KP"), R("R256"), C("l"), A.is_equal, 32768.0, A.mult)
-        masks(0)
-        scans(0, (0, 1))
-        codes(1)
         scans(0, (2, 3))
+        codes(1)
         counts(0, range(N))
         masks(1)
         scans(1, range(N))
@@ -468,11 +476,6 @@ def rank_program(g, core, T, topo):
         counts(1, (2, 3))
         mm([("P3", 0, 256, R("BO256"), R("I1"), True, False)])
         mm([("P3", 0, 256, R("BO16"), R("I2"), False, False)])
-        if t == 0:
-            ts(C("wi"), C("l"), 14.0, A.mult, 9.0, A.add)
-            act(R("WB"), R("BO"), scale=C("wi"))
-            act(R("WKF"), R("LS"), scale=C("wi"))
-            act(R("NBO"), R("BO"), scale=-1.0)
         if t < RO - 1:
             cp(R("RCF"), R("RC", 256 * (t + 1), 256 * (t + 1) + 256))
         scan(R("PK1"), R("KP"), ("P2", 0, 256), 0.0, A.max, A.min)
@@ -497,53 +500,73 @@ def rank_program(g, core, T, topo):
         note("G", [], [(land, 64 * p, 64 * p + 64) for p in range(N) if p != rank], ("arr%d" % t, 12), True)
         act((land, 64 * rank, 64 * rank + 64), (send, 64 * rank, 64 * rank + 64))
         if t == 0:
+            ts(C("wi"), C("l"), 3.5, A.mult, 2.25, A.add)
             ts(R("MK2"), R("R256"), C("l"), A.not_equal, 9984.0, A.mult)
+            ts(R("MKB"), R("R256"), C("l"), A.not_equal, 2.0 ** 21, A.mult)
+            ts(R("KZ"), R("R256"), 0.0, A.is_equal, ZK + 2.0 ** 20, A.mult)
             ts(R("I16"), R("I16"), C("l"), A.add)
+            ts(C("cr"), C("l"), 0.0, A.is_equal, -2048.0, A.mult)
+            ts(C("cr1"), C("l"), 1.0, A.is_equal, 0.25 - rank / 4.0, A.mult)
+            ts(R("KZ"), R("KZ"), -2.0 ** 20, A.add)
             ts(R("TB"), R("I16"), float(TR), A.add)
+            act(R("WB"), R("BO"), scale=C("wi"))
+            act(R("NBO"), R("BO"), scale=-1.0)
+            lin(C("cr"), C("cr"), 1.0, C("cr1"))
+            act(R("CR"), R("ONE256"), scale=C("cr"))
+            do("V", lambda: g.vector.reciprocal(ap(C("rc0")), ap(K("RN", 0))), [K("RN", 0)], [C("rc0")])
+            act(C("s2"), K("RN", 0), scale=1.0 / 2048)
+            fill(K("AC", 2), 256.0)
+            ts(C("aa"), C("rc0"), -2047.5, A.mult)
+            cp(K("AC", 0), C("aa"))
+            tt(K("AC", 1), C("aa"), K("AC", 0), A.subtract)
         else:
-            tt(R("UO2"), R("BC"), R("NK"), A.max)
+            tt(R("UO2"), R("BD"), R("NK"), A.max)
             cp((("USED", 0, TR + 256), R("UO2")), R("ONE256"))
         lin(C("Told"), C("Told"), 1.0, C("e%d" % t))
         lin(R("TI"), R("I16"), 1.0, C("Told"))
         if t < RO - 1:
-            act(("RN", 3 + t, 4 + t), C("e%d" % t))
+            act(K("RN", 3 + t), C("e%d" % t))
             prepare(t + 1)
             shares(t + 1)
             act(C("TqO"), C("Told"), scale=2.0 ** -12)
-        mm([("P1", 0, 256, R("WB"), R(land), True, True)])
-        mm([("P2", 0, 16, ("WKF", 128 * l, 128 * l + 128), (land, l, 256, 16), l == 0, l == 15) for l in range(16)])
-        cp(R("KRI"), ("P1", 0, 256))
-        ts(R("BRI"), R("KRI"), 2, A.arith_shift_right, 4095, A.bitwise_and)
-        cp(R("BR"), R("BRI"))
-        cp(R("KBI"), ("P2", 0, 16))
-        ts(R("NV"), ("P2", 0, 16), 0.0, A.is_lt, 4096.0, A.mult)
-        ts(R("BBI"), R("KBI"), 2, A.arith_shift_right, 4095, A.bitwise_and)
-        tt(R("BC"), R("BBI"), R("NV"), A.add)
-        cp(R("UO"), R("BC"))
-        act(R("UG"), (("USED", 0, TR + 256), R("UO")))
-        if t < RO - 1:
-            prepare2(t + 1)
+            mm([("P4", 0, 1, R("IDN"), K("AC", i), i == 0, False) for i in range(3)] + [("P0", 0, 1, R("IDN"), K("AC", 2), True, False)])
+            sums(t + 1)
+            steps(t + 1)
+        mm([("P1", 0, 256, R("BO"), R("CR"), True, False), ("P1", 0, 256, R("IDN"), R("MKB"), False, False),
+            ("P2", 0, 256, R("BO"), R("CR"), True, False), ("P3", 0, 256, R("NID"), R("MK2"), True, False)])
+        mm([("P1", 0, 256, R("WB"), R(land), False, True)])
+        mm([("P2", 0, 256, R("WB"), R(land), False, True)])
+        pk = ("PK1", 15, 256, 16)
+        scan(R("PK1"), R("KZ"), ("P1", 0, 256), 0.0, A.max, A.min)
+        ts(R("XT"), ("P2", 0, 256), M35, A.add, M35 + 4096.0, A.subtract)
+        ts(R("T16"), pk, M35, A.add, M35 + 4096.0, A.subtract)
+        tt(R("BR"), ("P2", 0, 256), R("XT"), A.subtract)
+        tt(R("BC"), pk, R("T16"), A.subtract)
+        ts(R("NV"), pk, 2.0 ** 19, A.is_ge, 4096.0, A.mult)
         for n in range(16):
             c = 4 * (n % 4) + n // 4
             o = 512 * (c // 4) + 16 * (c % 4)
-            ts(("E", o, o + 256 - 16 * c), ("BR", 16 * c, 256), ("BC", c, c + 1), A.is_equal)
-            if c == 0:
-                mm([("P3", 0, 256, R("BO"), R("E", 0, 256), True, False), ("P3", 0, 16, R("NBO"), ("E", 0, 16), False, False)])
-            elif c < 15:
+            ts(("E", o, o + 256 - 16 * c), ("BR", 16 * c, 256), 0.25, A.add, K("BC", c), A.is_equal)
+            if c < 15:
                 mm([("P3", 16 * c + 16, 256, R("BO"), ("E", o + 16, o + 256 - 16 * c), False, False)])
-            if n == 6:
-                mm([("P3", 0, 256, R("BO"), R("UG"), False, False)])
+            if n == 1:
+                tt(R("BD"), R("BC"), R("NV"), A.add)
+            if n == 3:
+                ts(R("UO"), R("BD"), -2048.25, A.add)
+                act(R("UG"), (("USED", 0, TR + 256), R("UO")), scale=-1.0)
+                lin(R("BD"), R("BD"), 1.0, -2048.25)
         mm([("P3", 64 * k, 64 * k + 64, R("SU"), ("E", 512 * k, 512 * k + 64), False, k == 3) for k in range(4)])
-        tt(R("XP"), ("P3", 0, 256), R("MK2"), A.is_gt)
+        tt(R("XP"), ("P3", 0, 256), R("UG"), A.is_gt)
         scan(("XS", 16, 272), R("XP"), R("XP"), 0.0, A.add, A.max)
         sk = ("XS", 31, 272, 16)
-        mm([("P4", 0, 16, R("NBO"), sk, True, False), ("P4", 0, 16, R("UP"), sk, False, False), ("P4", 1, 16, R("NU"), ("XS", 31, 256, 16), False, True),
-            ("P4", 16, 17, R("NBO"), ("XS", 271, 272), True, True)])
+        if t < RO - 1:
+            mm([("P4", 0, 1, R("NBO"), K("XS", 271), False, True)])
+            mm([("P0", 0, 1, R("NBO"), K("XS", 271), False, True)])
+        mm([("P5", 0, 16, R("NBO"), sk, True, False), ("P5", 0, 16, R("UP"), sk, False, False), ("P5", 1, 16, R("NU"), ("XS", 31, 256, 16), False, True)])
         tt(R("NK"), sk, ("XS", 15, 256, 16), A.subtract)
-        tt(R("NK"), R("NK"), R("TB"), A.mult)
-        tt(R("PO"), ("P4", 0, 16), R("TI"), A.add)
-        tt(R("SO"), R("PO"), R("NK"), A.max)
 
+    tt(R("NK"), R("NK"), R("TB"), A.mult)
+    places()
     cp((("BANK", 0, TR + 256), R("SO")), R("LAND%d" % (RO - 1)))
     dma("Y", T.y[:, :], T.BANK[:, B:TR], [("BANK", B, TR)], [])
     for s in sorted(count):

@@ -13,6 +13,11 @@ EPS = 2.0 ** -13
 NONE = 4096
 ZK = 2.0 ** 20 - 2047.625
 
+ORDER = "z:0:64 x:64:128 Xz:0:64 Ymax:64:128 Yx:0:64 Zy:64:128 sum:0:128 x:128:160 y:128:160 sub:128:160:P5 x:160:192 y:160:192 sub:160:192:P6 abs:128:160:P5 x:224:256 abs:160:192:P6 Zd:128:160 Zd:160:192 Yadd:240:256 Zy:240:256 x:192:224 y:192:224 add:192:224:P7 z:192:224 first:0 cut:192:224:P7 y:224:240 add:224:240:P0 z:224:240 cut:224:240:P0 sum:128:256 first:1 first:2 first:3"
+HOP = 120
+PASSES = 2
+FIX = 1
+
 SCRATCH = {}
 
 
@@ -25,8 +30,8 @@ _sb("bfloat16", BANK=TR + 256, CAND=J + DUM, TX=J, TY=J, TZ=J, USED=TR + 256, ON
     UG=256, E=2048, XP=256, XS=272, SEND0=256, SEND1=256, SEND2=256, LAND0=256, LAND1=256, LAND2=256, BO=128, BO16=128,
     BO256=128, NBO=128, IDN=128, NID=128, ID4=128, UP=128, NU=128, SU=128, WB=128, LS=2048, WT=16, KP=256, MK2=256, MKB=256, CR=256,
     rowg=128, rowl=128, rowk=128, R256=256, sB=64, IOC=256, AL=256, SG=256, GM=128, LT=1024, X1=256, X2=256, OB=256, AC=8)
-_sb("float32", sR=256, IC0=256, NIC=256, cols=64, RN=8, ra8=8, AS=8, M0=8, M1=8, AA=8, AB=8, T8=32, T9=32, PRE=4, HL=16, I16=16, TB=16,
-    TI=16, NK=16, C16=16, C256=16, W1T=64, W2S=72, W3S=1040, PK1=256, SEL8=128, NF=8, LX=256, LOT=128, HIT=128, IN2=2, CC=2,
+_sb("float32", sR=256, IC0=256, NIC=256, cols=64, RN=8, ra8=8, AS=8, M0=8, MS=8, M1=8, AA=8, AB=8, T8=32, T9=32, PRE=4, HL=16, I16=16, TB=16,
+    TI=16, NK=16, C4K=16, W1T=64, W2S=72, W3S=1088, PK1=256, SEL8=128, NF=8, LX=256, LOT=128, HIT=128, IN2=2, CC=2,
     TRI=128, ONE=128, F1=128, F1b=128, JL=128, ZT=256, RCF=256, XT=256, YT=256, BC=16, BD=16, NV=16, PO=16, KZ=256, T16=16, BIA=4)
 _sb("int32", RA=768, RB=768, RC=768, ip=8, NI=8, WI=4, KI=256, KRI=256)
 _sb("uint16", XO=256, YO=256, ZO=256, O1=16, O2=16, O3=16, UO=16, SO=16, UO2=16, BR=256)
@@ -42,7 +47,8 @@ def rank_program(g, core, T, topo):
     if rank is None:
         return
     queue = {"V": g.vector, "S": g.scalar, "P": g.tensor, "G": g, "Y": g.sync}
-    count, snap, recs, names, nd = {}, {}, {}, {}, [0]
+    count, snap, recs, names, nd, calls = {}, {}, {}, {}, [0], []
+    hold, lead = [], [0]
     known = {q: {} for q in queue}
 
     def psum(b):
@@ -75,36 +81,98 @@ def rank_program(g, core, T, topo):
             keep = [r for r in recs.get(b, []) if r[2] or r[4] != q or not (r[0] >= lo and r[1] <= hi)]
             recs[b] = keep + [(lo, hi, False, tok, q)]
 
-    def do(q, fn, reads, writes):
-        deps(q, reads, writes)
-        s = "c" + q
-        count[s] = count.get(s, 0) + 1
-        fn().then_inc(T.sem[s], 1)
-        note(q, reads, writes, (s, count[s]))
+    def later(q, issue, reads, writes, busy, more=0):
+        calls.append((q, issue, reads, writes, busy, more, list(hold), lead[0]))
+
+    def do(q, fn, reads, writes, busy=64):
+        def issue():
+            s = "c" + q
+            count[s] = count.get(s, 0) + 1
+            fn().then_inc(T.sem[s], 1)
+            note(q, reads, writes, (s, count[s]))
+        later(q, issue, reads, writes, max(busy, 64))
 
     def mm(lst, rows=(0, 128)):
         reads = [x[3][:3] for x in lst] + [x[4][:3] for x in lst]
         writes = [x[:3] for x in lst]
-        deps("P", reads, writes)
-        last = None
-        for x in lst:
-            o, c0, c1, lh, rh, st, sp = x[:7]
-            kp = rh[4] if len(rh) > 4 else 128
-            lv = T[lh[0]][0:kp, lh[1]:lh[2]:lh[3] if len(lh) > 3 else 1]
-            rv = T[rh[0]][0:kp, rh[1]:rh[2]:rh[3] if len(rh) > 3 else 1]
-            last = g.tensor.matmul(T[o][rows[0]:rows[1], c0:c1:x[7] if len(x) > 7 else 1], lv, rv, st, sp)
-        count["cP"] = count.get("cP", 0) + 1
-        last.then_inc(T.sem["cP"], 1)
-        note("P", reads, writes, ("cP", count["cP"]))
 
-    def dma(q, out, in_, reads, writes, sem=None):
-        deps(q, reads, writes)
-        if sem is None:
+        def issue():
+            last = None
+            for x in lst:
+                o, c0, c1, lh, rh, st, sp = x[:7]
+                kp = rh[4] if len(rh) > 4 else 128
+                lv = T[lh[0]][0:kp, lh[1]:lh[2]:lh[3] if len(lh) > 3 else 1]
+                rv = T[rh[0]][0:kp, rh[1]:rh[2]:rh[3] if len(rh) > 3 else 1]
+                last = g.tensor.matmul(T[o][rows[0]:rows[1], c0:c1:x[7] if len(x) > 7 else 1], lv, rv, st, sp)
+            count["cP"] = count.get("cP", 0) + 1
+            last.then_inc(T.sem["cP"], 1)
+            note("P", reads, writes, ("cP", count["cP"]))
+        later("P", issue, reads, writes, sum(max(min(64, size(x[3])), size(x[4])) * (1 if short(x[3]) else 4) for x in lst))
+
+    def dma(q, pairs, reads, writes, more):
+        def issue():
             sem = "d%d" % nd[0]
             nd[0] += 1
-        queue[q].dma_start(out, in_).then_inc(T.sem[sem], 16)
-        count[sem] = count.get(sem, 0) + 16
-        note(q, reads, writes, (sem, count[sem]))
+            for out, in_ in pairs:
+                queue[q].dma_start(out, in_).then_inc(T.sem[sem], 16)
+            count[sem] = 16 * len(pairs)
+            note(q, reads, writes, (sem, count[sem]))
+        later(q, issue, reads, writes, 64 * len(pairs), more)
+
+    def size(r):
+        return 16 * size(r[1]) if pair(r) else len(range(r[1], r[2], r[3] if len(r) > 3 else 1))
+
+    def short(*rs):
+        return all(SCRATCH[r[0]][2] in ("bfloat16", "uint16") for r in rs)
+
+    def cycles(out, in0, fast):
+        return 60 + 3.8 * size(out) if pair(out) else 70 + 1.56 * size(in0) if pair(in0) else size(in0) * fast
+
+    def schedule():
+        seen, pre = {}, []
+        for i, (q, _, reads, writes, _, _, held, _) in enumerate(calls):
+            e = {}
+            for lst, w in ((reads + held, False), (writes, True)):
+                for b, lo, hi in lst:
+                    for r in seen.get(b, []):
+                        meet = r[0] < hi and r[1] > lo and (w or r[2])
+                        if meet or (psum(b) and (r[4] != q or q == "P")):
+                            e[r[3]] = 0 if r[4] == q == "P" and psum(b) else HOP + calls[r[3]][5]
+            for lst, w in ((writes, True), (reads, False)):
+                for b, lo, hi in lst:
+                    old = seen.get(b, [])
+                    seen[b] = [r for r in old if not (w and r[0] >= lo and r[1] <= hi)] + [(lo, hi, w, i, q)]
+            pre.append(e)
+        post = [{} for _ in calls]
+        for i, e in enumerate(pre):
+            for j, gap in e.items():
+                post[j][i] = gap
+
+        def place(order, before, tail):
+            taken, end = {q: [] for q in queue}, {}
+            for i in order:
+                at, busy, l = max([end[j] + gap for j, gap in before[i].items()] + [calls[i][5] if tail else 0]), calls[i][4], taken[calls[i][0]]
+                k = len(l)
+                while k and l[k - 1][1] > at:
+                    k -= 1
+                while k < len(l) and l[k][0] < at + busy:
+                    at = max(at, l[k][1])
+                    k += 1
+                l.insert(k, (at, at + busy))
+                end[i] = at + busy
+            return end
+
+        every, best = range(len(calls)), None
+        end = place(every, pre, False)
+        for n in range(PASSES):
+            back = place(sorted(every, key=lambda i: (-end[i], -i)), post, True)
+            end = place(sorted(every, key=lambda i: (-back[i], i)), pre, False)
+            last = max(end[i] + calls[i][5] for i in every)
+            if best is None or last < best:
+                best, order = last, sorted(every, key=lambda i: (end[i] - calls[i][4], i))
+        for i in order:
+            deps(calls[i][0], calls[i][2], calls[i][3])
+            calls[i][1]()
 
     def ap(r):
         return T[r[0]][:, r[1]:r[2]:r[3]] if len(r) > 3 else T[r[0]][:, r[1]:r[2]]
@@ -125,41 +193,44 @@ def rank_program(g, core, T, topo):
         return ap(x[0]).indirect(ap(x[1])) if pair(x) else ap(x) if isinstance(x, tuple) else x
 
     def ts(out, in0, s1, op0, s2=None, op1=None):
+        n = cycles(out, in0, 0.5 if short(out, in0) else 1)
         if op1 is None:
-            do("V", lambda: g.vector.tensor_scalar(ap(out), view(in0), view(s1), None, op0), regs(in0, s1), regs(out))
+            do("V", lambda: g.vector.tensor_scalar(ap(out), view(in0), view(s1), None, op0), regs(in0, s1), regs(out), n)
         else:
-            do("V", lambda: g.vector.tensor_scalar(ap(out), view(in0), view(s1), view(s2), op0, op1), regs(in0, s1, s2), regs(out))
+            do("V", lambda: g.vector.tensor_scalar(ap(out), view(in0), view(s1), view(s2), op0, op1), regs(in0, s1, s2), regs(out), n)
 
     def tt(out, in0, in1, op):
-        do("V", lambda: g.vector.tensor_tensor(ap(out), view(in0), view(in1), op), regs(in0, in1), regs(out))
+        n = cycles(out, in0, 1 if pair(in0) or psum(in0[0]) or psum(in1[0]) else 2)
+        do("V", lambda: g.vector.tensor_tensor(ap(out), view(in0), view(in1), op), regs(in0, in1), regs(out), n)
 
     def cp(out, in0):
         if pair(out):
-            do("V", lambda: g.vector.tensor_copy(view(out), ap(in0)), regs(in0) + [out[1][:3]], [out[0][:3]])
+            do("V", lambda: g.vector.tensor_copy(view(out), ap(in0)), regs(in0) + [out[1][:3]], [out[0][:3]], cycles(out, in0, 1))
         else:
-            do("V", lambda: g.vector.tensor_copy(ap(out), view(in0)), regs(in0), regs(out))
+            do("V", lambda: g.vector.tensor_copy(ap(out), view(in0)), regs(in0), regs(out), cycles(out, in0, 0.5 if short(*regs(out, in0)) else 1))
 
     def scan(out, d0, d1, init, op0, op1):
-        do("V", lambda: g.vector.tensor_tensor_scan(ap(out), ap(d0), ap(d1), view(init), op0, op1), regs(d0, d1, init), regs(out))
+        do("V", lambda: g.vector.tensor_tensor_scan(ap(out), ap(d0), ap(d1), view(init), op0, op1), regs(d0, d1, init), regs(out),
+           cycles(out, d0, 0.5 if short(out, d0, d1) else 1))
 
     def fill(r, c):
-        do("V", lambda: g.vector.memset(ap(r), c), [], regs(r))
+        do("V", lambda: g.vector.memset(ap(r), c), [], regs(r), cycles(r, r, 0.5 if short(r) else 1))
 
     def act(out, in0, func=F.Copy, scale=1.0, acc=None, bias=0.0):
         do("S", lambda: g.scalar.activation(ap(out), view(in0), func, bias=view(bias), scale=view(scale), accum_out=view(acc)),
-           regs(in0, scale, bias), regs(out, acc))
+           regs(in0, scale, bias), regs(out, acc), cycles(out, in0, 1))
 
     def lin(out, in0, scale, bias):
         act(out, in0, F.Identity, scale, None, bias)
 
     def iota(r, pattern, base=0, cm=0):
         if SCRATCH[r[0]][2] == "int32":
-            do("G", lambda: g.iota(ap(r), pattern, base, cm), [], regs(r))
+            do("G", lambda: g.iota(ap(r), pattern, base, cm), [], regs(r), 160 + 2 * size(r))
         else:
-            do("G", lambda: g.iota(ap(r), pattern, base, cm, allow_small_or_imprecise_dtypes=True), [], regs(r))
+            do("G", lambda: g.iota(ap(r), pattern, base, cm, allow_small_or_imprecise_dtypes=True), [], regs(r), 160 + 2 * size(r))
 
     def sel(out, in0, pattern, op, fl, base, cm):
-        do("G", lambda: g.affine_select(ap(out), ap(in0), pattern, op, fl, base, cm), regs(in0), regs(out))
+        do("G", lambda: g.affine_select(ap(out), ap(in0), pattern, op, fl, base, cm), regs(in0), regs(out), 200 + 2 * size(out))
 
     def R(b, lo=0, hi=None, *step):
         return (b, lo, SCRATCH[b][1][1] if hi is None else hi) + step
@@ -172,16 +243,14 @@ def rank_program(g, core, T, topo):
             names[name] = len(names)
         return K("cols", names[name])
 
-    dma("Y", T.NI[0:8, 0:4], T.ncl[:, :], [], [("NI", 0, 4)])
-    dma("S", T.NI[0:8, 4:6], T.lim[:, :], [], [("NI", 4, 6)])
-    dma("Y", T.RC[:, 0:256], T.rc[:, 0:256], [], [R("RC", 0, 256)])
-    dma("S", T.BANK[:, 0:B], T.bank[:, :], [], [("BANK", 0, B)])
-    dma("Y", T.RA[:, 0:256], T.ra[:, 0:256], [], [R("RA", 0, 256)])
-    dma("Y", T.RB[:, 0:256], T.rb[:, 0:256], [], [R("RB", 0, 256)])
-    dma("Y", T.KRI[:, 0:256], T.used[:, :], [], [R("KRI")])
-    dma("Y", T.RC[:, 256:768], T.rc[:, 256:768], [], [R("RC", 256)])
-    dma("Y", T.RA[:, 256:768], T.ra[:, 256:768], [], [R("RA", 256)])
-    dma("Y", T.RB[:, 256:768], T.rb[:, 256:768], [], [R("RB", 256)])
+    dma("Y", [(T.NI[0:8, 0:4], T.ncl[:, :])], [], [("NI", 0, 4)], 2000)
+    dma("S", [(T.BANK[:, 0:B], T.bank[:, :])], [], [("BANK", 0, B)], 8000)
+    dma("Y", [(T.RC[:, 0:256], T.rc[:, 0:256])], [], [R("RC", 0, 256)], 3000)
+    dma("S", [(T.NI[0:8, 4:6], T.lim[:, :])], [], [("NI", 4, 6)], 2000)
+    dma("Y", [(T.RA[:, 0:256], T.ra[:, 0:256])], [], [R("RA", 0, 256)], 3000)
+    dma("Y", [(T.RB[:, 0:256], T.rb[:, 0:256])], [], [R("RB", 0, 256)], 3000)
+    dma("Y", [(T.KRI[:, 0:256], T.used[:, :])], [("BANK", 0, 16)], [R("KRI")], 3000)
+    dma("Y", [(T[r][:, 256:768], T[r.lower()][:, 256:768]) for r in ("RC", "RA", "RB")], [("BANK", 0, 16)], [R(r, 256) for r in ("RC", "RA", "RB")], 6000)
 
     ip = K("ip", 0)
     iota(ip, [[0, 1]], 0, 1)
@@ -194,12 +263,12 @@ def rank_program(g, core, T, topo):
     iota(R("R256"), [[0, 16], [1, 16]])
     iota(R("CAND", J, J + DUM), [[0, DUM]], NONE)
     iota(R("W2S", 64, 72), [[0, 8]], 1000000)
-    iota(R("W3S", 1024, 1040), [[0, 16]], 1000000)
+    iota(R("W3S", 512, 544), [[0, 32]], 1000000)
+    iota(R("W3S", 1056, 1088), [[0, 32]], 1000000)
     iota(R("LS"), [[0, 2048]])
     iota(R("sB"), [[1, 64]])
     iota(R("sR"), [[0, 4], [1, 64]])
-    iota(R("C16"), [[16, 4], [0, 4]])
-    iota(R("C256"), [[256, 4], [0, 4]])
+    iota(R("C4K"), [[4096, 4], [0, 4]])
     iota(R("I16"), [[16, 16]])
     iota(R("ONE256"), [[0, 256]], 1)
     iota(("XS", 0, 16), [[0, 16]])
@@ -231,10 +300,11 @@ def rank_program(g, core, T, topo):
     lin(C("on"), C("k6"), 1.0, m0)
     act(C("hc"), C("h"), scale=1.0 / 128)
     lin(C("jb"), C("sg"), 2032.0, 6500.0)
-    act(C("sg8"), C("sg"), scale=-8.0)
+    act(C("sg8"), C("sg"), scale=8.0)
+    act(C("hh"), C("sg"), scale=0.5)
     lin(R("AS"), R("ra8"), 1.0, C("kk"))
     act(R("ONE"), R("BO"), scale=C("h0"))
-    lin(C("gm"), C("on"), -2048.0, 2048.0)
+    lin(C("gm"), C("on"), 2048.0, -2048.0)
     lin(C("b1"), C("on"), -10000.0, 4.0 - M24)
     act(C("c7"), K("M0", 7), scale=C("h0"))
     act(C("c6"), K("M0", 6), scale=C("h0"))
@@ -244,6 +314,8 @@ def rank_program(g, core, T, topo):
     lin(C("zc"), C("h"), 0.0, -1920.5 + EPS)
     lin(C("clo"), C("c7"), -0.5, C("c6"))
     tt(C("m01"), m0, K("M0", 1), A.subtract)
+    act(C("m01s"), C("m01"), scale=EPS)
+    act(R("MS"), R("M0"), scale=EPS)
     ts(R("TRI"), R("rowk"), C("k"), A.is_gt, 2.0, A.mult)
     do("V", lambda: g.vector.tensor_copy(T.NF[0:8, 0:6], T.NI[0:8, 0:6]), [("NI", 0, 6)], [("NF", 0, 6)])
     mm([("P0", 8, 14, ("SEL8", 0, 128), ("NF", 0, 6, 1, 8), True, True)])
@@ -286,8 +358,10 @@ def rank_program(g, core, T, topo):
         tt(lo, R("PRE"), R("BIA"), A.add)
         ts(hi, lo, M27, A.add, M27, A.subtract)
         tt(lo, R("PRE"), hi, A.subtract)
-        ts(("HL", 2, 4), ("HL", 2, 4), C("chi"), A.add)
-        ts(("HL", 6, 8), ("HL", 6, 8), C("clo"), A.add)
+        ts(("HL", 0, 2), ("HL", 0, 2), EPS, A.mult)
+        ts(("HL", 4, 6), ("HL", 4, 6), EPS, A.mult)
+        ts(("HL", 2, 4), ("HL", 2, 4), C("chi"), A.add, 0.5, A.mult)
+        ts(("HL", 6, 8), ("HL", 6, 8), C("clo"), A.add, 0.5, A.mult)
 
     def gath(o, c0, c1):
         return (("BANK", 0, TR), (o, c0 // 16, c1 // 16))
@@ -305,35 +379,38 @@ def rank_program(g, core, T, topo):
     def decode(t):
         ct, c2, e = K("CC", 0), K("CC", 1), C("e%d" % t)
         if t:
-            act(e, ("P0", 0, 1))
-            lin(C("Tq"), ("P0", 0, 1), 2.0 ** -12, C("TqO"))
-            lin(R("ZT"), R("RCF"), C("Tq"), C("zc"))
             ts(C("w2"), ("P4", 0, 1), C("s2"), A.mult, M24, A.add)
+            lin(C("Tq"), ("P0", 0, 1), 2.0 ** -12, C("TqO"))
+            lin(R("ZT", 0, 128), R("RCF", 0, 128), C("Tq"), C("zc"))
+            cp(e, ("P0", 0, 1))
             tt(R("NK"), R("NK"), R("TB"), A.mult)
         ts(R("CC"), R("IN2"), C("w2"), A.add, 4.0, A.subtract)
-        if t:
-            places()
         act(R("SG"), R("NIC"), F.Sign, ct, C("cnt"), c2)
+        if t:
+            tt(R("PO"), ("P5", 0, 16), R("TI"), A.add)
+        ts(C("al"), ct, C("sg8"), A.mult)
+        ts(C("ga"), c2, C("gm"), A.mult, C("hh"), A.add)
         lo = [K("HL", 4 + i) for i in range(4)]
         if t:
             lo[0], lo[1] = K("HL", 8), K("HL", 9)
-            lin(lo[0], K("M0", 3 + t), e, K("HL", 4))
-            lin(lo[1], C("m01"), e, K("HL", 5))
-        ts(C("al"), ct, C("sg8"), A.mult)
-        ts(C("ga"), c2, C("gm"), A.mult, C("h0"), A.add)
+            ts(lo[0], e, K("MS", 3 + t), A.mult, K("HL", 4), A.add)
+            ts(lo[1], e, C("m01s"), A.mult, K("HL", 5), A.add)
+            lin(R("ZT", 128), R("RCF", 128), C("Tq"), C("zc"))
+            tt(R("SO"), R("PO"), R("NK"), A.max)
         ts(R("AL"), R("IOC"), ct, A.mult, c2, A.is_ge)
         if t:
+            cp((("BANK", 0, TR + 256), R("SO")), R("LAND%d" % (t - 1)))
             list_z()
-        ts(C("th"), C("cnt"), C("al"), A.mult, C("ga"), A.add)
-        ts(R("GM"), R("JL"), ct, A.mult, C("th"), A.is_ge)
+        lin(C("th"), C("cnt"), C("al"), C("ga"))
+        act(R("GM"), R("JL"), F.Sign, ct, None, C("th"))
         for n, (i, pb) in enumerate(((0, "P1"), (2, "P3"), (1, "P2"), (3, "P4"))):
             for u, c in enumerate((K("HL", i), lo[i])):
                 lt = ("LT", 256 * n + 128 * u, 256 * n + 128 * u + 128)
-                ts(lt, R("GM"), c, A.mult, 1.0 if i > 1 else 2.0 ** -12, A.mult)
-            mm([(pb, 0, 256, ("LT", 256 * n, 256 * n + 128), R("AL"), True, False), (pb, 0, 256, lt, R("AL"), False, True)])
-        if t:
-            cp((("BANK", 0, TR + 256), R("SO")), R("LAND%d" % (t - 1)))
-        sg("TZ", "ZO", 0, 1024)
+                if t == 0 and u:
+                    ts(lt, R("GM"), c, A.mult, c, A.add)
+                else:
+                    lin(lt, R("GM"), c, c)
+                mm([(pb, 0, 256, lt, R("AL"), u == 0, u == 1)])
         ra, rb = R("RA", 256 * t, 256 * t + 256), R("RB", 256 * t, 256 * t + 256)
         tt(R("XT"), ("P1", 0, 256), ra, A.mult)
         tt(R("YT"), ("P2", 0, 256), rb, A.mult)
@@ -353,8 +430,9 @@ def rank_program(g, core, T, topo):
         pb, pc, a = "P%d" % (1 + h), "P%d" % (3 + h), (128 * h, 128 * h + 128)
         ts(R("KI", *a), (pb, 128, 256), 0.125, A.add)
         tt(R("X1", *a), (pb, 0, 128), R("LOT"), A.is_lt)
+        mm([(pc, 0, 128, R("X1", *a), R("ID4"), True, False)])
         tt(R("X2", *a), (pb, 0, 128), R("HIT"), A.is_gt)
-        mm([(pc, 0, 128, R("X1", *a), R("ID4"), True, False), (pc, 0, 128, R("X2", *a), R("ID4"), False, False)])
+        mm([(pc, 0, 128, R("X2", *a), R("ID4"), False, False)])
         tt(R("OB", *a), (pb, 128, 256), R("KI", *a), A.subtract)
         mm([(pc, 0, 128, R("OB", *a), R("IDN"), False, True)])
 
@@ -374,6 +452,7 @@ def rank_program(g, core, T, topo):
         for pb, o, c in q:
             mm([(pb, o, o + 128, R("BO"), ("SC", c, c + 128), True, False), (pb, o, o + 128, R("NU"), ("FM", c, c + 128), False, True)])
         for pb, o, c in q:
+            c += 32 * (c // 512)
             act(R("W3S", c, c + 128), (pb, o, o + 128))
 
     anti(0)
@@ -398,94 +477,92 @@ def rank_program(g, core, T, topo):
             ts(R("NID"), R("F1"), 0.0, A.is_equal, -1.0, A.mult)
             ts(R("ID4"), R("F1"), 0.0, A.is_equal, 4.0, A.mult)
             cp(R("UG"), R("KRI"))
-            dma("Y", T.UD[:, :], T.UG[:, 0:256], [R("UG")], [("UD", 0, 4096)])
-            for l in range(16):
-                dma("Y", T.USED[l::16, 0:Q], T.UD[:, :], [("UD", 0, 4096)], [("USED", 0, Q)] if l == 15 else [], "dU")
+            dma("Y", [(T.UD[:, :], T.UG[:, 0:256])], [R("UG")], [("UD", 0, 4096)], 3000)
+            dma("Y", [(T.USED[l::16, 0:Q], T.UD[:, :]) for l in range(16)], [("UD", 0, 4096)], [("USED", 0, Q)], 4000)
             for i in (4, 5):
                 li, o = ("LX", 128 * (i - 4), 128 * (i - 4) + 128), 128 * (i - 3)
-                do("S", lambda: g.scalar.activation(T.LX[0:8, li[1]:li[2]], T.SEL8[0:8, 0:128], F.Identity, bias=T.NF[0:8, i:i + 1], scale=0.0),
+                do("S", lambda li=li, i=i: g.scalar.activation(T.LX[0:8, li[1]:li[2]], T.SEL8[0:8, 0:128], F.Identity, bias=T.NF[0:8, i:i + 1], scale=0.0),
                    [R("SEL8"), ("NF", i, i + 1)], [li])
                 mm([("P0", o, o + 128, li, ("SEL8", 0, 128, 1, 8), True, True)])
-        sg("TX", "XO", 1024, 1024)
-        tt(R("TX", 0, 1024), gath("XO", 0, 1024), R("TZ", 0, 1024), A.min)
-        tt(R("CAND", 0, 1024), gath("YO", 0, 1024), R("TX", 0, 1024), A.min)
-        for i in range(2):
-            c = 2048 + 512 * i
-            sg("TX", "XO", c, 512)
-            sg("TY", "YO", c, 512)
-            add2("P%d" % (5 + i), c, 512, "NID")
-        sg("TX", "XO", 3072, 512)
-        for i in range(2):
-            act(R("TZ", 2048 + 512 * i, 2560 + 512 * i), ("P%d" % (5 + i), 0, 512), F.Abs)
-        tt(R("TY", 1024, 2048), gath("YO", 1024, 2048), R("TX", 1024, 2048), A.max)
-        tt(R("CAND", 1024, 2048), gath("ZO", 1024, 2048), R("TY", 1024, 2048), A.min)
         if t == 0:
             cp(R("WT", 0, 8), ("BO", 0, 128, 16))
             ts(C("s4"), C("q"), -0.5, A.mult, 0.25, A.add)
             cp(R("LOT"), ("P0", 128, 256))
             cp(R("HIT"), ("P0", 256, 384))
             ts(R("WT", 8, 16), R("WT", 0, 8), C("s4"), A.mult)
-        sumkey(0, 0, 128)
-        tt(R("CAND", 2048, 3072), gath("ZO", 2048, 3072), R("TZ", 2048, 3072), A.min)
-        sg("TY", "YO", 3072, 512)
-        add2("P7", 3072, 512, "IDN")
-        sg("TX", "XO", 3584, 512)
-        sg("TY", "YO", 3584, 512)
-        sg("TZ", "ZO", 3072, 512)
-        codes(0)
-        add2("P5", 3584, 512, "IDN")
-        sg("TZ", "ZO", 3584, 256)
-        sg("TZ", "ZO", 3840, 256)
-        masks(0)
-        tt(R("CAND", 3072, 3584), ("P7", 0, 512), R("TZ", 3072, 3584), A.min)
-        sumkey(1, 0, 96)
-        scans(0, (0, 1))
-        tt(R("CAND", 3584, 3840), ("P5", 0, 256), R("TZ", 3584, 3840), A.min)
-        tt(R("CAND", 3840, 4096), ("P5", 256, 512), R("TZ", 3840, 4096), A.min)
-        sumkey(1, 96, 128)
-        if t == 0:
             sel(R("UP"), R("BO"), [[-1, 128]], A.is_gt, 0.0, 0, 1)
-            sel(R("SU"), R("BO"), [[1, 128]], A.is_gt, 0.0, 0, -1)
             act(R("NU"), R("UP"), scale=-1.0)
+        lead[0] = FIX
+        for step in ORDER.split():
+            what, c, d, pb = (step.split(":") + [""] * 3)[:4]
+            c, d = 16 * int(c or 0), 16 * int(d or 0)
+            if what in "xyz":
+                sg("T" + what.upper(), what.upper() + "O", c, d - c)
+            elif what in ("sub", "add"):
+                add2(pb, c, d - c, "NID" if what == "sub" else "IDN")
+            elif what == "abs":
+                act(R("TZ", c, d), (pb, 0, d - c), F.Abs)
+            elif what == "cut":
+                tt(R("CAND", c, d), (pb, 0, d - c), R("TZ", c, d), A.min)
+            elif what == "sum":
+                sumkey(c // 2048, c % 2048 // 16, (d - 1) % 2048 // 16 + 1)
+            elif what == "first":
+                (codes, masks, lambda h: scans(h, range(N)), lambda h: counts(h, range(N)))[c // 16](0)
+            else:
+                o, w, op = {"Xz": ("TX", "TZ", A.min), "Yx": ("CAND", "TX", A.min), "Ymax": ("TY", "TX", A.max), "Yadd": ("TY", "TX", A.add),
+                            "Zy": ("CAND", "TY", A.min), "Zd": ("CAND", "TZ", A.min)}[what]
+                tt(R(o, c, d), gath(what[0] + "O", c, d), R(w, c, d), op)
+        lead[0] = 0
+        if t == 0:
+            sel(R("SU"), R("BO"), [[1, 128]], A.is_gt, 0.0, 0, -1)
             act(R("BO16"), R("BO"), scale=16.0)
             act(R("BO256"), R("BO"), scale=256.0)
             for l in range(16):
                 act(("LS", 128 * l + l, 128 * l + 128, 16), ("BO", 0, 128, 16))
             ts(R("KP"), R("R256"), C("l"), A.is_equal, 32768.0, A.mult)
-        scans(0, (2, 3))
         codes(1)
-        counts(0, range(N))
         masks(1)
         scans(1, range(N))
         mm([("P0", 64, 128, R("BO"), ("SC", 15, 1024, 16), True, True)])
-        mm([("P7", 0, 64, ("LS", 128 * b, 128 * b + 128), ("SC", b, 1024, 16), b == 0, False) for b in range(11)])
+        for b in range(0, 16, 2):
+            mm([("P7", 0, 64, ("LS", 128 * i, 128 * i + 128), ("SC", i, 1024, 16), i == 0, i == 15) for i in (b, b + 1)])
         scan(R("W1T"), R("KP", 0, 64), ("P0", 64, 128), 0.0, A.max, A.min)
         for p in range(N):
-            ts(("I1", 64 * p, 64 * p + 64), R("sB"), ("W1T", 16 * p + 15, 16 * p + 16), A.is_ge)
-        mm([("P1", 0, 256, R("BO"), R("I1"), True, True)])
-        mm([("P7", 0, 64, ("LS", 128 * b, 128 * b + 128), ("SC", b, 1024, 16), False, b == 15) for b in range(11, 16)])
+            ts(("I1", 64 * p, 64 * p + 64), R("sB"), ("W1T", 16 * p + 15, 16 * p + 16), A.is_ge, float(p), A.add)
+            if p % 2:
+                mm([("P%d" % (1 + p // 2), 0, 128, R("BO256"), ("I1", 64 * p - 64, 64 * p + 64), True, True)])
         act(R("W2S", 0, 64), ("P7", 0, 64))
-        mm([("P2", 0, 256, R("BO16"), R("I1"), True, False)])
+        def H(b, u, w=128):
+            return (b, w * u, w * u + w)
+
+        def picks(banks):
+            for u in range(2):
+                scan(H("PK1", u), H("KP", u), (banks[u], 0, 128), 0.0, A.max, A.min)
+            return [("PK1", 128 * u + 15, 128 * u + 128, 16) for u in range(2)]
+
+        def add(banks, u, i, first, last):
+            mm([(banks[u], 0, 128, R({"I1": "BO256", "I2": "BO16", "XP": "BO"}[i]), H(i, u), first, last)])
+
+        b2, b3 = ("P3", "P4"), ("P0", "P7")
+        for u, pk in enumerate(picks(("P1", "P2"))):
+            ts(H("O1", u, 8), pk, 1.0 / 256, A.mult)
+            add(b2, u, "I1", True, False)
         counts(1, (0, 1))
-        if t < RO - 1:
-            anti(t + 1)
-        scan(R("PK1"), R("KP"), ("P1", 0, 256), 0.0, A.max, A.min)
-        tt(R("O1"), ("PK1", 15, 256, 16), R("C16"), A.add)
-        tt(R("I2"), (("W2S", 0, 72), R("O1")), R("sR"), A.is_le)
-        mm([("P2", 0, 256, R("BO"), R("I2"), False, True)])
+        for u in range(2):
+            tt(H("I2", u), (R("W2S"), H("O1", u, 8)), H("sR", u), A.is_le)
+            add(b2, u, "I2", False, True)
         counts(1, (2, 3))
-        mm([("P3", 0, 256, R("BO256"), R("I1"), True, False)])
-        mm([("P3", 0, 256, R("BO16"), R("I2"), False, False)])
-        if t < RO - 1:
-            cp(R("RCF"), R("RC", 256 * (t + 1), 256 * (t + 1) + 256))
-        scan(R("PK1"), R("KP"), ("P2", 0, 256), 0.0, A.max, A.min)
-        tt(R("O2"), ("PK1", 15, 256, 16), R("C256"), A.add)
-        tt(R("XP"), (("W3S", 0, 1040), R("O2")), R("sR"), A.is_le)
-        mm([("P3", 0, 256, R("BO"), R("XP"), False, True)])
-        scan(R("PK1"), R("KP"), ("P3", 0, 256), 0.0, A.max, A.min)
-        cp(R("O3"), ("PK1", 15, 256, 16))
-        cp(R(send), (("CAND", 0, J + DUM), R("O3")))
-        deps("G", [R(send)], [])
+        for u, pk in enumerate(picks(b2)):
+            ts(H("O2", u, 8), pk, 1.0 / 16, A.mult, -512.0 * u, A.add)
+            add(b3, u, "I1", True, False)
+            add(b3, u, "I2", False, False)
+        for u in range(2):
+            tt(H("XP", u), (H("W3S", u, 544), H("O2", u, 8)), H("sR", u), A.is_le)
+            add(b3, u, "XP", False, True)
+        for u, pk in enumerate(picks(b3)):
+            tt(H("O3", u, 8), pk, H("C4K", u, 8), A.subtract)
+        act(H(send, 0), (("CAND", 0, J + DUM), H("O3", 0, 8)))
+        cp(H(send, 1), (("CAND", 0, J + DUM), H("O3", 1, 8)))
         tr, lo = [], 0
         for d, ne in ((1, 4), (2, 4), (3, 4)):
             p = (rank + d) % N
@@ -494,11 +571,15 @@ def rank_program(g, core, T, topo):
             lo += ne
             tr.append(RemoteDMATransfer(dst_ids=[DstId(rid=rid, pnc=pid)], dma_engine_mask=mask, remote_sem=T.sem["arr%d" % t],
                                         src=T[send][:, 64 * p:64 * p + 64], dst=T[land][:, 64 * rank:64 * rank + 64]))
-        g.remote_dma_fused(tr, local_sem=T.sem["snt%d" % t])
-        count["snt%d" % t] = 12
-        count["arr%d" % t] = 12
-        note("G", [], [(land, 64 * p, 64 * p + 64) for p in range(N) if p != rank], ("arr%d" % t, 12), True)
+        others = [(land, 64 * p, 64 * p + 64) for p in range(N) if p != rank]
+
+        def write(t=t, tr=tr, others=others):
+            g.remote_dma_fused(tr, local_sem=T.sem["snt%d" % t])
+            count["snt%d" % t] = count["arr%d" % t] = 12
+            note("G", [], others, ("arr%d" % t, 12), True)
+        later("G", write, [R(send)], others, 100, 4000 if t else 7000)
         act((land, 64 * rank, 64 * rank + 64), (send, 64 * rank, 64 * rank + 64))
+        hold[:] = [R(send)]
         if t == 0:
             ts(C("wi"), C("l"), 3.5, A.mult, 2.25, A.add)
             ts(R("MK2"), R("R256"), C("l"), A.not_equal, 9984.0, A.mult)
@@ -519,21 +600,25 @@ def rank_program(g, core, T, topo):
             ts(C("aa"), C("rc0"), -2047.5, A.mult)
             cp(K("AC", 0), C("aa"))
             tt(K("AC", 1), C("aa"), K("AC", 0), A.subtract)
-        else:
-            tt(R("UO2"), R("BD"), R("NK"), A.max)
-            cp((("USED", 0, TR + 256), R("UO2")), R("ONE256"))
-        lin(C("Told"), C("Told"), 1.0, C("e%d" % t))
-        lin(R("TI"), R("I16"), 1.0, C("Told"))
-        if t < RO - 1:
-            act(K("RN", 3 + t), C("e%d" % t))
-            prepare(t + 1)
-            shares(t + 1)
-            act(C("TqO"), C("Told"), scale=2.0 ** -12)
-            mm([("P4", 0, 1, R("IDN"), K("AC", i), i == 0, False) for i in range(3)] + [("P0", 0, 1, R("IDN"), K("AC", 2), True, False)])
-            sums(t + 1)
-            steps(t + 1)
         mm([("P1", 0, 256, R("BO"), R("CR"), True, False), ("P1", 0, 256, R("IDN"), R("MKB"), False, False),
             ("P2", 0, 256, R("BO"), R("CR"), True, False), ("P3", 0, 256, R("NID"), R("MK2"), True, False)])
+        lin(C("Told"), C("Told"), 1.0, C("e%d" % t))
+        if t < RO - 1:
+            act(K("RN", 3 + t), C("e%d" % t))
+            anti(t + 1)
+            mm([("P4", 0, 1, R("IDN"), K("AC", i), i == 0, False) for i in range(3)] + [("P0", 0, 1, R("IDN"), K("AC", 2), True, False)])
+            prepare(t + 1)
+        lin(R("TI"), R("I16"), 1.0, C("Told"))
+        if t:
+            tt(R("UO2"), R("BD"), R("NK"), A.max)
+            cp((("USED", 0, TR + 256), R("UO2")), R("ONE256"))
+        if t < RO - 1:
+            shares(t + 1)
+            act(C("TqO"), C("Told"), scale=2.0 ** -12)
+            steps(t + 1)
+            cp(R("RCF"), R("RC", 256 * (t + 1), 256 * (t + 1) + 256))
+            sums(t + 1)
+        hold[:] = []
         mm([("P1", 0, 256, R("WB"), R(land), False, True)])
         mm([("P2", 0, 256, R("WB"), R(land), False, True)])
         pk = ("PK1", 15, 256, 16)
@@ -568,6 +653,7 @@ def rank_program(g, core, T, topo):
     tt(R("NK"), R("NK"), R("TB"), A.mult)
     places()
     cp((("BANK", 0, TR + 256), R("SO")), R("LAND%d" % (RO - 1)))
-    dma("Y", T.y[:, :], T.BANK[:, B:TR], [("BANK", B, TR)], [])
+    dma("Y", [(T.y[:, :], T.BANK[:, B:TR])], [("BANK", B, TR)], [], 3000)
+    schedule()
     for s in sorted(count):
         g.wait_ge(T.sem[s], count[s])

@@ -13,10 +13,30 @@ EPS = 2.0 ** -13
 NONE = 4096
 ZK = 2.0 ** 20 - 2047.625
 
-ORDER = "z:0:64 x:64:128 Xz:0:64 Ymax:64:128 Yx:0:64 Zy:64:128 sum:0:128 x:128:160 y:128:160 sub:128:160:P5 x:160:192 y:160:192 sub:160:192:P6 abs:128:160:P5 x:224:256 abs:160:192:P6 Zd:128:160 Zd:160:192 Yadd:240:256 Zy:240:256 x:192:224 y:192:224 add:192:224:P7 z:192:224 first:0 cut:192:224:P7 y:224:240 add:224:240:P0 z:224:240 cut:224:240:P0 sum:128:256 first:1 first:2 first:3"
+ORDER = "z:0:64 x:64:128 Xz:0:64 Ymax:64:128 Yx:0:64 Zy:64:128 sum:0:128 x:128:160 y:128:160 sub:128:160:P5 x:160:192 y:160:192 sub:160:192:P6 abs:128:160:P5 x:192:224 abs:160:192:P6 Zd:128:160 Yadd:192:208 first:0 Zd:160:192 Zy:192:208 x:224:256 y:208:224 add:208:224:P7 z:208:224 cut:208:224:P7 y:224:256 add:224:256:P0 first:1 sum:128:224 first:2 z:224:256 cut:224:256:P0 sum:224:256 first:3"
+ORDER1 = "z:0:64 x:64:128 Xz:0:64 Ymax:64:128 Yx:0:64 Zy:64:128 sum:0:128 x:128:160 y:128:160 sub:128:160:P5 x:160:192 y:160:192 sub:160:192:P6 abs:128:160:P5 x:192:224 y:192:224 add:192:224:P7 abs:160:192:P6 x:224:256 y:224:256 add:224:256:P0 z:192:224 z:224:256 Zd:128:160 first:0 Zd:160:192 cut:192:224:P7 sum:128:224 first:1 first:2 cut:224:256:P0 sum:224:256 first:3"
+TTG = 1.56
+FIXED = {"V": 40, "S": 50}
 HOP = 120
-PASSES = 2
+TRIES = 10000
+SLACK = 0.0015
+COSTS = ((1.3, 3.0, 60, 120, 1.2), (1.56, 3.8, 0, 100, 1.0), (2.0, 4.5, 50, 90, 0.9))
+CUT = 256
+FLY = 1000
+HOLD = ("KI", 128)
 FIX = 1
+NEAR = 300
+ISSUE = []
+BANKT = 4000
+DM = 1200
+OWN = 4
+LV = 6
+US = 8
+PARTS = (0, 128, 256)
+EG = (0, 4, 8, 12, 16)
+BRC = ((0, 256),)
+EO = (0, 4, 8, 12, 1, 5, 9, 13, 2, 6, 10, 14, 3, 7, 11, 15)
+PAIRS = ()
 
 SCRATCH = {}
 
@@ -27,12 +47,12 @@ def _sb(dtype, **kw):
 
 
 _sb("bfloat16", BANK=TR + 256, CAND=J + DUM, TX=J, TY=J, TZ=J, USED=TR + 256, ONE256=256, FM=1024, SC=1024, I1=256, I2=256,
-    UG=256, E=2048, XP=256, XS=272, SEND0=256, SEND1=256, SEND2=256, LAND0=256, LAND1=256, LAND2=256, BO=128, BO16=128,
-    BO256=128, NBO=128, IDN=128, NID=128, ID4=128, UP=128, NU=128, SU=128, WB=128, LS=2048, WT=16, KP=256, MK2=256, MKB=256, CR=256,
-    rowg=128, rowl=128, rowk=128, R256=256, sB=64, IOC=256, AL=256, SG=256, GM=128, LT=1024, X1=256, X2=256, OB=256, AC=8)
-_sb("float32", sR=256, IC0=256, NIC=256, cols=64, RN=8, ra8=8, AS=8, M0=8, MS=8, M1=8, AA=8, AB=8, T8=32, T9=32, PRE=4, HL=16, I16=16, TB=16,
-    TI=16, NK=16, C4K=16, W1T=64, W2S=72, W3S=1088, PK1=256, SEL8=128, NF=8, LX=256, LOT=128, HIT=128, IN2=2, CC=2,
-    TRI=128, ONE=128, F1=128, F1b=128, JL=128, ZT=256, RCF=256, XT=256, YT=256, BC=16, BD=16, NV=16, PO=16, KZ=256, T16=16, BIA=4)
+    UG=256, E=2048, E2=1024, E3=1024, XP=256, XS=272, SEND0=256, SEND1=256, SEND2=256, LAND0=256, LAND1=256, LAND2=256, BO=128,
+    NBO=128, IDN=128, NID=128, ID4=128, UP=128, NU=128, SU=128, WB=128, LS=2048, WT=24, KP=256, MK2=256, MKB=256, CR=256,
+    rowl=128, R256=256, sB=64, IOC=256, AL=256, SG=256, GM=128, LT=1024, X1=512, R3=256, OB=256, AC=8)
+_sb("float32", sR=256, IC0=256, NIC=256, cols=64, RN=8, ra8=8, AS=8, M0=8, MS=8, M1=8, AA=8, AB=8, T8=64, PRE=4, HL=16, I16=16, TB=16,
+    TI=16, NK=16, T2=16, T3=16, W1T=64, W2S=72, W3S=1088, PK1=256, SEL8=128, NF=8, LX=256, LOT=256, IN2=2, CC=2,
+    TRI=128, ONE=128, JL=128, ZT=256, RCF=256, XT=256, YT=256, BC=16, BI=16, BD=16, NV=16, PO=16, KZ=256, T16=16, BIA=4)
 _sb("int32", RA=768, RB=768, RC=768, ip=8, NI=8, WI=4, KI=256, KRI=256)
 _sb("uint16", XO=256, YO=256, ZO=256, O1=16, O2=16, O3=16, UO=16, SO=16, UO2=16, BR=256)
 SCRATCH["UD"] = ("dram", [8, 4096], "bfloat16")
@@ -46,9 +66,10 @@ def rank_program(g, core, T, topo):
     rank = T.rank_of(core)
     if rank is None:
         return
+    owners = sorted(range(N), key=lambda p: (p == rank, topo.die(T.cores[p]) == topo.die(core)))
     queue = {"V": g.vector, "S": g.scalar, "P": g.tensor, "G": g, "Y": g.sync}
     count, snap, recs, names, nd, calls = {}, {}, {}, {}, [0], []
-    hold, lead = [], [0]
+    hold, lead, now = [], [0], [0]
     known = {q: {} for q in queue}
 
     def psum(b):
@@ -82,15 +103,16 @@ def rank_program(g, core, T, topo):
             recs[b] = keep + [(lo, hi, False, tok, q)]
 
     def later(q, issue, reads, writes, busy, more=0):
-        calls.append((q, issue, reads, writes, busy, more, list(hold), lead[0]))
+        b, ga, sc = busy if isinstance(busy, tuple) else (busy, 0, 0)
+        calls.append((q, issue, reads, writes, b + 1.56 * ga + 3.8 * sc + FIXED.get(q, 0), more, list(hold), lead[0], (b, ga, sc)))
 
-    def do(q, fn, reads, writes, busy=64):
+    def do(q, fn, reads, writes, busy=8):
         def issue():
             s = "c" + q
             count[s] = count.get(s, 0) + 1
             fn().then_inc(T.sem[s], 1)
             note(q, reads, writes, (s, count[s]))
-        later(q, issue, reads, writes, max(busy, 64))
+        later(q, issue, reads, writes, busy if isinstance(busy, tuple) or q == "G" else busy + 20)
 
     def mm(lst, rows=(0, 128)):
         reads = [x[3][:3] for x in lst] + [x[4][:3] for x in lst]
@@ -126,11 +148,11 @@ def rank_program(g, core, T, topo):
         return all(SCRATCH[r[0]][2] in ("bfloat16", "uint16") for r in rs)
 
     def cycles(out, in0, fast):
-        return 60 + 3.8 * size(out) if pair(out) else 70 + 1.56 * size(in0) if pair(in0) else size(in0) * fast
+        return (20, 0, size(out)) if pair(out) else (20, size(in0), 0) if pair(in0) else size(in0) * fast
 
     def schedule():
         seen, pre = {}, []
-        for i, (q, _, reads, writes, _, _, held, _) in enumerate(calls):
+        for i, (q, _, reads, writes, _, _, held, _, _) in enumerate(calls):
             e = {}
             for lst, w in ((reads + held, False), (writes, True)):
                 for b, lo, hi in lst:
@@ -163,13 +185,65 @@ def rank_program(g, core, T, topo):
             return end
 
         every, best = range(len(calls)), None
-        end = place(every, pre, False)
-        for n in range(PASSES):
+        def length(end):
+            return max(end[i] + calls[i][5] for i in every)
+
+        def turn(end):
+            return sorted(every, key=lambda i: (end[i] - calls[i][4], i))
+
+        def justify(end):
             back = place(sorted(every, key=lambda i: (-end[i], -i)), post, True)
-            end = place(sorted(every, key=lambda i: (-back[i], i)), pre, False)
-            last = max(end[i] + calls[i][5] for i in every)
-            if best is None or last < best:
-                best, order = last, sorted(every, key=lambda i: (end[i] - calls[i][4], i))
+            return place(sorted(every, key=lambda i: (-back[i], i)), pre, False)
+
+        def priced(ga, sc, fixed, hop, far):
+            busy = [c[4] if c[0] not in "VS" or c[5] else 55 + ga * c[8][1] + sc * c[8][2] if c[8][1] + c[8][2] else
+                    c[8][0] - 20 + fixed if fixed else max(64, c[8][0] - 20) for c in calls]
+            return busy, [[(j, gap and hop + far * calls[j][5]) for j, gap in e.items()] for e in pre]
+
+        def replay(order, price):
+            busy, before = price
+            free, last, end, why = {}, {}, [0.0] * len(calls), [None] * len(calls)
+            for i in order:
+                q = calls[i][0]
+                at, w = free.get(q, 0.0), last.get(q)
+                why[i] = (w, True)
+                for j, gap in before[i]:
+                    if end[j] + gap >= at:
+                        at, why[i] = end[j] + gap, (j, False)
+                end[i] = free[q] = at + busy[i]
+                last[q] = i
+            i, pairs = order[-1], []
+            while why[i][0] is not None:
+                pairs += [(why[i][0], i)] if why[i][1] else []
+                i = why[i][0]
+            return end[order[-1]], pairs
+
+        if not ISSUE:
+            order, rng = turn(justify(place(every, pre, False))), np.random.default_rng(0)
+            prices = [priced(*c) for c in COSTS]
+            found = [replay(order, p) for p in prices]
+            unit = [f[0] for f in found]
+            now_ = best = 1.0
+            ISSUE.extend(order)
+            for n in range(TRIES):
+                pairs = found[n % len(prices)][1]
+                j, i = pairs[int(rng.integers(len(pairs)))]
+                a, b = order.index(j), order.index(i)
+                need = {i}
+                for x in order[b:a - 1 if a else None:-1]:
+                    if any(y in need for y in post[x]):
+                        need.add(x)
+                if j in need:
+                    continue
+                new = order[:a] + [x for x in order[a:b + 1] if x in need] + [x for x in order[a:b + 1] if x not in need] + order[b + 1:]
+                got = [replay(new, p) for p in prices]
+                mean = sum(f[0] / u for f, u in zip(got, unit)) / len(unit)
+                if mean <= now_ + SLACK * (1 - n / TRIES) * rng.random() ** 3:
+                    order, found, now_ = new, got, mean
+                    if mean < best:
+                        best = mean
+                        ISSUE[:] = order
+        order = ISSUE
         for i in order:
             deps(calls[i][0], calls[i][2], calls[i][3])
             calls[i][1]()
@@ -243,38 +317,44 @@ def rank_program(g, core, T, topo):
             names[name] = len(names)
         return K("cols", names[name])
 
-    dma("Y", [(T.NI[0:8, 0:4], T.ncl[:, :])], [], [("NI", 0, 4)], 2000)
-    dma("S", [(T.BANK[:, 0:B], T.bank[:, :])], [], [("BANK", 0, B)], 8000)
-    dma("Y", [(T.RC[:, 0:256], T.rc[:, 0:256])], [], [R("RC", 0, 256)], 3000)
-    dma("S", [(T.NI[0:8, 4:6], T.lim[:, :])], [], [("NI", 4, 6)], 2000)
-    dma("Y", [(T.RA[:, 0:256], T.ra[:, 0:256])], [], [R("RA", 0, 256)], 3000)
-    dma("Y", [(T.RB[:, 0:256], T.rb[:, 0:256])], [], [R("RB", 0, 256)], 3000)
+    dma("Y", [(T.NI[0:8, 0:4], T.ncl[:, :])], [], [("NI", 0, 4)], DM)
+    dma("S", [(T.BANK[:, 0:B], T.bank[:, :])], [], [("BANK", 0, B)], BANKT)
+    dma("Y", [(T.RC[:, 0:256], T.rc[:, 0:256])], [], [R("RC", 0, 256)], 2 * DM)
+    dma("S", [(T.NI[0:8, 4:6], T.lim[:, :])], [], [("NI", 4, 6)], 2 * DM)
+    dma("Y", [(T.RA[:, 0:256], T.ra[:, 0:256])], [], [R("RA", 0, 256)], 2 * DM)
+    dma("Y", [(T.RB[:, 0:256], T.rb[:, 0:256])], [], [R("RB", 0, 256)], 2 * DM)
     dma("Y", [(T.KRI[:, 0:256], T.used[:, :])], [("BANK", 0, 16)], [R("KRI")], 3000)
     dma("Y", [(T[r][:, 256:768], T[r.lower()][:, 256:768]) for r in ("RC", "RA", "RB")], [("BANK", 0, 16)], [R(r, 256) for r in ("RC", "RA", "RB")], 6000)
 
     ip = K("ip", 0)
     iota(ip, [[0, 1]], 0, 1)
+    def group(b, fl):
+        sel(R(b), R(b), [[-16, 8], [0, 16]], A.is_ge, fl, 0, 1)
+        sel(R(b), R(b), [[16, 8], [0, 16]], A.is_ge, fl, 15, -1)
+
+    iota(R("SEL8"), [[0, 128]], 1)
+    sel(R("SEL8"), R("SEL8"), [[-1, 8], [0, 16]], A.is_equal, 0.0, 0, 1)
     iota(R("ra8"), [[1, 8]])
-    iota(R("rowg"), [[1, 8], [0, 16]])
-    iota(R("rowk"), [[0, 16], [1, 8]])
+    iota(R("BO"), [[0, 128]], 1)
+    group("BO", 0.0)
     iota(R("IC0"), [[1, 256]])
     iota(R("rowl"), [[0, 8], [1, 16]])
-    iota(R("F1"), [[1, 128]], 0, -1)
+    for b, v in (("IDN", 1), ("NID", -1), ("ID4", 4)):
+        iota(R(b), [[0, 128]], v)
+        sel(R(b), R(b), [[-1, 128]], A.is_equal, 0.0, 0, 1)
+    iota(R("BANK", B, TR + 256), [[0, 1024]])
     iota(R("R256"), [[0, 16], [1, 16]])
     iota(R("CAND", J, J + DUM), [[0, DUM]], NONE)
-    iota(R("W2S", 64, 72), [[0, 8]], 1000000)
-    iota(R("W3S", 512, 544), [[0, 32]], 1000000)
-    iota(R("W3S", 1056, 1088), [[0, 32]], 1000000)
+    iota(R("W2S"), [[0, 72]], 1000000)
+    iota(R("W3S", 1024, 1056), [[0, 32]], 1000000)
     iota(R("LS"), [[0, 2048]])
     iota(R("sB"), [[1, 64]])
     iota(R("sR"), [[0, 4], [1, 64]])
-    iota(R("C4K"), [[4096, 4], [0, 4]])
     iota(R("I16"), [[16, 16]])
     iota(R("ONE256"), [[0, 256]], 1)
     iota(("XS", 0, 16), [[0, 16]])
     iota(R("USED", TR, TR + 256), [[0, 256]], 1)
 
-    fill(R("BANK", B, TR + 256), 0.0)
     fill(R("RN"), 0.0)
     fill(R("BIA", 0, 1), 7.5)
     fill(R("BIA", 1, 2), -7.5)
@@ -292,14 +372,12 @@ def rank_program(g, core, T, topo):
     ts(R("M0"), R("ra8"), C("k"), A.is_equal)
     ts(R("M1"), R("ra8"), C("k"), A.subtract, -1.0, A.is_equal)
     ts(C("k6"), C("k"), 6.0, A.is_ge)
-    ts(R("SEL8"), R("rowg"), C("p"), A.is_equal)
-    ts(R("BO"), R("rowg"), C("g"), A.is_equal)
     lin(C("h0"), C("h"), -1.0, 1.0)
     lin(C("sg"), C("h"), 2.0, -1.0)
     lin(C("kk"), C("k6"), 100.0, C("k"))
     lin(C("on"), C("k6"), 1.0, m0)
     act(C("hc"), C("h"), scale=1.0 / 128)
-    lin(C("jb"), C("sg"), 2032.0, 6500.0)
+    act(C("jb"), C("sg"), scale=2032.0)
     act(C("sg8"), C("sg"), scale=8.0)
     act(C("hh"), C("sg"), scale=0.5)
     lin(R("AS"), R("ra8"), 1.0, C("kk"))
@@ -316,15 +394,18 @@ def rank_program(g, core, T, topo):
     tt(C("m01"), m0, K("M0", 1), A.subtract)
     act(C("m01s"), C("m01"), scale=EPS)
     act(R("MS"), R("M0"), scale=EPS)
-    ts(R("TRI"), R("rowk"), C("k"), A.is_gt, 2.0, A.mult)
-    do("V", lambda: g.vector.tensor_copy(T.NF[0:8, 0:6], T.NI[0:8, 0:6]), [("NI", 0, 6)], [("NF", 0, 6)])
-    mm([("P0", 8, 14, ("SEL8", 0, 128), ("NF", 0, 6, 1, 8), True, True)])
-    tt(R("TRI"), R("TRI"), R("ONE"), A.mult)
+    sel(R("TRI"), R("ONE"), [[16, 8], [0, 2], [1, 8]], A.is_gt, 0.0, 0, -1)
+    ts(C("km"), C("k"), -1.0, A.add, 2.0, A.min)
+    act(C("b0"), C("on"), scale=-10000.0)
+    do("V", lambda: g.vector.tensor_copy(T.NF[0:8, 0:4], T.NI[0:8, 0:4]), [("NI", 0, 4)], [("NF", 0, 4)])
+    do("V", lambda: g.vector.tensor_copy(T.NF[0:8, 4:6], T.NI[0:8, 4:6]), [("NI", 4, 6)], [("NF", 4, 6)])
+    mm([("P0", 8, 12, ("SEL8", 0, 128), ("NF", 0, 4, 1, 8), True, True)])
     cp(("RN", 0, 3), ("P0", 8, 11))
     cp(C("e0"), ("P0", 11, 12))
     lin(R("IOC"), R("IC0"), 1.0 / 128, C("hc"))
     lin(R("NIC"), R("IC0"), -1.0 / 128, -2.0 ** -19)
-    lin(R("F1b"), R("rowl"), C("sg"), C("jb"))
+    lin(R("JL"), R("rowl"), C("sg"), C("jb"))
+    group("JL", -6500.0)
 
     def anti(t):
         ts(R("AA"), R("AS"), float(3 + t), A.is_equal)
@@ -333,7 +414,7 @@ def rank_program(g, core, T, topo):
     def prepare(t):
         for i, (m, c) in enumerate((("M0", "PNL"), ("AA", "PNR"), ("M1", "dS"), ("AB", "Qc"))):
             tt(R("T8", 8 * i, 8 * i + 8), R("RN"), R(m), A.mult)
-            act(R("T9", 8 * i, 8 * i + 8), R("T8", 8 * i, 8 * i + 8), acc=C(c))
+            act(R("T8", 32 + 8 * i, 40 + 8 * i), R("T8", 8 * i, 8 * i + 8), acc=C(c))
 
     def shares(t):
         tt(K("WI", 0), C("PNL"), C("PNR"), A.mult)
@@ -343,7 +424,7 @@ def rank_program(g, core, T, topo):
 
     def sums(t):
         ts(K("IN2", 0), ("P6", 0, 1), 4.0 - M24, A.add)
-        ts(K("IN2", 1), ("P6", 1, 2), C("b1"), A.add)
+        ts(K("IN2", 1), ("P6", 1, 2), 2.0, A.mult, C("b1"), A.add)
 
     def steps(t):
         lin(K("PRE", 0), C("dS"), -1.0, C("PNL"))
@@ -364,7 +445,7 @@ def rank_program(g, core, T, topo):
         ts(("HL", 6, 8), ("HL", 6, 8), C("clo"), A.add, 0.5, A.mult)
 
     def gath(o, c0, c1):
-        return (("BANK", 0, TR), (o, c0 // 16, c1 // 16))
+        return (("BANK", 0, B + N * CAP * now[0]), (o, c0 // 16, c1 // 16))
 
     def sg(b, o, c, n):
         act(R(b, c, c + n), gath(o, c, c + n))
@@ -379,12 +460,12 @@ def rank_program(g, core, T, topo):
     def decode(t):
         ct, c2, e = K("CC", 0), K("CC", 1), C("e%d" % t)
         if t:
-            ts(C("w2"), ("P4", 0, 1), C("s2"), A.mult, M24, A.add)
+            ts(C("w2"), ("P2", 0, 1), C("s2"), A.mult, M24, A.add)
             lin(C("Tq"), ("P0", 0, 1), 2.0 ** -12, C("TqO"))
             lin(R("ZT", 0, 128), R("RCF", 0, 128), C("Tq"), C("zc"))
-            cp(e, ("P0", 0, 1))
+            act(e, ("P0", 0, 1))
             tt(R("NK"), R("NK"), R("TB"), A.mult)
-        ts(R("CC"), R("IN2"), C("w2"), A.add, 4.0, A.subtract)
+            ts(R("CC"), R("IN2"), C("w2"), A.add, 4.0, A.subtract)
         act(R("SG"), R("NIC"), F.Sign, ct, C("cnt"), c2)
         if t:
             tt(R("PO"), ("P5", 0, 16), R("TI"), A.add)
@@ -393,47 +474,59 @@ def rank_program(g, core, T, topo):
         lo = [K("HL", 4 + i) for i in range(4)]
         if t:
             lo[0], lo[1] = K("HL", 8), K("HL", 9)
-            ts(lo[0], e, K("MS", 3 + t), A.mult, K("HL", 4), A.add)
-            ts(lo[1], e, C("m01s"), A.mult, K("HL", 5), A.add)
+            lin(lo[0], e, K("MS", 3 + t), K("HL", 4))
+            lin(lo[1], e, C("m01s"), K("HL", 5))
             lin(R("ZT", 128), R("RCF", 128), C("Tq"), C("zc"))
             tt(R("SO"), R("PO"), R("NK"), A.max)
         ts(R("AL"), R("IOC"), ct, A.mult, c2, A.is_ge)
         if t:
             cp((("BANK", 0, TR + 256), R("SO")), R("LAND%d" % (t - 1)))
             list_z()
-        lin(C("th"), C("cnt"), C("al"), C("ga"))
-        act(R("GM"), R("JL"), F.Sign, ct, None, C("th"))
+        if t:
+            lin(C("th"), C("cnt"), C("al"), C("ga"))
+            act(R("GM"), R("JL"), F.Sign, ct, None, C("th"))
+        else:
+            ts(C("nct"), ct, -1.0, A.mult)
+            ts(C("th"), C("cnt"), C("al"), A.mult, C("ga"), A.add)
+            ts(R("GM"), R("JL"), C("nct"), A.mult, C("th"), A.is_lt)
         for n, (i, pb) in enumerate(((0, "P1"), (2, "P3"), (1, "P2"), (3, "P4"))):
             for u, c in enumerate((K("HL", i), lo[i])):
                 lt = ("LT", 256 * n + 128 * u, 256 * n + 128 * u + 128)
-                if t == 0 and u:
+                if t == 0:
+                    ts(lt, R("GM"), c, A.mult, 2.0, A.mult)
+                elif 2 * n + u >= LV:
                     ts(lt, R("GM"), c, A.mult, c, A.add)
                 else:
                     lin(lt, R("GM"), c, c)
-                mm([(pb, 0, 256, lt, R("AL"), u == 0, u == 1)])
-        ra, rb = R("RA", 256 * t, 256 * t + 256), R("RB", 256 * t, 256 * t + 256)
-        tt(R("XT"), ("P1", 0, 256), ra, A.mult)
-        tt(R("YT"), ("P2", 0, 256), rb, A.mult)
-        tt(R("XT"), ("P3", 0, 256), R("XT"), A.add)
-        tt(R("YT"), ("P4", 0, 256), R("YT"), A.add)
-        ts(R("XO"), R("XT"), M23 + 1920.0, A.add, M23, A.subtract)
-        ts(R("YO"), R("YT"), M23 + 1920.0, A.add, M23, A.subtract)
+                mm([(pb, 0, CUT, lt, R("AL", 0, CUT), u == 0, u == 1)])
+        lists(t, 0, CUT, ("P1", "P3", "P2", "P4"))
+        if CUT < 256:
+            for n, pb in enumerate(("P5", "P6", "P7", "P0")):
+                mm([(pb, CUT, 256, ("LT", 256 * n + 128 * u, 256 * n + 128 * u + 128), R("AL", CUT), u == 0, u == 1) for u in range(2)])
+            lists(t, CUT, 256, ("P5", "P6", "P7", "P0"))
+
+    def lists(t, c, d, pb):
+        ra, rb = R("RA", 256 * t + c, 256 * t + d), R("RB", 256 * t + c, 256 * t + d)
+        tt(R("XT", c, d), (pb[0], c, d), ra, A.mult)
+        tt(R("YT", c, d), (pb[2], c, d), rb, A.mult)
+        tt(R("XT", c, d), (pb[1], c, d), R("XT", c, d), A.add)
+        tt(R("YT", c, d), (pb[3], c, d), R("YT", c, d), A.add)
+        ts(R("XO", c, d), R("XT", c, d), M23 + 1920.0, A.add, M23, A.subtract)
+        ts(R("YO", c, d), R("YT", c, d), M23 + 1920.0, A.add, M23, A.subtract)
 
     def add2(pb, c, n, w):
         mm([(pb, 0, n, R("IDN"), ("TX", c, c + n), True, False), (pb, 0, n, R(w), ("TY", c, c + n), False, True)])
 
     def sumkey(h, r0, r1):
         c = 2048 * h
-        mm([("P%d" % (1 + h), l, 256, ("CAND", c + 16 * r0 + l, c + 16 * r1, 16), R("WT"), True, True, 16) for l in range(16)], (r0, r1))
+        mm([("P%d" % (1 + h), l, 384, ("CAND", c + 16 * r0 + l, c + 16 * r1, 16), R("WT"), True, True, 16) for l in range(16)], (r0, r1))
 
     def codes(h):
         pb, pc, a = "P%d" % (1 + h), "P%d" % (3 + h), (128 * h, 128 * h + 128)
-        ts(R("KI", *a), (pb, 128, 256), 0.125, A.add)
-        tt(R("X1", *a), (pb, 0, 128), R("LOT"), A.is_lt)
-        mm([(pc, 0, 128, R("X1", *a), R("ID4"), True, False)])
-        tt(R("X2", *a), (pb, 0, 128), R("HIT"), A.is_gt)
-        mm([(pc, 0, 128, R("X2", *a), R("ID4"), False, False)])
-        tt(R("OB", *a), (pb, 128, 256), R("KI", *a), A.subtract)
+        ts(R("KI", *a), (pb, 256, 384), 0.125, A.add)
+        tt(R("X1", 256 * h, 256 * h + 256), (pb, 0, 256), R("LOT"), A.is_lt)
+        mm([(pc, 0, 128, R("X1", 256 * h + 128 * i, 256 * h + 128 * i + 128), R("ID4"), i == 0, False) for i in range(2)])
+        tt(R("OB", *a), (pb, 256, 384), R("KI", *a), A.subtract)
         mm([(pc, 0, 128, R("OB", *a), R("IDN"), False, True)])
 
     def part(h):
@@ -441,7 +534,7 @@ def rank_program(g, core, T, topo):
 
     def masks(h):
         for p, f in enumerate(part(h)):
-            ts(("FM",) + f, ("P%d" % (3 + h), 0, 128), (0.0, 0.25, -0.5, -0.25)[p], A.is_equal)
+            ts(("FM",) + f, ("P%d" % (3 + h), 0, 128), (0.0, 0.25, -0.5, -0.25)[owners[p]], A.is_equal)
 
     def scans(h, ps):
         for f in [part(h)[p] for p in ps]:
@@ -452,44 +545,40 @@ def rank_program(g, core, T, topo):
         for pb, o, c in q:
             mm([(pb, o, o + 128, R("BO"), ("SC", c, c + 128), True, False), (pb, o, o + 128, R("NU"), ("FM", c, c + 128), False, True)])
         for pb, o, c in q:
-            c += 32 * (c // 512)
             act(R("W3S", c, c + 128), (pb, o, o + 128))
 
     anti(0)
     prepare(0)
-    ts(K("WI", 2), C("e0"), K("RN", 0), A.mult)
-    tt(R("F1b"), R("F1b"), R("BO"), A.mult)
-    ts(K("WI", 3), K("WI", 2), 12, A.arith_shift_right)
+    for i in range(2):
+        ts(K("IN2", i), ("P0", 8 + i, 9 + i), ("P0", 11 - i, 12 - i), A.mult, 2.0 ** -11, A.mult)
+    ts(R("IN2"), R("IN2"), -1.0 + 2.0 ** -12, A.add, M24, A.add)
+    ts(R("IN2"), R("IN2"), M24, A.subtract)
+    ts(C("w2"), K("IN2", 1), C("km"), A.mult, C("b0"), A.add)
+    tt(K("CC", 0), K("IN2", 0), K("IN2", 1), A.add)
+    tt(K("CC", 1), K("IN2", 0), C("w2"), A.add)
     lin(C("Told"), C("e0"), -1.0, float(B))
-    shares(0)
-    ts(C("w2"), K("WI", 3), 2.0, A.mult, M24, A.add)
     ts(R("ZT"), R("RC", 0, 256), B / 4096.0, A.mult, -1920.5 + EPS, A.add)
-    sums(0)
-    lin(R("JL"), R("F1b"), 1.0, -6500.0)
     steps(0)
     list_z()
+    for i in (4, 5):
+        li, o = ("LX", 128 * (i - 4), 128 * (i - 4) + 128), 128 * (i - 3)
+        do("S", lambda li=li, i=i: g.scalar.activation(T.LX[0:8, li[1]:li[2]], T.SEL8[0:8, 0:128], F.Identity, bias=T.NF[0:8, i:i + 1], scale=0.0),
+           [R("SEL8"), ("NF", i, i + 1)], [li], 128)
+        mm([("P7", o, o + 128, li, ("SEL8", 0, 128, 1, 8), True, True)])
+    act(R("LOT", 0, 128), ("P7", 128, 256))
+    act(R("LOT", 128, 256), ("P7", 256, 384), scale=-1.0)
 
     for t in range(RO):
-        land, send = "LAND%d" % t, "SEND%d" % t
+        land, send, now[0] = "LAND%d" % t, "SEND%d" % t, t
         decode(t)
         if t == 0:
-            ts(R("IDN"), R("F1"), 0.0, A.is_equal)
-            ts(R("NID"), R("F1"), 0.0, A.is_equal, -1.0, A.mult)
-            ts(R("ID4"), R("F1"), 0.0, A.is_equal, 4.0, A.mult)
             cp(R("UG"), R("KRI"))
             dma("Y", [(T.UD[:, :], T.UG[:, 0:256])], [R("UG")], [("UD", 0, 4096)], 3000)
             dma("Y", [(T.USED[l::16, 0:Q], T.UD[:, :]) for l in range(16)], [("UD", 0, 4096)], [("USED", 0, Q)], 4000)
-            for i in (4, 5):
-                li, o = ("LX", 128 * (i - 4), 128 * (i - 4) + 128), 128 * (i - 3)
-                do("S", lambda li=li, i=i: g.scalar.activation(T.LX[0:8, li[1]:li[2]], T.SEL8[0:8, 0:128], F.Identity, bias=T.NF[0:8, i:i + 1], scale=0.0),
-                   [R("SEL8"), ("NF", i, i + 1)], [li])
-                mm([("P0", o, o + 128, li, ("SEL8", 0, 128, 1, 8), True, True)])
         if t == 0:
-            cp(R("WT", 0, 8), ("BO", 0, 128, 16))
-            ts(C("s4"), C("q"), -0.5, A.mult, 0.25, A.add)
-            cp(R("LOT"), ("P0", 128, 256))
-            cp(R("HIT"), ("P0", 256, 384))
-            ts(R("WT", 8, 16), R("WT", 0, 8), C("s4"), A.mult)
+            lin(C("s4"), C("q"), -0.5, 0.25)
+            for i, c in enumerate((1.0, -1.0, C("s4"))):
+                act(R("WT", 8 * i, 8 * i + 8), ("BO", 0, 128, 16), scale=c)
             sel(R("UP"), R("BO"), [[-1, 128]], A.is_gt, 0.0, 0, 1)
             act(R("NU"), R("UP"), scale=-1.0)
         lead[0] = FIX
@@ -515,74 +604,101 @@ def rank_program(g, core, T, topo):
         lead[0] = 0
         if t == 0:
             sel(R("SU"), R("BO"), [[1, 128]], A.is_gt, 0.0, 0, -1)
-            act(R("BO16"), R("BO"), scale=16.0)
-            act(R("BO256"), R("BO"), scale=256.0)
+            for u in range(len(PARTS) - 1):
+                lin(C("r%d" % u), C("l"), -16.0, -256.0 * (PARTS[u] // CAP))
+            lin(C("r3"), C("l"), -16.0, -float(J))
+            act(C("h2"), C("h0"), scale=2.0)
+            act(C("h5"), C("h"), scale=512.0)
+            for c in range(0, 256, 32):
+                first = c // CAP == max(x for x in PARTS if x <= c) // CAP
+                lin(R("R3", c, c + 32), R("R256", c, c + 32), C("h2"), C("h5") if first else 0.0)
             for l in range(16):
                 act(("LS", 128 * l + l, 128 * l + 128, 16), ("BO", 0, 128, 16))
             ts(R("KP"), R("R256"), C("l"), A.is_equal, 32768.0, A.mult)
         codes(1)
         masks(1)
         scans(1, range(N))
-        mm([("P0", 64, 128, R("BO"), ("SC", 15, 1024, 16), True, True)])
-        for b in range(0, 16, 2):
-            mm([("P7", 0, 64, ("LS", 128 * i, 128 * i + 128), ("SC", i, 1024, 16), i == 0, i == 15) for i in (b, b + 1)])
-        scan(R("W1T"), R("KP", 0, 64), ("P0", 64, 128), 0.0, A.max, A.min)
-        for p in range(N):
-            ts(("I1", 64 * p, 64 * p + 64), R("sB"), ("W1T", 16 * p + 15, 16 * p + 16), A.is_ge, float(p), A.add)
-            if p % 2:
-                mm([("P%d" % (1 + p // 2), 0, 128, R("BO256"), ("I1", 64 * p - 64, 64 * p + 64), True, True)])
-        act(R("W2S", 0, 64), ("P7", 0, 64))
-        def H(b, u, w=128):
-            return (b, w * u, w * u + w)
+        def H(b, u, k=1):
+            return (b, PARTS[u] // k, PARTS[u + 1] // k)
 
-        def picks(banks):
-            for u in range(2):
-                scan(H("PK1", u), H("KP", u), (banks[u], 0, 128), 0.0, A.max, A.min)
-            return [("PK1", 128 * u + 15, 128 * u + 128, 16) for u in range(2)]
+        def pick(bank, u):
+            scan(H("PK1", u), H("KP", u), H(bank, u), 0.0, A.max, A.min)
+            return ("PK1", PARTS[u] + 15, PARTS[u + 1], 16)
 
-        def add(banks, u, i, first, last):
-            mm([(banks[u], 0, 128, R({"I1": "BO256", "I2": "BO16", "XP": "BO"}[i]), H(i, u), first, last)])
+        def add(bank, u, i, first, last):
+            mm([H(bank, u) + (R("BO"), H(i, u), first, last)])
 
-        b2, b3 = ("P3", "P4"), ("P0", "P7")
-        for u, pk in enumerate(picks(("P1", "P2"))):
-            ts(H("O1", u, 8), pk, 1.0 / 256, A.mult)
-            add(b2, u, "I1", True, False)
+        b1, b2, b3 = ("P2", "P4", "P4"), ("P1", "P3", "P7"), ("P0", "P2", "P5")
+        for u in range(2):
+            add(b2[u], u, "R256", True, False)
+        def tables(p0, p1, bank):
+            c, d = 16 * p0, 16 * p1
+            mm([(bank, 256 + c, 256 + d, R("BO"), ("SC", 16 * c + 15, 16 * d, 16), True, True)])
+            for b in range(0, 16, 2):
+                mm([("P7", c, d, ("LS", 128 * i, 128 * i + 128), ("SC", 16 * c + i, 16 * d, 16), i == 0, i == 15) for i in (b, b + 1)])
+            scan(R("W1T", c, d), R("KP", c, d), (bank, 256 + c, 256 + d), 0.0, A.max, A.min)
+            for p in range(p0, p1):
+                ts(("I1", 64 * p, 64 * p + 64), R("sB"), ("W1T", 16 * p + 15, 16 * p + 16), A.is_ge, float(p), A.add)
+            act(R("W2S", c, d), ("P7", c, d))
+
+        tables(0, OWN, "P0")
+        for u in range(2):
+            add(b1[u], u, "I1", True, True)
         counts(1, (0, 1))
-        for u in range(2):
-            tt(H("I2", u), (R("W2S"), H("O1", u, 8)), H("sR", u), A.is_le)
-            add(b2, u, "I2", False, True)
-        counts(1, (2, 3))
-        for u, pk in enumerate(picks(b2)):
-            ts(H("O2", u, 8), pk, 1.0 / 16, A.mult, -512.0 * u, A.add)
-            add(b3, u, "I1", True, False)
-            add(b3, u, "I2", False, False)
-        for u in range(2):
-            tt(H("XP", u), (H("W3S", u, 544), H("O2", u, 8)), H("sR", u), A.is_le)
-            add(b3, u, "XP", False, True)
-        for u, pk in enumerate(picks(b3)):
-            tt(H("O3", u, 8), pk, H("C4K", u, 8), A.subtract)
-        act(H(send, 0), (("CAND", 0, J + DUM), H("O3", 0, 8)))
-        cp(H(send, 1), (("CAND", 0, J + DUM), H("O3", 1, 8)))
-        tr, lo = [], 0
-        for d, ne in ((1, 4), (2, 4), (3, 4)):
-            p = (rank + d) % N
+        counts(1, (2,) if len(PARTS) > 3 else (2, 3))
+
+        def search(us):
+            for u in us:
+                pk = pick(b1[u], u)
+                cp(H("O1", u, 16), pk)
+                lin(H("T2", u, 16), pk, 16.0, C("r%d" % u))
+                add(b3[u], u, "R3", True, False)
+            for u in us:
+                tt(H("I2", u), (R("W2S"), H("O1", u, 16)), H("sR", u), A.is_le)
+                add(b2[u], u, "I2", False, True)
+            for u in us:
+                tt(H("O2", u, 16), pick(b2[u], u), H("T2", u, 16), A.add)
+            for u in us:
+                w = 256 * (PARTS[u] // CAP)
+                tt(H("XP", u), (("W3S", w, min(w + 544, 1056)), H("O2", u, 16)), H("sR", u), A.is_le)
+                add(b3[u], u, "XP", False, True)
+                ts(H("T3", u, 16), H("O2", u, 16), 16.0, A.mult, C("r3"), A.add)
+            for u in us:
+                tt(H("O3", u, 16), pick(b3[u], u), H("T3", u, 16), A.add)
+
+        search((0, 1))
+        act(H(send, 0), (("CAND", 0, J + DUM), H("O3", 0, 16)))
+        cp(R(send, PARTS[1], 192), (("CAND", 0, J + DUM), R("O3", PARTS[1] // 16, 12)))
+        tr = []
+        for i, p in enumerate(owners[:-1]):
             rid, pid = topo.addr(T.cores[p])[:2]
-            mask = sum(1 << x for x in topo.engines(core, T.cores[p])[lo:lo + ne])
-            lo += ne
+            e = topo.engines(core, T.cores[p])
+            mask = sum(1 << x for x in (e[0::2] + e[1::2])[4 * i:4 * i + 4])
             tr.append(RemoteDMATransfer(dst_ids=[DstId(rid=rid, pnc=pid)], dma_engine_mask=mask, remote_sem=T.sem["arr%d" % t],
-                                        src=T[send][:, 64 * p:64 * p + 64], dst=T[land][:, 64 * rank:64 * rank + 64]))
-        others = [(land, 64 * p, 64 * p + 64) for p in range(N) if p != rank]
+                                        src=T[send][:, 64 * i:64 * i + 64], dst=T[land][:, 64 * rank:64 * rank + 64]))
+        others = [(land, 64 * p, 64 * p + 64) for p in owners[:-1]]
 
         def write(t=t, tr=tr, others=others):
             g.remote_dma_fused(tr, local_sem=T.sem["snt%d" % t])
             count["snt%d" % t] = count["arr%d" % t] = 12
             note("G", [], others, ("arr%d" % t, 12), True)
-        later("G", write, [R(send)], others, 100, 4000 if t else 7000)
-        act((land, 64 * rank, 64 * rank + 64), (send, 64 * rank, 64 * rank + 64))
-        hold[:] = [R(send)]
+        later("G", write, [R(send, 0, 192)], others, 100, FLY if t else 2 * FLY)
+        if len(PARTS) > 3:
+            add(b1[2], 2, "I1", True, True)
+            counts(1, (3,))
+            add(b2[2], 2, "R256", True, False)
+            search((2,))
+            act((land, 64 * rank, 64 * rank + 64), (("CAND", 0, J + DUM), R("O3", 12, 16)))
+        else:
+            cp((land, 64 * rank, 64 * rank + 64), (("CAND", 0, J + DUM), R("O3", 12, 16)))
+        hold[:] = [R(*HOLD)]
         if t == 0:
             ts(C("wi"), C("l"), 3.5, A.mult, 2.25, A.add)
             ts(R("MK2"), R("R256"), C("l"), A.not_equal, 9984.0, A.mult)
+            if PAIRS:
+                fill(R("E2"), 2.0)
+            for c in PAIRS:
+                ts(R("MK2", 16 * c + 16), R("MK2", 16 * c + 16), 32.0, A.add)
             ts(R("MKB"), R("R256"), C("l"), A.not_equal, 2.0 ** 21, A.mult)
             ts(R("KZ"), R("R256"), 0.0, A.is_equal, ZK + 2.0 ** 20, A.mult)
             ts(R("I16"), R("I16"), C("l"), A.add)
@@ -600,18 +716,21 @@ def rank_program(g, core, T, topo):
             ts(C("aa"), C("rc0"), -2047.5, A.mult)
             cp(K("AC", 0), C("aa"))
             tt(K("AC", 1), C("aa"), K("AC", 0), A.subtract)
-        mm([("P1", 0, 256, R("BO"), R("CR"), True, False), ("P1", 0, 256, R("IDN"), R("MKB"), False, False),
-            ("P2", 0, 256, R("BO"), R("CR"), True, False), ("P3", 0, 256, R("NID"), R("MK2"), True, False)])
+        for b, w, c, first in (("P1", "BO", "CR", True), ("P1", "IDN", "MKB", False), ("P4", "BO", "CR", True), ("P3", "NID", "MK2", True)):
+            mm([(b, 0, 256, R(w), R(c), first, False)])
         lin(C("Told"), C("Told"), 1.0, C("e%d" % t))
         if t < RO - 1:
             act(K("RN", 3 + t), C("e%d" % t))
             anti(t + 1)
-            mm([("P4", 0, 1, R("IDN"), K("AC", i), i == 0, False) for i in range(3)] + [("P0", 0, 1, R("IDN"), K("AC", 2), True, False)])
+            hold[:] = [R(land)]
+            mm([("P2", 0, 1, R("IDN"), K("AC", i), i == 0, False) for i in range(3)] + [("P0", 0, 1, R("IDN"), K("AC", 2), True, False)])
+            hold[:] = [R(*HOLD)]
             prepare(t + 1)
         lin(R("TI"), R("I16"), 1.0, C("Told"))
         if t:
             tt(R("UO2"), R("BD"), R("NK"), A.max)
-            cp((("USED", 0, TR + 256), R("UO2")), R("ONE256"))
+            for c in range(0, 16, US):
+                cp((("USED", 0, TR + 256), R("UO2", c, c + US)), R("ONE256", 0, 16 * US))
         if t < RO - 1:
             shares(t + 1)
             act(C("TqO"), C("Told"), scale=2.0 ** -12)
@@ -620,32 +739,44 @@ def rank_program(g, core, T, topo):
             sums(t + 1)
         hold[:] = []
         mm([("P1", 0, 256, R("WB"), R(land), False, True)])
-        mm([("P2", 0, 256, R("WB"), R(land), False, True)])
+        mm([("P4", 0, 256, R("WB"), R(land), False, True)])
         pk = ("PK1", 15, 256, 16)
         scan(R("PK1"), R("KZ"), ("P1", 0, 256), 0.0, A.max, A.min)
-        ts(R("XT"), ("P2", 0, 256), M35, A.add, M35 + 4096.0, A.subtract)
         ts(R("T16"), pk, M35, A.add, M35 + 4096.0, A.subtract)
-        tt(R("BR"), ("P2", 0, 256), R("XT"), A.subtract)
         tt(R("BC"), pk, R("T16"), A.subtract)
+        for c, d in BRC:
+            ts(R("XT", c, d), ("P4", c, d), M35, A.add, M35 + 4096.0, A.subtract)
+            tt(R("BR", c, d), ("P4", c, d), R("XT", c, d), A.subtract)
         ts(R("NV"), pk, 2.0 ** 19, A.is_ge, 4096.0, A.mult)
+        if PAIRS:
+            lin(R("BI"), R("BC"), 1.0, -0.25)
         for n in range(16):
-            c = 4 * (n % 4) + n // 4
-            o = 512 * (c // 4) + 16 * (c % 4)
-            ts(("E", o, o + 256 - 16 * c), ("BR", 16 * c, 256), 0.25, A.add, K("BC", c), A.is_equal)
-            if c < 15:
+            c = EO[n]
+            k = max(i for i in range(len(EG) - 1) if EG[i] <= c)
+            o = 256 * k + 16 * c
+            if c - 1 in PAIRS:
+                f = 256 * PAIRS.index(c - 1)
+                ts(("E2", f + 16 * c + 16, f + 256), ("BR", 16 * c + 16, 256), K("BI", c), A.is_equal, 2.0, A.add)
+                scan(("E3", f + 16 * c, f + 256), ("E", o, o + 256 - 16 * c), ("E2", f + 16 * c, f + 256), 2.0, A.min, A.add)
+                mm([("P3", 16 * c, 256, R("BO"), ("E3", f + 16 * c, f + 256), False, False)])
+                ts(("E", o, o + 16), ("BR", 16 * c, 16 * c + 16), K("BI", c), A.is_equal)
+            else:
+                ts(("E", o, o + 256 - 16 * c), ("BR", 16 * c, 256), 0.25, A.add, K("BC", c), A.is_equal)
+            if c < 15 and c not in PAIRS and c - 1 not in PAIRS:
                 mm([("P3", 16 * c + 16, 256, R("BO"), ("E", o + 16, o + 256 - 16 * c), False, False)])
+            if c + 1 == EG[k + 1]:
+                mm([("P3", 16 * EG[k], 16 * c + 16, R("SU"), ("E", 256 * k + 16 * EG[k], o + 16), False, n == 15)])
             if n == 1:
                 tt(R("BD"), R("BC"), R("NV"), A.add)
             if n == 3:
                 ts(R("UO"), R("BD"), -2048.25, A.add)
                 act(R("UG"), (("USED", 0, TR + 256), R("UO")), scale=-1.0)
                 lin(R("BD"), R("BD"), 1.0, -2048.25)
-        mm([("P3", 64 * k, 64 * k + 64, R("SU"), ("E", 512 * k, 512 * k + 64), False, k == 3) for k in range(4)])
         tt(R("XP"), ("P3", 0, 256), R("UG"), A.is_gt)
         scan(("XS", 16, 272), R("XP"), R("XP"), 0.0, A.add, A.max)
         sk = ("XS", 31, 272, 16)
         if t < RO - 1:
-            mm([("P4", 0, 1, R("NBO"), K("XS", 271), False, True)])
+            mm([("P2", 0, 1, R("NBO"), K("XS", 271), False, True)])
             mm([("P0", 0, 1, R("NBO"), K("XS", 271), False, True)])
         mm([("P5", 0, 16, R("NBO"), sk, True, False), ("P5", 0, 16, R("UP"), sk, False, False), ("P5", 1, 16, R("NU"), ("XS", 31, 256, 16), False, True)])
         tt(R("NK"), sk, ("XS", 15, 256, 16), A.subtract)

@@ -1,3 +1,4 @@
+import math
 import numpy as np
 from concourse.bass import DstId, RemoteDMATransfer
 from concourse.mybir import dt, AluOpType as A, AxisListType, ActivationFunctionType as F
@@ -8,84 +9,126 @@ DUM = 288
 M23 = 8388608.0
 M24 = 16777218.0
 M27 = 201326592.0
-M35 = 1.5 * 2.0 ** 35
+MB = 532480.0
 EPS = 2.0 ** -13
 NONE = 4096
-ZK = 2.0 ** 20 - 2047.625
+ZK = 786432.0 + 4095.875
 
-ORDER = "z:0:64 x:64:128 Xz:0:64 Ymax:64:128 Yx:0:64 Zy:64:128 sum:0:128 x:128:160 y:128:160 sub:128:160:P5 x:160:192 y:160:192 sub:160:192:P6 abs:128:160:P5 x:192:224 abs:160:192:P6 Zd:128:160 Yadd:192:208 first:0 Zd:160:192 Zy:192:208 x:224:256 y:208:224 add:208:224:P7 z:208:224 cut:208:224:P7 y:224:256 add:224:256:P0 first:1 sum:128:224 first:2 z:224:256 cut:224:256:P0 sum:224:256 first:3"
-ORDER1 = "z:0:64 x:64:128 Xz:0:64 Ymax:64:128 Yx:0:64 Zy:64:128 sum:0:128 x:128:160 y:128:160 sub:128:160:P5 x:160:192 y:160:192 sub:160:192:P6 abs:128:160:P5 x:192:224 y:192:224 add:192:224:P7 abs:160:192:P6 x:224:256 y:224:256 add:224:256:P0 z:192:224 z:224:256 Zd:128:160 first:0 Zd:160:192 cut:192:224:P7 sum:128:224 first:1 first:2 cut:224:256:P0 sum:224:256 first:3"
-TTG = 1.56
-FIXED = {"V": 40, "S": 50}
-HOP = 120
-TRIES = 10000
-SLACK = 0.0015
-COSTS = ((1.3, 3.0, 60, 120, 1.2), (1.56, 3.8, 0, 100, 1.0), (2.0, 4.5, 50, 90, 0.9))
-CUT = 256
-FLY = 1000
-HOLD = ("KI", 128)
-FIX = 1
-NEAR = 300
-ISSUE = []
-BANKT = 4000
-DM = 1200
-OWN = 4
-LV = 6
+ORDER = ("z:0:64 x:64:128 Xz:0:64 Ymax:64:128 x:128:160 y:128:160 sub:128:160:P5 Yx:0:64 x:160:192 y:160:192 sub:160:192:P6 Zy:64:128 "
+         "sum:0:128 abs:128:160:P5 x:192:224 abs:160:192:P6 Zd:128:160 Yadd:192:224 Zd:160:192 x:224:256 y:224:256 first:0 sum:128:192 "
+         "Zy:192:224 first:1 first:2 add:224:256:P0 z:224:256 sum:192:224 cut:224:256:P0 sum:224:256 first:3")
+COSTS = ((1.56, 3.8, 0, 200, 1.0), (1.3, 3.0, 40, 220, 1.2), (2.0, 4.5, 0, 160, 0.8))
+TRIES, SEED, USE, HEAT = 260000, 0, 3, (0.002, 0.0001)
+FLY = 1100
+BANKT = 6500
+DM = 2000
+LV = "VSVSVSVS"
+SV = "SVV"
+EN = dict(al="V", ga="V", th="V", T16="V", X1="SV", CD="SV", W3="VVVVVVVV", A1="V")
+PARTS = ((0, 2), (2, 3), (3, 4))
+CE = (("P7", "P3", "P7", "P3"), ("P1", "P3", "P1", "P3"))
+UK = 11
 US = 8
-PARTS = (0, 128, 256)
-EG = (0, 4, 8, 12, 16)
-BRC = ((0, 256),)
-EO = (0, 4, 8, 12, 1, 5, 9, 13, 2, 6, 10, 14, 3, 7, 11, 15)
-PAIRS = ()
+EO = (8, 10, 12, 14, 0, 2, 4, 6, 9, 11, 13, 15, 1, 3, 5, 7)
+HOLD = ("KI", 128)
+START = (0, 1)
+ORDER0 = ORDER.replace("z:0:64 ", "z:0:64 Z:224:256 ", 1).replace(" z:224:256", "")
+DIRECT = 0
+EG = 2
+FIX = "VS"
+ENG, CALLS = ((0, 2), (2, 4), (4, 6)), ((0, 3),)
+CN = ("SSSS", "SSSS")
+KEYS = (((128, 256), "P1", "P4"), ((0, 128), "P2", "P5"))
+INP = (1, 1)
+FS = 40
+PASSES, WIDE = 16, 120
+DBG = []
+ISSUE = []
 
-SCRATCH = {}
-
-
-def _sb(dtype, **kw):
-    for n, w in kw.items():
-        SCRATCH[n] = ("sbuf", [128, w], dtype)
-
-
-_sb("bfloat16", BANK=TR + 256, CAND=J + DUM, TX=J, TY=J, TZ=J, USED=TR + 256, ONE256=256, FM=1024, SC=1024, I1=256, I2=256,
-    UG=256, E=2048, E2=1024, E3=1024, XP=256, XS=272, SEND0=256, SEND1=256, SEND2=256, LAND0=256, LAND1=256, LAND2=256, BO=128,
-    NBO=128, IDN=128, NID=128, ID4=128, UP=128, NU=128, SU=128, WB=128, LS=2048, WT=24, KP=256, MK2=256, MKB=256, CR=256,
-    rowl=128, R256=256, sB=64, IOC=256, AL=256, SG=256, GM=128, LT=1024, X1=512, R3=256, OB=256, AC=8)
-_sb("float32", sR=256, IC0=256, NIC=256, cols=64, RN=8, ra8=8, AS=8, M0=8, MS=8, M1=8, AA=8, AB=8, T8=64, PRE=4, HL=16, I16=16, TB=16,
-    TI=16, NK=16, T2=16, T3=16, W1T=64, W2S=72, W3S=1088, PK1=256, SEL8=128, NF=8, LX=256, LOT=256, IN2=2, CC=2,
-    TRI=128, ONE=128, JL=128, ZT=256, RCF=256, XT=256, YT=256, BC=16, BI=16, BD=16, NV=16, PO=16, KZ=256, T16=16, BIA=4)
-_sb("int32", RA=768, RB=768, RC=768, ip=8, NI=8, WI=4, KI=256, KRI=256)
-_sb("uint16", XO=256, YO=256, ZO=256, O1=16, O2=16, O3=16, UO=16, SO=16, UO2=16, BR=256)
-SCRATCH["UD"] = ("dram", [8, 4096], "bfloat16")
+BUF = dict(bfloat16=dict(BANK=TR + 256, USED=TR + 256, CAND=J + DUM, TX=J, TY=J, TZ=J, JK=2048, JS=2048, R64=256, AL=256, SG=256, GM=128, LT=1024, X1=512, OB=256,
+                         CD=256, FM=1024, SC=1024, W3S=1088, I1=256, I2=256, XP=256, SEND=768, LAND=768, HB=256, T16=16, E=2048, UG=256, D=256,
+                         XS=272, C1=256, C0=256, LX=128, GR=128, LR=128, TM=128, BO=128, NU=128, IDN=128, NID=128, WQ=128, WB=128, JL=128,
+                         IOC=256, WT=32, S32=128, SK=384, ONE=256, R16=256, MKS=256, sR=256, KP=256, MKB=256, DG=256, CK=256, UB=256, RST=48),
+           float32=dict(ZT=256, JC=128, XT=256, YT=256, RCF=256, T2=16, T3=16, PK=256, BC=16, NK=16, PO=16, RN=48, T8=48, PB=48, CF=16, SEL=128, ACC=32, A1=32, OC=16, SV=4, IC0=256,
+                        NIC=256, ONF=128, TRI=128, KZ=256, I48=48, REP=48, E7=48, MV=48, MK=144, XW=64, I16=16, TB=32, NE=16, QR=16, QS=16, cols=96, turn=208),
+           int32=dict(RA=768, RB=768, RC=768, KI=256, WI=4, ip=12, NI=4, UI=256),
+           uint16=dict(XO=256, YO=256, ZO=256, O1=16, O2=16, O3=16, UO=16, SO=16, UO2=16, BR=256))
+PLACE, SCRATCH = {}, {}
+for _d in BUF:
+    _at = 0
+    for _n, _w in BUF[_d].items():
+        if _w > 1000:
+            SCRATCH[_n] = ("sbuf", [128, _w], _d)
+            PLACE[_n] = (_n, 0, _w, _d)
+        else:
+            PLACE[_n] = ("pool_" + _d, _at, _w, _d)
+            _at += -(-_w // 16) * 16
+    SCRATCH["pool_" + _d] = ("sbuf", [128, _at], _d)
 for _b in range(8):
     SCRATCH["P%d" % _b] = ("psum", [128, 512], "float32")
+    PLACE["P%d" % _b] = ("P%d" % _b, 0, 512, "float32")
 
-SEMAPHORES = ["cV", "cS", "cP", "cG"] + ["d%d" % i for i in range(12)] + ["dU", "arr0", "arr1", "arr2", "snt0", "snt1", "snt2"]
+SEMAPHORES = ["cV", "cS", "cP", "cG"] + ["d%d" % i for i in range(16)] + [x + str(i) for x in ("arr", "snt") for i in range(RO)]
 
 
 def rank_program(g, core, T, topo):
     rank = T.rank_of(core)
     if rank is None:
         return
-    owners = sorted(range(N), key=lambda p: (p == rank, topo.die(T.cores[p]) == topo.die(core)))
+    def order(q):
+        return sorted(range(N), key=lambda p: (p == q, topo.die(T.cores[p]) == topo.die(T.cores[q])))
+
+    owners = order(rank)
     queue = {"V": g.vector, "S": g.scalar, "P": g.tensor, "G": g, "Y": g.sync}
     count, snap, recs, names, nd, calls = {}, {}, {}, {}, [0], []
-    hold, lead, now = [], [0], [0]
     known = {q: {} for q in queue}
+    hold = []
+
+    def R(b, lo=0, hi=None, step=1, p=(0, 128)):
+        return (b, lo, PLACE[b][2] if hi is None else hi, step) + p
+
+    def K(b, i, p=(0, 128)):
+        return R(b, i, i + 1, 1, p)
+
+    def C(name, p=(0, 128)):
+        return K("cols", names.setdefault(name, len(names)), p)
+
+    def ap(r):
+        b, at = PLACE[r[0]][:2]
+        return T[b][r[4]:r[5], at + r[1]:at + r[2]:r[3]] if r[3] > 1 else T[b][r[4]:r[5], at + r[1]:at + r[2]]
+
+    def pair(x):
+        return isinstance(x, tuple) and isinstance(x[0], tuple)
+
+    def regs(*xs):
+        return [r for x in xs if isinstance(x, tuple) for r in (x if pair(x) else [x])]
+
+    def view(x):
+        return ap(x[0]).indirect(ap(x[1])) if pair(x) else ap(x) if isinstance(x, tuple) else x
 
     def psum(b):
         return b[0] == "P" and b[1:].isdigit()
 
+    def meet(r, s):
+        return r[1] < s[2] and s[1] < r[2] and r[4] < s[5] and s[4] < r[5]
+
+    def inside(r, s):
+        return s[3] == 1 and r[1] >= s[1] and r[2] <= s[2] and r[4] >= s[4] and r[5] <= s[5]
+
+    def size(r):
+        return 16 * size(r[1]) if pair(r) else len(range(r[1], r[2], r[3]))
+
+    def short(*rs):
+        return all(PLACE[r[0]][3] in ("bfloat16", "uint16") for r in rs)
+
     def deps(q, reads, writes):
         need = {}
         for lst, w in ((reads, False), (writes, True)):
-            for b, lo, hi in lst:
-                for r in recs.get(b, []):
-                    if psum(b):
-                        if r[4] == q and (q == "P" or r[0] >= hi or r[1] <= lo or not (w or r[2])):
-                            continue
-                    elif r[0] >= hi or r[1] <= lo or not (w or r[2]):
-                        continue
-                    need[r[3][0]] = max(need.get(r[3][0], 0), r[3][1])
+            for x in lst:
+                for r, wrote, tok, q2 in recs.get(x[0], []):
+                    clash = meet(r, x) and (w or wrote)
+                    if (q2 != q or clash and q != "P") if psum(x[0]) else clash:
+                        need[tok[0]] = max(need.get(tok[0], 0), tok[1])
         for s, v in need.items():
             if known[q].get(s, 0) < v:
                 queue[q].wait_ge(T.sem[s], v)
@@ -96,40 +139,31 @@ def rank_program(g, core, T, topo):
 
     def note(q, reads, writes, tok, remote=False):
         snap[tok] = {} if remote else dict(known[q])
-        for b, lo, hi in writes:
-            recs[b] = [r for r in recs.get(b, []) if not (r[0] >= lo and r[1] <= hi)] + [(lo, hi, True, tok, q)]
-        for b, lo, hi in reads:
-            keep = [r for r in recs.get(b, []) if r[2] or r[4] != q or not (r[0] >= lo and r[1] <= hi)]
-            recs[b] = keep + [(lo, hi, False, tok, q)]
+        for x in writes:
+            recs[x[0]] = [r for r in recs.get(x[0], []) if not inside(r[0], x)] + [(x, True, tok, q)]
+        for x in reads:
+            recs[x[0]] = [r for r in recs.get(x[0], []) if r[1] or r[3] != q or not inside(r[0], x)] + [(x, False, tok, q)]
 
     def later(q, issue, reads, writes, busy, more=0):
-        b, ga, sc = busy if isinstance(busy, tuple) else (busy, 0, 0)
-        calls.append((q, issue, reads, writes, b + 1.56 * ga + 3.8 * sc + FIXED.get(q, 0), more, list(hold), lead[0], (b, ga, sc)))
+        calls.append((q, issue, reads, writes, busy if isinstance(busy, tuple) else (busy, 0, 0), more, list(hold)))
 
-    def do(q, fn, reads, writes, busy=8):
+    def do(q, fn, reads, writes, busy):
         def issue():
             s = "c" + q
             count[s] = count.get(s, 0) + 1
             fn().then_inc(T.sem[s], 1)
             note(q, reads, writes, (s, count[s]))
-        later(q, issue, reads, writes, busy if isinstance(busy, tuple) or q == "G" else busy + 20)
+        later(q, issue, reads, writes, busy)
 
-    def mm(lst, rows=(0, 128)):
-        reads = [x[3][:3] for x in lst] + [x[4][:3] for x in lst]
-        writes = [x[:3] for x in lst]
+    def mm(*lst):
+        reads, writes = [x[1] for x in lst] + [x[2] for x in lst], [x[0] for x in lst]
 
         def issue():
-            last = None
-            for x in lst:
-                o, c0, c1, lh, rh, st, sp = x[:7]
-                kp = rh[4] if len(rh) > 4 else 128
-                lv = T[lh[0]][0:kp, lh[1]:lh[2]:lh[3] if len(lh) > 3 else 1]
-                rv = T[rh[0]][0:kp, rh[1]:rh[2]:rh[3] if len(rh) > 3 else 1]
-                last = g.tensor.matmul(T[o][rows[0]:rows[1], c0:c1:x[7] if len(x) > 7 else 1], lv, rv, st, sp)
+            last = [g.tensor.matmul(ap(o), ap(lh), ap(rh), st, sp) for o, lh, rh, st, sp in lst][-1]
             count["cP"] = count.get("cP", 0) + 1
             last.then_inc(T.sem["cP"], 1)
             note("P", reads, writes, ("cP", count["cP"]))
-        later("P", issue, reads, writes, sum(max(min(64, size(x[3])), size(x[4])) * (1 if short(x[3]) else 4) for x in lst))
+        later("P", issue, reads, writes, sum(max(min(64, size(x[1])), size(x[2])) * (1 if short(x[1]) else 4) for x in lst))
 
     def dma(q, pairs, reads, writes, more):
         def issue():
@@ -141,650 +175,613 @@ def rank_program(g, core, T, topo):
             note(q, reads, writes, (sem, count[sem]))
         later(q, issue, reads, writes, 64 * len(pairs), more)
 
-    def size(r):
-        return 16 * size(r[1]) if pair(r) else len(range(r[1], r[2], r[3] if len(r) > 3 else 1))
-
-    def short(*rs):
-        return all(SCRATCH[r[0]][2] in ("bfloat16", "uint16") for r in rs)
-
     def cycles(out, in0, fast):
-        return (20, 0, size(out)) if pair(out) else (20, size(in0), 0) if pair(in0) else size(in0) * fast
+        return (0, 0, size(out)) if pair(out) else (0, size(in0), 0) if pair(in0) else size(in0) * fast
 
     def schedule():
         seen, pre = {}, []
-        for i, (q, _, reads, writes, _, _, held, _, _) in enumerate(calls):
+        for i, (q, _, reads, writes, _, _, held) in enumerate(calls):
             e = {}
             for lst, w in ((reads + held, False), (writes, True)):
-                for b, lo, hi in lst:
-                    for r in seen.get(b, []):
-                        meet = r[0] < hi and r[1] > lo and (w or r[2])
-                        if meet or (psum(b) and (r[4] != q or q == "P")):
-                            e[r[3]] = 0 if r[4] == q == "P" and psum(b) else HOP + calls[r[3]][5]
+                for x in lst:
+                    for r, wrote, j, q2 in seen.get(x[0], []):
+                        if meet(r, x) and (w or wrote) or psum(x[0]) and (q2 != q or q == "P"):
+                            e[j] = not (q2 == q == "P" and psum(x[0]) or x[0] == "turn") or e.get(j, False)
             for lst, w in ((writes, True), (reads, False)):
-                for b, lo, hi in lst:
-                    old = seen.get(b, [])
-                    seen[b] = [r for r in old if not (w and r[0] >= lo and r[1] <= hi)] + [(lo, hi, w, i, q)]
+                for x in lst:
+                    seen[x[0]] = [r for r in seen.get(x[0], []) if not (w and inside(r[0], x))] + [(x, w, i, q)]
             pre.append(e)
-        post = [{} for _ in calls]
-        for i, e in enumerate(pre):
-            for j, gap in e.items():
-                post[j][i] = gap
+        every, who = range(len(calls)), [c[0] for c in calls]
+        post = [[] for _ in every]
+        for i in every:
+            for j in pre[i]:
+                post[j].append(i)
+        sinks = [i for i in every if not post[i]]
 
-        def place(order, before, tail):
-            taken, end = {q: [] for q in queue}, {}
+        def priced(ga, sc, fixed, hop, far):
+            busy = [c[4][0] if c[0] not in "VS" or c[5] else 60 + ga * c[4][1] + sc * c[4][2] if c[4][1] + c[4][2] else
+                    (c[4][0] + fixed if fixed else max(64, c[4][0])) + FS * (c[0] == "S") for c in calls]
+            return busy, [[(j, hop + far * calls[j][5] if w else 0) for j, w in e.items()] for e in pre], [far * c[5] for c in calls]
+
+        def fit(order, busy, before, head):
+            taken, end = {q: [] for q in queue}, [0.0] * len(calls)
             for i in order:
-                at, busy, l = max([end[j] + gap for j, gap in before[i].items()] + [calls[i][5] if tail else 0]), calls[i][4], taken[calls[i][0]]
+                at, l = max([end[j] + gap for j, gap in before[i]] + [head[i]]), taken[who[i]]
                 k = len(l)
                 while k and l[k - 1][1] > at:
                     k -= 1
-                while k < len(l) and l[k][0] < at + busy:
+                while k < len(l) and l[k][0] < at + busy[i]:
                     at = max(at, l[k][1])
                     k += 1
-                l.insert(k, (at, at + busy))
-                end[i] = at + busy
+                l.insert(k, (at, at + busy[i]))
+                end[i] = at + busy[i]
             return end
 
-        every, best = range(len(calls)), None
-        def length(end):
-            return max(end[i] + calls[i][5] for i in every)
+        def first(busy, before, more):
+            after = [[(j, dict(before[j])[i]) for j in post[i]] for i in every]
+            tail = more[:]
+            for i in reversed(every):
+                tail[i] = busy[i] + max([tail[i]] + [tail[j] + gap for j, gap in after[i]])
+            end = fit(sorted(every, key=lambda i: (-tail[i], i)) if START[0] else every, busy, before, [0] * len(calls))
+            for _ in range(START[1]):
+                back = fit(sorted(every, key=lambda i: (-end[i], -i)), busy, after, more)
+                end = fit(sorted(every, key=lambda i: (-back[i], i)), busy, before, [0] * len(calls))
+            return sorted(every, key=lambda i: (end[i] - busy[i], i))
 
-        def turn(end):
-            return sorted(every, key=lambda i: (end[i] - calls[i][4], i))
-
-        def justify(end):
-            back = place(sorted(every, key=lambda i: (-end[i], -i)), post, True)
-            return place(sorted(every, key=lambda i: (-back[i], i)), pre, False)
-
-        def priced(ga, sc, fixed, hop, far):
-            busy = [c[4] if c[0] not in "VS" or c[5] else 55 + ga * c[8][1] + sc * c[8][2] if c[8][1] + c[8][2] else
-                    c[8][0] - 20 + fixed if fixed else max(64, c[8][0] - 20) for c in calls]
-            return busy, [[(j, gap and hop + far * calls[j][5]) for j, gap in e.items()] for e in pre]
-
-        def replay(order, price):
-            busy, before = price
-            free, last, end, why = {}, {}, [0.0] * len(calls), [None] * len(calls)
+        def sweep(order, busy, links, end, free):
             for i in order:
-                q = calls[i][0]
-                at, w = free.get(q, 0.0), last.get(q)
-                why[i] = (w, True)
+                at = free[who[i]]
+                for j, gap in links[i]:
+                    if end[j] + gap > at:
+                        at = end[j] + gap
+                end[i] = free[who[i]] = at + busy[i]
+
+        def frame(order, a, b, price):
+            busy, before, more = price
+            end, tail, out, free, next_ = [0.0] * len(calls), [0.0] * len(calls), more[:], dict.fromkeys(queue, 0.0), dict.fromkeys(queue, 0.0)
+            sweep(order[:a], busy, before, end, free)
+            for i in reversed(order[b:]):
+                tail[i] = next_[who[i]] = busy[i] + max(out[i], next_[who[i]])
                 for j, gap in before[i]:
-                    if end[j] + gap >= at:
-                        at, why[i] = end[j] + gap, (j, False)
-                end[i] = free[q] = at + busy[i]
-                last[q] = i
-            i, pairs = order[-1], []
-            while why[i][0] is not None:
-                pairs += [(why[i][0], i)] if why[i][1] else []
-                i = why[i][0]
-            return end[order[-1]], pairs
+                    out[j] = max(out[j], gap + tail[i])
+            return busy, before, end, free, out, next_, max([end[i] + out[i] for i in order[:a]] + [0.0])
+
+        def run(part, f):
+            busy, before, end, free, out, next_, rest = f
+            end, free = end[:], dict(free)
+            sweep(part, busy, before, end, free)
+            return max(rest, max([end[i] + out[i] for i in part]), max([free[q] + next_[q] for q in free])), end
+
+        def path(part, f, got):
+            busy, before, _, _, out, next_, _ = f
+            (total, end), last, prev, pairs = got, {}, {}, []
+            for i in part:
+                prev[i], last[who[i]] = last.get(who[i]), i
+            w = [i for i in part if end[i] + out[i] >= total - 1e-6] + [i for q, i in last.items() if end[i] + next_[q] >= total - 1e-6]
+            while w and w[0] in prev:
+                i = w[0]
+                at = end[i] - busy[i] - 1e-6
+                w = [j for j, gap in before[i] if end[j] + gap >= at]
+                if not w and prev[i] is not None and end[prev[i]] >= at:
+                    pairs.append((prev[i], i))
+                    w = [prev[i]]
+            return pairs
+
+        def move(part, j, i, far, ahead):
+            a, b = part.index(j), part.index(i)
+            if ahead:
+                a = ([a] + [x for x in range(a - 1, max(a - 40, -1), -1) if who[part[x]] == who[i]])[:far + 1][-1]
+                need = {i}
+                for x in reversed(part[a:b + 1]):
+                    if not need.isdisjoint(post[x]):
+                        need.add(x)
+            else:
+                b = ([b] + [x for x in range(b + 1, min(b + 40, len(part))) if who[part[x]] == who[i]])[:far + 1][-1]
+                need = {j}
+                for x in part[a:b + 1]:
+                    if not need.isdisjoint(pre[x]):
+                        need.add(x)
+            if part[a if ahead else b] not in need:
+                return part[:a] + sorted(part[a:b + 1], key=lambda x: (x in need) != ahead) + part[b + 1:]
 
         if not ISSUE:
-            order, rng = turn(justify(place(every, pre, False))), np.random.default_rng(0)
-            prices = [priced(*c) for c in COSTS]
-            found = [replay(order, p) for p in prices]
-            unit = [f[0] for f in found]
-            now_ = best = 1.0
+            prices, rng = [priced(*c) for c in COSTS[:USE]], np.random.default_rng(SEED)
+            def length(order):
+                return [run(order, frame(order, 0, len(order), p))[0] for p in prices]
+            order = min((first(*p) for p in prices), key=lambda o: sum(length(o)))
+            unit, best = length(order), 1.0
             ISSUE.extend(order)
-            for n in range(TRIES):
-                pairs = found[n % len(prices)][1]
-                j, i = pairs[int(rng.integers(len(pairs)))]
-                a, b = order.index(j), order.index(i)
-                need = {i}
-                for x in order[b:a - 1 if a else None:-1]:
-                    if any(y in need for y in post[x]):
-                        need.add(x)
-                if j in need:
-                    continue
-                new = order[:a] + [x for x in order[a:b + 1] if x in need] + [x for x in order[a:b + 1] if x not in need] + order[b + 1:]
-                got = [replay(new, p) for p in prices]
-                mean = sum(f[0] / u for f, u in zip(got, unit)) / len(unit)
-                if mean <= now_ + SLACK * (1 - n / TRIES) * rng.random() ** 3:
-                    order, found, now_ = new, got, mean
-                    if mean < best:
-                        best = mean
-                        ISSUE[:] = order
-        order = ISSUE
-        for i in order:
+            starts = [a for n in range(PASSES) for a in range(-(n % 2) * WIDE // 4, len(calls) - WIDE // 2, WIDE // 2)]
+            for n, a in enumerate(starts):
+                a, b, heat = max(a, 0), a + WIDE, HEAT[0] * (HEAT[1] / HEAT[0]) ** (n / len(starts))
+                part, frames = order[a:b], [frame(order, a, b, p) for p in prices]
+                got = [run(part, f) for f in frames]
+                paths, now = [path(part, f, x) for f, x in zip(frames, got)], sum(x[0] / u for x, u in zip(got, unit)) / USE
+                for d0, d1, d2, d3, d4 in rng.random((TRIES // len(starts), 5)).tolist():
+                    pairs = paths[int(d4 * USE)]
+                    new = pairs and move(part, *pairs[int(d0 * len(pairs))], (0, 0, 1, 2, 4)[int(d1 * 5)], d2 < 0.5)
+                    if new:
+                        got = [run(new, f) for f in frames]
+                        mean = sum(x[0] / u for x, u in zip(got, unit)) / USE
+                        if mean <= now - heat * math.log(1 - d3):
+                            part, now, paths = new, mean, [path(new, f, x) for f, x in zip(frames, got)]
+                            if mean < best:
+                                best = mean
+                                ISSUE[:] = order[:a] + part + order[b:]
+                order = order[:a] + part + order[b:]
+            DBG.extend([unit, best])
+        for i in ISSUE:
             deps(calls[i][0], calls[i][2], calls[i][3])
             calls[i][1]()
 
-    def ap(r):
-        return T[r[0]][:, r[1]:r[2]:r[3]] if len(r) > 3 else T[r[0]][:, r[1]:r[2]]
-
-    def pair(x):
-        return isinstance(x, tuple) and isinstance(x[0], tuple)
-
-    def regs(*xs):
-        out = []
-        for x in xs:
-            if pair(x):
-                out += [x[0][:3], x[1][:3]]
-            elif isinstance(x, tuple):
-                out.append(x[:3])
-        return out
-
-    def view(x):
-        return ap(x[0]).indirect(ap(x[1])) if pair(x) else ap(x) if isinstance(x, tuple) else x
-
     def ts(out, in0, s1, op0, s2=None, op1=None):
-        n = cycles(out, in0, 0.5 if short(out, in0) else 1)
+        n = cycles(out, in0, 0.5 if short(*regs(out, in0)) else 1)
         if op1 is None:
-            do("V", lambda: g.vector.tensor_scalar(ap(out), view(in0), view(s1), None, op0), regs(in0, s1), regs(out), n)
+            do("V", lambda: g.vector.tensor_scalar(ap(out), view(in0), view(s1), None, op0), regs(in0, s1), [out], n)
         else:
-            do("V", lambda: g.vector.tensor_scalar(ap(out), view(in0), view(s1), view(s2), op0, op1), regs(in0, s1, s2), regs(out), n)
+            do("V", lambda: g.vector.tensor_scalar(ap(out), view(in0), view(s1), view(s2), op0, op1), regs(in0, s1, s2), [out], n)
 
     def tt(out, in0, in1, op):
         n = cycles(out, in0, 1 if pair(in0) or psum(in0[0]) or psum(in1[0]) else 2)
-        do("V", lambda: g.vector.tensor_tensor(ap(out), view(in0), view(in1), op), regs(in0, in1), regs(out), n)
+        do("V", lambda: g.vector.tensor_tensor(ap(out), view(in0), view(in1), op), regs(in0, in1), [out], n)
 
     def cp(out, in0):
         if pair(out):
-            do("V", lambda: g.vector.tensor_copy(view(out), ap(in0)), regs(in0) + [out[1][:3]], [out[0][:3]], cycles(out, in0, 1))
+            do("V", lambda: g.vector.tensor_copy(view(out), ap(in0)), [in0, out[1]], [out[0]], cycles(out, in0, 1))
         else:
-            do("V", lambda: g.vector.tensor_copy(ap(out), view(in0)), regs(in0), regs(out), cycles(out, in0, 0.5 if short(*regs(out, in0)) else 1))
+            do("V", lambda: g.vector.tensor_copy(ap(out), view(in0)), regs(in0), [out], cycles(out, in0, 0.5 if short(*regs(out, in0)) else 1))
 
     def scan(out, d0, d1, init, op0, op1):
-        do("V", lambda: g.vector.tensor_tensor_scan(ap(out), ap(d0), ap(d1), view(init), op0, op1), regs(d0, d1, init), regs(out),
+        do("V", lambda: g.vector.tensor_tensor_scan(ap(out), ap(d0), ap(d1), view(init), op0, op1), regs(d0, d1, init), [out],
            cycles(out, d0, 0.5 if short(out, d0, d1) else 1))
 
     def fill(r, c):
-        do("V", lambda: g.vector.memset(ap(r), c), [], regs(r), cycles(r, r, 0.5 if short(r) else 1))
+        do("V", lambda: g.vector.memset(ap(r), c), [], [r], cycles(r, r, 0.5 if short(r) else 1))
 
     def act(out, in0, func=F.Copy, scale=1.0, acc=None, bias=0.0):
+        n = cycles(out, in0, 1)
         do("S", lambda: g.scalar.activation(ap(out), view(in0), func, bias=view(bias), scale=view(scale), accum_out=view(acc)),
-           regs(in0, scale, bias), regs(out, acc), cycles(out, in0, 1))
+           regs(in0, scale, bias), regs(out, acc), max(n, 64) + 24 if acc else n)
 
-    def lin(out, in0, scale, bias):
-        act(out, in0, F.Identity, scale, None, bias)
+    def lin(out, in0, scale, bias, q="S"):
+        if q == "S":
+            act(out, in0, F.Identity, scale, None, bias)
+        else:
+            ts(out, in0, scale, A.mult, bias, A.add)
 
     def iota(r, pattern, base=0, cm=0):
-        if SCRATCH[r[0]][2] == "int32":
-            do("G", lambda: g.iota(ap(r), pattern, base, cm), [], regs(r), 160 + 2 * size(r))
+        if PLACE[r[0]][3] == "int32":
+            do("G", lambda: g.iota(ap(r), pattern, base, cm), [], [r], 160 + 2 * size(r))
         else:
-            do("G", lambda: g.iota(ap(r), pattern, base, cm, allow_small_or_imprecise_dtypes=True), [], regs(r), 160 + 2 * size(r))
+            do("G", lambda: g.iota(ap(r), pattern, base, cm, allow_small_or_imprecise_dtypes=True), [], [r], 160 + 2 * size(r))
 
     def sel(out, in0, pattern, op, fl, base, cm):
-        do("G", lambda: g.affine_select(ap(out), ap(in0), pattern, op, fl, base, cm), regs(in0), regs(out), 200 + 2 * size(out))
+        do("G", lambda: g.affine_select(ap(out), ap(in0), pattern, op, fl, base, cm), [in0], [out], 200 + 2 * size(out))
 
-    def R(b, lo=0, hi=None, *step):
-        return (b, lo, SCRATCH[b][1][1] if hi is None else hi) + step
-
-    def K(b, i):
-        return (b, i, i + 1)
-
-    def C(name):
-        if name not in names:
-            names[name] = len(names)
-        return K("cols", names[name])
-
-    dma("Y", [(T.NI[0:8, 0:4], T.ncl[:, :])], [], [("NI", 0, 4)], DM)
-    dma("S", [(T.BANK[:, 0:B], T.bank[:, :])], [], [("BANK", 0, B)], BANKT)
-    dma("Y", [(T.RC[:, 0:256], T.rc[:, 0:256])], [], [R("RC", 0, 256)], 2 * DM)
-    dma("S", [(T.NI[0:8, 4:6], T.lim[:, :])], [], [("NI", 4, 6)], 2 * DM)
-    dma("Y", [(T.RA[:, 0:256], T.ra[:, 0:256])], [], [R("RA", 0, 256)], 2 * DM)
-    dma("Y", [(T.RB[:, 0:256], T.rb[:, 0:256])], [], [R("RB", 0, 256)], 2 * DM)
-    dma("Y", [(T.KRI[:, 0:256], T.used[:, :])], [("BANK", 0, 16)], [R("KRI")], 3000)
-    dma("Y", [(T[r][:, 256:768], T[r.lower()][:, 256:768]) for r in ("RC", "RA", "RB")], [("BANK", 0, 16)], [R(r, 256) for r in ("RC", "RA", "RB")], 6000)
+    p32, ni = (0, 32), PLACE["NI"][1]
+    dma("Y", [(T.pool_int32[0:32, ni:ni + 1], T.ncl[:, :])], [], [K("NI", 0)], DM)
+    for b, n, more in (("RC", 256, DM + 900), ("BANK", B, BANKT), ("RA", 256, BANKT + 800), ("RB", 256, BANKT + 1600)):
+        calls[-1][3].append(K("turn", len(calls)))
+        hold[:] = [K("turn", len(calls))]
+        dma("Y", [(ap(R(b, 0, n)), T[b.lower()][:, 0:n])], [], [R(b, 0, n)], more)
+    calls[-1][3].append(K("turn", len(calls)))
+    hold[:] = [K("turn", len(calls))]
+    dma("Y", [(T.pool_int32[i:32:2, ni + 1:ni + 2], T.lim[:, :]) for i in range(2)], [], [K("NI", 1)], BANKT + 900)
+    hold[:] = []
+    dma("Y", [(ap(R("UI")), T.used[:, :])], [R("BANK", 0, 16)], [R("UI")], 2 * DM)
+    dma("Y", [(ap(R(b, 256)), T[b.lower()][:, 256:768]) for b in ("RC", "RA", "RB")], [R("BANK", 0, 16)], [R(b, 256) for b in ("RC", "RA", "RB")], 3 * DM)
 
     ip = K("ip", 0)
     iota(ip, [[0, 1]], 0, 1)
-    def group(b, fl):
-        sel(R(b), R(b), [[-16, 8], [0, 16]], A.is_ge, fl, 0, 1)
-        sel(R(b), R(b), [[16, 8], [0, 16]], A.is_ge, fl, 15, -1)
-
-    iota(R("SEL8"), [[0, 128]], 1)
-    sel(R("SEL8"), R("SEL8"), [[-1, 8], [0, 16]], A.is_equal, 0.0, 0, 1)
-    iota(R("ra8"), [[1, 8]])
-    iota(R("BO"), [[0, 128]], 1)
-    group("BO", 0.0)
+    iota(R("GR"), [[1, 8], [0, 16]])
+    iota(R("I48"), [[0, 6], [1, 8]])
+    iota(R("I16"), [[1, 16]])
+    iota(R("LR"), [[0, 8], [1, 16]])
     iota(R("IC0"), [[1, 256]])
-    iota(R("rowl"), [[0, 8], [1, 16]])
-    for b, v in (("IDN", 1), ("NID", -1), ("ID4", 4)):
-        iota(R(b), [[0, 128]], v)
-        sel(R(b), R(b), [[-1, 128]], A.is_equal, 0.0, 0, 1)
-    iota(R("BANK", B, TR + 256), [[0, 1024]])
-    iota(R("R256"), [[0, 16], [1, 16]])
-    iota(R("CAND", J, J + DUM), [[0, DUM]], NONE)
-    iota(R("W2S"), [[0, 72]], 1000000)
-    iota(R("W3S", 1024, 1056), [[0, 32]], 1000000)
-    iota(R("LS"), [[0, 2048]])
-    iota(R("sB"), [[1, 64]])
-    iota(R("sR"), [[0, 4], [1, 64]])
-    iota(R("I16"), [[16, 16]])
-    iota(R("ONE256"), [[0, 256]], 1)
-    iota(("XS", 0, 16), [[0, 16]])
-    iota(R("USED", TR, TR + 256), [[0, 256]], 1)
-
-    fill(R("RN"), 0.0)
-    fill(R("BIA", 0, 1), 7.5)
-    fill(R("BIA", 1, 2), -7.5)
-    fill(R("BIA", 2, 4), 0.0)
-    fill(R("AB"), 0.0)
-    ts(K("ip", 1), ip, 15, A.bitwise_and)
-    ts(K("ip", 2), ip, 7, A.bitwise_and)
-    ts(K("ip", 3), ip, 3, A.logical_shift_right, 1, A.bitwise_and)
-    ts(K("ip", 4), ip, 4, A.logical_shift_right)
-    ts(K("ip", 5), ip, 1, A.bitwise_and)
-    for c in "plkhgq":
+    iota(R("TM"), [[0, 16], [1, 8]])
+    iota(R("ONE"), [[0, 256]], 1)
+    cols = (("p", 0, 127), ("g", 4, 7), ("l", 0, 15), ("k", 0, 7), ("r", 3, 1), ("q", 0, 1), ("g4", 2, 7), ("i4", 0, 3), ("kd", 1, 1))
+    for i, (c, sh, m) in enumerate(cols):
         C(c)
-    cp(("cols", 0, 6), ("ip", 0, 6))
-    m0 = K("M0", 0)
-    ts(R("M0"), R("ra8"), C("k"), A.is_equal)
-    ts(R("M1"), R("ra8"), C("k"), A.subtract, -1.0, A.is_equal)
-    ts(C("k6"), C("k"), 6.0, A.is_ge)
-    lin(C("h0"), C("h"), -1.0, 1.0)
-    lin(C("sg"), C("h"), 2.0, -1.0)
-    lin(C("kk"), C("k6"), 100.0, C("k"))
-    lin(C("on"), C("k6"), 1.0, m0)
-    act(C("hc"), C("h"), scale=1.0 / 128)
-    act(C("jb"), C("sg"), scale=2032.0)
-    act(C("sg8"), C("sg"), scale=8.0)
-    act(C("hh"), C("sg"), scale=0.5)
-    lin(R("AS"), R("ra8"), 1.0, C("kk"))
-    act(R("ONE"), R("BO"), scale=C("h0"))
-    lin(C("gm"), C("on"), 2048.0, -2048.0)
-    lin(C("b1"), C("on"), -10000.0, 4.0 - M24)
-    act(C("c7"), K("M0", 7), scale=C("h0"))
-    act(C("c6"), K("M0", 6), scale=C("h0"))
+        ts(K("ip", i + 1), ip, sh, A.logical_shift_right, m, A.bitwise_and)
+    cp(R("cols", 0, len(cols)), R("ip", 1, len(cols) + 1))
+    ts(R("SEL", p=p32), R("GR", p=p32), C("g4", p32), A.is_equal)
+    ts(R("REP", p=p32), R("I48", p=p32), C("i4", p32), A.is_equal)
+    ts(R("E7"), R("I48"), 7.0, A.is_equal)
+    ts(R("RST"), R("I48"), 0.0, A.not_equal)
+    cp(C("nf", p32), K("NI", 0, p32))
+    ts(R("MV", p=p32), R("REP", p=p32), C("nf", p32), A.mult)
+    mm((R("P0", 0, 48), R("SEL", p=p32), R("MV", p=p32), True, True))
+    tt(R("RN"), R("P0", 0, 48), R("E7"), A.add)
+    ts(R("BO"), R("GR"), C("g"), A.is_equal)
+    lin(C("r0"), C("r"), -1.0, 1.0)
+    lin(C("sg"), C("r"), 2.0, -1.0)
+    ts(C("k0"), C("k"), 0.0, A.is_equal)
+    ts(C("k6"), C("k"), 6.0, A.is_equal)
+    ts(C("k1"), C("k"), 1.0, A.is_equal)
+    lin(C("on"), C("k0"), 1.0, C("k6"))
+    act(C("k0r"), C("k0"), scale=C("r"))
+    ts(C("f"), C("k"), 0.5, A.is_ge, C("k0r"), A.add)
+    ts(C("f6"), C("k"), 5.5, A.is_lt, C("f"), A.mult)
+    act(C("sg8"), C("sg"), scale=-8.0)
+    lin(C("gm"), C("on"), -2048.0, 2048.0)
     act(C("gm"), C("gm"), scale=C("sg"))
-    act(C("chi"), C("c7"), scale=-1920.0)
+    lin(C("cm"), C("on"), -16.0, -2032.0)
+    act(C("cm"), C("cm"), scale=C("sg"))
+    lin(C("b1"), C("on"), -10000.0, -M24)
+    act(C("c6"), C("k6"), scale=C("r"))
     act(C("c6"), C("c6"), scale=EPS)
-    lin(C("zc"), C("h"), 0.0, -1920.5 + EPS)
-    lin(C("clo"), C("c7"), -0.5, C("c6"))
-    tt(C("m01"), m0, K("M0", 1), A.subtract)
-    act(C("m01s"), C("m01"), scale=EPS)
-    act(R("MS"), R("M0"), scale=EPS)
-    sel(R("TRI"), R("ONE"), [[16, 8], [0, 2], [1, 8]], A.is_gt, 0.0, 0, -1)
-    ts(C("km"), C("k"), -1.0, A.add, 2.0, A.min)
-    act(C("b0"), C("on"), scale=-10000.0)
-    do("V", lambda: g.vector.tensor_copy(T.NF[0:8, 0:4], T.NI[0:8, 0:4]), [("NI", 0, 4)], [("NF", 0, 4)])
-    do("V", lambda: g.vector.tensor_copy(T.NF[0:8, 4:6], T.NI[0:8, 4:6]), [("NI", 4, 6)], [("NF", 4, 6)])
-    mm([("P0", 8, 12, ("SEL8", 0, 128), ("NF", 0, 4, 1, 8), True, True)])
-    cp(("RN", 0, 3), ("P0", 8, 11))
-    cp(C("e0"), ("P0", 11, 12))
-    lin(R("IOC"), R("IC0"), 1.0 / 128, C("hc"))
-    lin(R("NIC"), R("IC0"), -1.0 / 128, -2.0 ** -19)
-    lin(R("JL"), R("rowl"), C("sg"), C("jb"))
-    group("JL", -6500.0)
+    lin(C("cs"), C("k0r"), -1920.5, C("c6"))
+    lin(C("cy"), C("k1"), -1.0, C("k0r"))
+    act(C("rc"), C("r"), scale=1.0 / 128)
+    ts(R("MK", 0, 8), R("I48", 0, 8), C("k"), A.is_equal, C("f6"), A.mult)
+    ts(R("MK", 24, 32), R("I48", 0, 8), C("k"), A.subtract, -1.0, A.is_equal)
+    tt(R("MK", 16, 24), R("MK", 0, 8), R("MK", 24, 32), A.subtract)
+    act(K("MK", 31), C("cs"))
+    ts(R("XW", 0, 16), R("I16"), C("k"), A.add, 7.0, A.is_equal)
+    ts(R("XW", 0, 16), R("XW", 0, 16), C("f6"), A.mult)
+    act(R("XW", 16, 32), R("XW", 0, 16), scale=2.0 ** -12)
+    tt(R("XW", 33, 48), R("XW", 1, 16), R("XW", 0, 15), A.subtract)
+    lin(R("XW", 48, 64), R("XW", 0, 16), -1.0, C("k0r"))
 
-    def anti(t):
-        ts(R("AA"), R("AS"), float(3 + t), A.is_equal)
-        ts(R("AB", 1), R("AS", 1), float(4 + t), A.is_equal)
+    def picks(t):
+        o, m = 48 * t, 4 - t
+        if t:
+            act(R("MK", o, o + 32), R("MK", 0, 32))
+            ts(K("MK", o + 23), C("k"), 3.0 + t, A.is_equal, 128.0, A.mult)
+            act(C("ux%d" % t), K("MK", o + 23), scale=2.0 ** -20)
+        act(R("MK", o + 8, o + 16), R("XW", 16 + m, 24 + m))
+        act(K("MK", o + 32), K("XW", m))
+        act(R("MK", o + 33, o + 39), R("XW", 33 + m, 39 + m))
+        act(K("MK", o + 39), C("cy"), scale=128.0 if t else 0.0)
+        act(R("MK", o + 40, o + 47), R("XW", 48 + m, 55 + m))
+        act(K("MK", o + 47), C("cs"))
+
+    picks(0)
+    act(R("ONF"), R("BO"), scale=C("r"))
+    ts(R("TRI"), R("TM"), C("k"), A.is_gt, 2.0, A.mult)
+    tt(R("TRI"), R("TRI"), R("ONF"), A.mult)
+    lin(R("IOC"), R("IC0"), 1.0 / 128, C("rc"))
+    lin(R("NIC"), R("IC0"), -1.0 / 128, -2.0 ** -19)
+    lin(R("JL"), R("LR"), C("sg"), 64.0)
+    tt(R("JL"), R("JL"), R("BO"), A.mult)
+    ts(R("JL"), R("JL"), -64.0, A.add)
+    iota(R("IDN"), [[0, 128]], 1)
+    sel(R("IDN"), R("IDN"), [[-1, 128]], A.is_equal, 0.0, 0, 1)
+
+    def common():
+        act(R("NID"), R("IDN"), scale=-1.0)
+        lin(C("s4"), C("q"), -0.5, 0.25)
+        ts(R("WT", 0, 8), R("I48", 0, 8), C("g"), A.is_equal)
+        act(R("WT", 8, 16), R("WT", 0, 8), scale=-1.0)
+        act(R("WT", 16, 24), R("WT", 0, 8), scale=C("s4"))
+        lin(C("ks"), C("kd"), 2.0, -1.0)
+        lin(C("qs"), C("q"), -2.0, 1.0)
+        ts(C("lv", p32), K("NI", 1, p32), C("ks", p32), A.mult, 0.5, A.add)
+        ts(C("lh", p32), C("lv", p32), M27, A.add, M27, A.subtract)
+        ts(C("lh", p32), C("lh", p32), C("qs", p32), A.mult)
+        ts(C("lv", p32), C("lv", p32), C("q", p32), A.mult, C("lh", p32), A.add)
+        act(R("LX", p=p32), R("ONE", 0, 128, 1, p32), scale=C("lv", p32))
+        lin(C("kd0"), C("kd"), -1.0, 1.0)
+        for i, c in enumerate((C("kd0", p32), C("kd", p32), 0.0)):
+            act(R("SK", 128 * i, 128 * i + 128, 1, p32), R("SEL", p=p32), scale=c)
+        iota(R("R16"), [[0, 16], [1, 16]])
+        iota(R("CAND", J, J + DUM), [[0, DUM]], NONE)
+        iota(R("W3S", 1024), [[0, 64]])
+        iota(R("sR"), [[0, 4], [1, 64]])
+        iota(R("TB"), [[B, 2], [16, 16]], TR - B)
+        iota(R("XS", 0, 16), [[0, 16]])
+        zero = R("BANK", B, TR + 256)
+        iota(zero, [[0, 1024]])
+        dma("Y", [(ap(R("USED", c, c + 1024)), ap(zero)) for c in range(0, Q, 1024)], [zero, R("RB", 256)], [R("USED", 0, Q)], 2 * DM)
+        iota(R("USED", TR, TR + 256), [[0, 256]], 1)
+        for p in range(N):
+            iota(R("OC", 4 * p, 4 * p + 4), [[0, 4]], 256 * p + 64 * (CN[0][p] + CN[1][p]).count("S"))
+        iota(R("R64"), [[0, 256]], 1)
+        sel(R("R64"), R("R64"), [[0, 4], [1, 64]], A.not_equal, 0.0, 0, 0)
+        iota(R("SV"), [[16, 4]])
+        sel(R("NU"), R("BO"), [[-1, 128]], A.is_gt, 0.0, 0, 1)
+        act(R("NU"), R("NU"), scale=-1.0)
+        ts(R("KP"), R("R16"), C("l"), A.is_equal, 32768.0, A.mult)
+        ts(R("SV"), R("SV"), C("l"), A.add, 0.5, A.add)
+        iota(R("KZ"), [[0, 256]], -2 ** 20)
+        sel(R("KZ"), R("KZ"), [[0, 16], [1, 16]], A.not_equal, ZK, 0, 0)
+        for p in range(N):
+            lin(R("MKS", 64 * p, 64 * p + 64), R("KP", 0, 64), -64.0 - p / 8.0, 2.0 ** 21)
+        hold[:] = []
+
+    def arrivals():
+        lin(R("MKB"), R("KP"), -64.0, 2.0 ** 21)
+        act(R("DG"), R("KP"), scale=-2.0 ** -14)
+        lin(R("TB"), R("TB"), 1.0, C("l"))
+        lin(C("wi"), C("l"), 3.5, 2.25)
+        act(R("WB"), R("BO"), scale=C("wi"))
+        ts(C("ck"), C("l"), 0.0, A.is_equal, MB, A.mult)
+        ts(C("ck1"), C("l"), 1.0, A.is_equal, 0.25 - rank / 4.0, A.mult)
+        lin(C("ck"), C("ck"), 1.0, C("ck1"))
+        act(R("CK"), R("ONE"), scale=C("ck"))
+        ts(R("QR"), R("I16"), C("l"), A.is_le, -0.75, A.mult)
+        lin(R("QR"), R("QR"), 1.0, 1.0)
+        scan(R("QS"), R("QR"), R("ONE", 0, 16), 1.0, A.mult, A.mult)
+        act(R("WQ"), R("BO"), scale=K("QS", 15))
+        act(C("uy"), C("cy"), scale=EPS)
+        act(C("s1"), K("RN", 0), scale=2.0 ** -12)
+        lin(C("b0"), K("RN", 0), 2.0 ** -4, -1.0 + 2.0 ** -12)
+        act(R("UB"), R("UI")) if EN.get("UB") else cp(R("UB"), R("UI"))
+        dma("Y", [(T.USED[0:128:16, 0:Q], ap(R("UB")))], [R("UB")], [R("USED", 0, Q)], DM)
 
     def prepare(t):
-        for i, (m, c) in enumerate((("M0", "PNL"), ("AA", "PNR"), ("M1", "dS"), ("AB", "Qc"))):
-            tt(R("T8", 8 * i, 8 * i + 8), R("RN"), R(m), A.mult)
-            act(R("T8", 32 + 8 * i, 40 + 8 * i), R("T8", 8 * i, 8 * i + 8), acc=C(c))
-
-    def shares(t):
-        tt(K("WI", 0), C("PNL"), C("PNR"), A.mult)
-        ts(K("WI", 1), K("WI", 0), 12, A.arith_shift_right)
-        cp(C("Wp"), K("WI", 1))
-        mm([("P6", 0, 1, R("ONE"), C("Wp"), True, True), ("P6", 1, 2, R("TRI"), C("Wp"), True, True)])
-
-    def sums(t):
-        ts(K("IN2", 0), ("P6", 0, 1), 4.0 - M24, A.add)
-        ts(K("IN2", 1), ("P6", 1, 2), 2.0, A.mult, C("b1"), A.add)
-
-    def steps(t):
-        lin(K("PRE", 0), C("dS"), -1.0, C("PNL"))
-        lin(K("PRE", 1), C("Qc"), -1.0, C("PNR"))
-        act(C("tm"), m0, scale=C("Told"))
-        act(K("PRE", 2), C("dS"))
-        lin(K("PRE", 3), C("PNR"), -1.0, C("tm"))
-        if t == 0:
-            lin(K("PRE", 0), K("M0", 3), C("e0"), K("PRE", 0))
-            lin(K("PRE", 1), C("m01"), C("e0"), K("PRE", 1))
-        hi, lo = ("HL", 0, 4), ("HL", 4, 8)
-        tt(lo, R("PRE"), R("BIA"), A.add)
-        ts(hi, lo, M27, A.add, M27, A.subtract)
-        tt(lo, R("PRE"), hi, A.subtract)
-        ts(("HL", 0, 2), ("HL", 0, 2), EPS, A.mult)
-        ts(("HL", 4, 6), ("HL", 4, 6), EPS, A.mult)
-        ts(("HL", 2, 4), ("HL", 2, 4), C("chi"), A.add, 0.5, A.mult)
-        ts(("HL", 6, 8), ("HL", 6, 8), C("clo"), A.add, 0.5, A.mult)
-
-    def gath(o, c0, c1):
-        return (("BANK", 0, B + N * CAP * now[0]), (o, c0 // 16, c1 // 16))
-
-    def sg(b, o, c, n):
-        act(R(b, c, c + n), gath(o, c, c + n))
-
-    def list_z():
-        ts(R("ZO"), R("ZT"), M23 + 1920.0, A.add, M23, A.subtract)
-
-    def places():
-        tt(R("PO"), ("P5", 0, 16), R("TI"), A.add)
-        tt(R("SO"), R("PO"), R("NK"), A.max)
+        tt(R("T8"), R("RN"), R("MK", 48 * t, 48 * t + 48), A.mult)
+        scan(R("PB"), R("RST"), R("T8"), 0.0, A.mult, A.add)
+        ts(K("WI", 0), K("PB", 7), K("PB", 15), A.mult, -1024.5 + EPS, A.add)
+        ts(C("wp"), K("WI", 0), 1024.0, A.add)
+        mm((K("P6", 0), R("ONF"), C("wp"), True, True), (K("P6", 1), R("TRI"), C("wp"), True, True))
+        ts(R("CF", 0, 4), R("PB", 23, 48, 8), M27, A.add, M27, A.subtract)
+        tt(R("CF", 4, 8), R("PB", 23, 48, 8), R("CF", 0, 4), A.subtract)
+        act(R("CF", 0, 8, 2), R("CF", 0, 8, 2), scale=2.0 ** -12)
+        if t:
+            lin(C("i0"), K("P6", 0), 1.0, -M24)
+            lin(C("i1"), K("P6", 1), 1.0, C("b1"))
+            cp(R("RCF"), R("RC", 256 * t, 256 * t + 256))
+        else:
+            cp(C("ct"), K("P6", 0))
+            ts(C("c2"), K("P6", 1), C("b1"), A.add, M24, A.add)
 
     def decode(t):
-        ct, c2, e = K("CC", 0), K("CC", 1), C("e%d" % t)
+        ct, c2 = C("ct"), C("c2")
+        cf = [K("CF", i) for i in range(8)]
         if t:
-            ts(C("w2"), ("P2", 0, 1), C("s2"), A.mult, M24, A.add)
-            lin(C("Tq"), ("P0", 0, 1), 2.0 ** -12, C("TqO"))
-            lin(R("ZT", 0, 128), R("RCF", 0, 128), C("Tq"), C("zc"))
-            act(e, ("P0", 0, 1))
-            tt(R("NK"), R("NK"), R("TB"), A.mult)
-            ts(R("CC"), R("IN2"), C("w2"), A.add, 4.0, A.subtract)
-        act(R("SG"), R("NIC"), F.Sign, ct, C("cnt"), c2)
-        if t:
-            tt(R("PO"), ("P5", 0, 16), R("TI"), A.add)
-        ts(C("al"), ct, C("sg8"), A.mult)
-        ts(C("ga"), c2, C("gm"), A.mult, C("hh"), A.add)
-        lo = [K("HL", 4 + i) for i in range(4)]
-        if t:
-            lo[0], lo[1] = K("HL", 8), K("HL", 9)
-            lin(lo[0], e, K("MS", 3 + t), K("HL", 4))
-            lin(lo[1], e, C("m01s"), K("HL", 5))
-            lin(R("ZT", 128), R("RCF", 128), C("Tq"), C("zc"))
-            tt(R("SO"), R("PO"), R("NK"), A.max)
-        ts(R("AL"), R("IOC"), ct, A.mult, c2, A.is_ge)
-        if t:
-            cp((("BANK", 0, TR + 256), R("SO")), R("LAND%d" % (t - 1)))
-            list_z()
-        if t:
-            lin(C("th"), C("cnt"), C("al"), C("ga"))
-            act(R("GM"), R("JL"), F.Sign, ct, None, C("th"))
+            e = C("e%d" % (t - 1))
+            lin(C("w2"), e, C("s1"), C("b0"))
+            ts(ct, C("w2"), M24, A.add, C("i0"), A.add)
+            ts(c2, C("w2"), M24, A.add, C("i1"), A.add)
+            lin(C("tq"), e, EPS, C("tq0") if t > 1 else (B + 128) / 4096.0)
+            lin(K("CF", 8), e, C("ux%d" % t), cf[4])
+            lin(K("CF", 9), e, C("uy"), cf[6])
+            cf[4], cf[6] = K("CF", 8), K("CF", 9)
+            lin(R("ZT"), R("RCF"), C("tq"), C("zc"))
         else:
-            ts(C("nct"), ct, -1.0, A.mult)
-            ts(C("th"), C("cnt"), C("al"), A.mult, C("ga"), A.add)
-            ts(R("GM"), R("JL"), C("nct"), A.mult, C("th"), A.is_lt)
-        for n, (i, pb) in enumerate(((0, "P1"), (2, "P3"), (1, "P2"), (3, "P4"))):
-            for u, c in enumerate((K("HL", i), lo[i])):
-                lt = ("LT", 256 * n + 128 * u, 256 * n + 128 * u + 128)
-                if t == 0:
-                    ts(lt, R("GM"), c, A.mult, 2.0, A.mult)
-                elif 2 * n + u >= LV:
-                    ts(lt, R("GM"), c, A.mult, c, A.add)
+            lin(C("zc"), C("r"), 0.0, -1920.5 + EPS)
+            ts(R("ZT"), R("RC", 0, 256), B / 4096.0, A.mult, -1920.5 + EPS, A.add)
+        ts(R("ZO"), R("ZT"), M23 + 1920.0, A.add, M23, A.subtract)
+        act(R("SG"), R("NIC"), F.Sign, ct, C("cnt"), c2)
+        lin(C("al"), ct, C("sg8"), 0.0, EN["al"])
+        lin(C("ga"), c2, C("gm"), C("r0"), EN["ga"])
+        lin(C("ga"), ct, C("cm"), C("ga"), EN["ga"])
+        ts(R("AL"), R("IOC"), ct, A.mult, c2, A.is_ge)
+        lin(C("th"), C("cnt"), C("al"), C("ga"), EN["th"])
+        if DIRECT:
+            lin(R("JC"), R("JL"), ct, 0.0, EN.get("JC", "V"))
+        ts(R("GM"), R("JL"), ct, A.mult, C("th"), A.is_ge)
+        for n in range(4):
+            pa, pb = R(("P1", "P2")[n // 2], 0, 256), R(("P3", "P4")[n // 2], 0, 256)
+            inp, xt = INP[n // 2], R(("XT", "YT")[n // 2])
+            if n % 2 == 0 and inp:
+                mm((pb, R("IDN"), R("ONE"), True, False))
+            for u in range(2):
+                lt = R("LT", 256 * n + 128 * u, 256 * n + 128 * u + 128)
+                if 2 * n + u < DIRECT:
+                    ts(lt, R("JC"), C("th"), A.is_ge, cf[n + 4 * u], A.mult)
                 else:
-                    lin(lt, R("GM"), c, c)
-                mm([(pb, 0, CUT, lt, R("AL", 0, CUT), u == 0, u == 1)])
-        lists(t, 0, CUT, ("P1", "P3", "P2", "P4"))
-        if CUT < 256:
-            for n, pb in enumerate(("P5", "P6", "P7", "P0")):
-                mm([(pb, CUT, 256, ("LT", 256 * n + 128 * u, 256 * n + 128 * u + 128), R("AL", CUT), u == 0, u == 1) for u in range(2)])
-            lists(t, CUT, 256, ("P5", "P6", "P7", "P0"))
-
-    def lists(t, c, d, pb):
-        ra, rb = R("RA", 256 * t + c, 256 * t + d), R("RB", 256 * t + c, 256 * t + d)
-        tt(R("XT", c, d), (pb[0], c, d), ra, A.mult)
-        tt(R("YT", c, d), (pb[2], c, d), rb, A.mult)
-        tt(R("XT", c, d), (pb[1], c, d), R("XT", c, d), A.add)
-        tt(R("YT", c, d), (pb[3], c, d), R("YT", c, d), A.add)
-        ts(R("XO", c, d), R("XT", c, d), M23 + 1920.0, A.add, M23, A.subtract)
-        ts(R("YO", c, d), R("YT", c, d), M23 + 1920.0, A.add, M23, A.subtract)
-
-    def add2(pb, c, n, w):
-        mm([(pb, 0, n, R("IDN"), ("TX", c, c + n), True, False), (pb, 0, n, R(w), ("TY", c, c + n), False, True)])
-
-    def sumkey(h, r0, r1):
-        c = 2048 * h
-        mm([("P%d" % (1 + h), l, 384, ("CAND", c + 16 * r0 + l, c + 16 * r1, 16), R("WT"), True, True, 16) for l in range(16)], (r0, r1))
+                    lin(lt, R("GM"), cf[n + 4 * u], 0.0, LV[2 * n + u])
+                mm((pb, lt, R("AL"), u == 0 and not inp, u == 1) if n % 2 else (pa, lt, R("AL"), u == 0, u == 1))
+            if n % 2 == 0:
+                tt(pb if inp else xt, pa, R(("RA", "RB")[n // 2], 256 * t, 256 * t + 256), A.mult)
+            else:
+                if not inp:
+                    tt(xt, pb, xt, A.add)
+                ts(R(("XO", "YO")[n // 2]), pb if inp else xt, M23 + 1920.0, A.add, M23, A.subtract)
+        if t == 1:
+            e = C("e0")
+            lin(C("n4"), e, 0.5, 128.0)
+            act(R("RN", 4, 48, 8), R("ONE", 0, 6), scale=C("n4"))
+            lin(C("tq0"), e, EPS, (B + 256) / 4096.0)
+            lin(C("tm1"), e, 0.5, 127.0)
+            lin(C("tm"), e, 0.5, 255.0)
+        if t == 2:
+            lin(C("tm2"), C("e1"), 0.5, C("tm"))
 
     def codes(h):
-        pb, pc, a = "P%d" % (1 + h), "P%d" % (3 + h), (128 * h, 128 * h + 128)
-        ts(R("KI", *a), (pb, 256, 384), 0.125, A.add)
-        tt(R("X1", 256 * h, 256 * h + 256), (pb, 0, 256), R("LOT"), A.is_lt)
-        mm([(pc, 0, 128, R("X1", 256 * h + 128 * i, 256 * h + 128 * i + 128), R("ID4"), i == 0, False) for i in range(2)])
-        tt(R("OB", *a), (pb, 256, 384), R("KI", *a), A.subtract)
-        mm([(pc, 0, 128, R("OB", *a), R("IDN"), False, True)])
+        pb, pc, a = "P%d" % (1 + h), R("P%d" % (3 + h), 0, 128), (128 * h, 128 * h + 128)
+        ts(R("KI", *a), R(pb, 256, 384), 0.125, A.add)
+        tt(R("OB", *a), R(pb, 256, 384), R("KI", *a), A.subtract)
+        if EN["X1"][h] == "S":
+            act(R("X1", 256 * h, 256 * h + 256), R(pb, 0, 256), F.Sign)
+        else:
+            ts(R("X1", 256 * h, 256 * h + 256), R(pb, 0, 256), 0.0, A.is_gt, 2.0, A.mult)
+        mm((pc, R("OB", *a), R("IDN"), True, False))
+        mm(*[(pc, R("X1", 256 * h + 128 * i, 256 * h + 128 * i + 128), R("NID"), False, i == 1) for i in range(2)])
+        if EN["CD"][h] == "S":
+            act(R("CD", *a), pc)
 
     def part(h):
         return [(256 * p + 128 * h, 256 * p + 128 * h + 128) for p in range(N)]
 
     def masks(h):
         for p, f in enumerate(part(h)):
-            ts(("FM",) + f, ("P%d" % (3 + h), 0, 128), (0.0, 0.25, -0.5, -0.25)[owners[p]], A.is_equal)
+            ts(R("FM", *f), R("CD", 128 * h, 128 * h + 128) if EN["CD"][h] == "S" else R("P%d" % (3 + h), 0, 128),
+               (0.0, 0.25, -0.5, -0.25)[owners[p]] - (2.0 if EN["X1"][h] == "S" else 4.0), A.is_equal)
 
-    def scans(h, ps):
-        for f in [part(h)[p] for p in ps]:
-            scan(("SC",) + f, ("FM",) + f, ("FM",) + f, ("SC", f[0] - 1, f[0]) if h else 0.0, A.add, A.max)
+    def scans(h):
+        for f in part(h):
+            scan(R("SC", *f), R("FM", *f), R("FM", *f), K("SC", f[0] - 1) if h else 0.0, A.add, A.max)
 
-    def counts(h, ps):
-        q = [("P%d" % (5 + p // 2), 256 * (p % 2) + 128 * h, 256 * p + 128 * h) for p in ps]
-        for pb, o, c in q:
-            mm([(pb, o, o + 128, R("BO"), ("SC", c, c + 128), True, False), (pb, o, o + 128, R("NU"), ("FM", c, c + 128), False, True)])
-        for pb, o, c in q:
-            act(R("W3S", c, c + 128), (pb, o, o + 128))
+    def counts(h, ps=range(N)):
+        q = [(R("P%d" % (5 + p // 2), 256 * (p % 2) + 128 * h, 256 * (p % 2) + 128 * h + 128), part(h)[p]) for p in ps]
+        for pb, f in q:
+            mm((pb, R("BO"), R("SC", *f), True, False), (pb, R("NU"), R("FM", *f), False, True))
+        for p, (pb, f) in zip(ps, q):
+            (act if EN["W3"][4 * h + p] == "S" else cp)(R("W3S", *f), pb)
 
-    anti(0)
-    prepare(0)
-    for i in range(2):
-        ts(K("IN2", i), ("P0", 8 + i, 9 + i), ("P0", 11 - i, 12 - i), A.mult, 2.0 ** -11, A.mult)
-    ts(R("IN2"), R("IN2"), -1.0 + 2.0 ** -12, A.add, M24, A.add)
-    ts(R("IN2"), R("IN2"), M24, A.subtract)
-    ts(C("w2"), K("IN2", 1), C("km"), A.mult, C("b0"), A.add)
-    tt(K("CC", 0), K("IN2", 0), K("IN2", 1), A.add)
-    tt(K("CC", 1), K("IN2", 0), C("w2"), A.add)
-    lin(C("Told"), C("e0"), -1.0, float(B))
-    ts(R("ZT"), R("RC", 0, 256), B / 4096.0, A.mult, -1920.5 + EPS, A.add)
-    steps(0)
-    list_z()
-    for i in (4, 5):
-        li, o = ("LX", 128 * (i - 4), 128 * (i - 4) + 128), 128 * (i - 3)
-        do("S", lambda li=li, i=i: g.scalar.activation(T.LX[0:8, li[1]:li[2]], T.SEL8[0:8, 0:128], F.Identity, bias=T.NF[0:8, i:i + 1], scale=0.0),
-           [R("SEL8"), ("NF", i, i + 1)], [li], 128)
-        mm([("P7", o, o + 128, li, ("SEL8", 0, 128, 1, 8), True, True)])
-    act(R("LOT", 0, 128), ("P7", 128, 256))
-    act(R("LOT", 128, 256), ("P7", 256, 384), scale=-1.0)
+    def blocks(h, ps):
+        for p in ps:
+            ce, o = R(CE[h][p], 64 * p, 64 * p + 64), 1024 * h + 256 * p
+            mm((ce, R("BO"), R("SC", part(h)[p][0] + 1, part(h)[p][1], 2), True, True))
+            for m in range(4):
+                jk = R("JK", o + 64 * m, o + 64 * m + 64)
+                if CN[h][p] == "S":
+                    act(jk, ce, F.Sign, -1.0, K("ACC", 16 * h + 4 * p + m), K("SV", m))
+                else:
+                    ts(jk, ce, K("SV", m), A.is_lt, 2.0, A.mult)
+            if CN[h][p] == "V":
+                scan(R("JS", o, o + 256), R("R64"), R("JK", o, o + 256), 0.0, A.mult, A.add)
 
-    for t in range(RO):
-        land, send, now[0] = "LAND%d" % t, "SEND%d" % t, t
-        decode(t)
-        if t == 0:
-            cp(R("UG"), R("KRI"))
-            dma("Y", [(T.UD[:, :], T.UG[:, 0:256])], [R("UG")], [("UD", 0, 4096)], 3000)
-            dma("Y", [(T.USED[l::16, 0:Q], T.UD[:, :]) for l in range(16)], [("UD", 0, 4096)], [("USED", 0, Q)], 4000)
-        if t == 0:
-            lin(C("s4"), C("q"), -0.5, 0.25)
-            for i, c in enumerate((1.0, -1.0, C("s4"))):
-                act(R("WT", 8 * i, 8 * i + 8), ("BO", 0, 128, 16), scale=c)
-            sel(R("UP"), R("BO"), [[-1, 128]], A.is_gt, 0.0, 0, 1)
-            act(R("NU"), R("UP"), scale=-1.0)
-        lead[0] = FIX
-        for step in ORDER.split():
+    def counted(h, c, d):
+        return R("ACC", 16 * h + 4 * c, 16 * h + 4 * d) if CN[h][c] == "S" else R("JS", 1024 * h + 256 * c + 63, 1024 * h + 256 * d, 64)
+
+    def operands(t):
+        def gath(o, c, d):
+            old = o == "XO" and d <= J // 2 or o == "YO" and c >= J // 2
+            return (R("BANK", 0, B if old else B + N * CAP * t), R(o, c // 16, d // 16))
+
+        for h in range(2):
+            mm((R("P%d" % (1 + h), 0, 384), R("LX", p=p32), R("SK", p=p32), True, False))
+        mark = len(calls)
+        steps(t, gath)
+        for q in FIX:
+            mine = [c for c in calls[mark:] if c[0] == q and (c[4][1] or c[4][0] >= 256)]
+            for i, (a, b) in enumerate(zip(mine, mine[1:])):
+                a[3].append(K("turn", 16 + 32 * (2 * t + "VS".index(q)) + i))
+                b[6].append(a[3][-1])
+
+    def steps(t, gath):
+        for step in (ORDER if t or not ORDER0 else ORDER0).split():
             what, c, d, pb = (step.split(":") + [""] * 3)[:4]
             c, d = 16 * int(c or 0), 16 * int(d or 0)
-            if what in "xyz":
-                sg("T" + what.upper(), what.upper() + "O", c, d - c)
+            if what == "Z":
+                cp(R("TZ", c, d), gath("ZO", c, d))
+            elif what in "xyz":
+                act(R("T" + what.upper(), c, d), gath(what.upper() + "O", c, d))
             elif what in ("sub", "add"):
-                add2(pb, c, d - c, "NID" if what == "sub" else "IDN")
+                mm((R(pb, 0, d - c), R("IDN"), R("TX", c, d), True, False), (R(pb, 0, d - c), R("NID" if what == "sub" else "IDN"), R("TY", c, d), False, True))
             elif what == "abs":
-                act(R("TZ", c, d), (pb, 0, d - c), F.Abs)
+                act(R("TZ", c, d), R(pb, 0, d - c) if pb else R("TY", c, d), F.Abs)
             elif what == "cut":
-                tt(R("CAND", c, d), (pb, 0, d - c), R("TZ", c, d), A.min)
+                tt(R("CAND", c, d), R(pb, 0, d - c), R("TZ", c, d), A.min)
             elif what == "sum":
-                sumkey(c // 2048, c % 2048 // 16, (d - 1) % 2048 // 16 + 1)
+                rows = (c % 2048 // 16, (d - 1) % 2048 // 16 + 1)
+                for m in range(0, 16, 8):
+                    mm(*[(R("P%d" % (1 + c // 2048), l, 384, 16, rows), R("CAND", c + l, d, 16), R("WT", 0, 24), False, l == 15) for l in range(m, m + 8)])
             elif what == "first":
-                (codes, masks, lambda h: scans(h, range(N)), lambda h: counts(h, range(N)))[c // 16](0)
+                (codes, masks, scans, counts)[c // 16](0)
             else:
                 o, w, op = {"Xz": ("TX", "TZ", A.min), "Yx": ("CAND", "TX", A.min), "Ymax": ("TY", "TX", A.max), "Yadd": ("TY", "TX", A.add),
-                            "Zy": ("CAND", "TY", A.min), "Zd": ("CAND", "TZ", A.min)}[what]
+                            "Ysub": ("TY", "TX", A.subtract), "Ymin": ("TY", "TX", A.min), "Xadd": ("TX", "TY", A.add), "Zx": ("CAND", "TX", A.min), "Zy": ("CAND", "TY", A.min), "Zd": ("CAND", "TZ", A.min)}[what]
                 tt(R(o, c, d), gath(what[0] + "O", c, d), R(w, c, d), op)
-        lead[0] = 0
-        if t == 0:
-            sel(R("SU"), R("BO"), [[1, 128]], A.is_gt, 0.0, 0, -1)
-            for u in range(len(PARTS) - 1):
-                lin(C("r%d" % u), C("l"), -16.0, -256.0 * (PARTS[u] // CAP))
-            lin(C("r3"), C("l"), -16.0, -float(J))
-            act(C("h2"), C("h0"), scale=2.0)
-            act(C("h5"), C("h"), scale=512.0)
-            for c in range(0, 256, 32):
-                first = c // CAP == max(x for x in PARTS if x <= c) // CAP
-                lin(R("R3", c, c + 32), R("R256", c, c + 32), C("h2"), C("h5") if first else 0.0)
-            for l in range(16):
-                act(("LS", 128 * l + l, 128 * l + 128, 16), ("BO", 0, 128, 16))
-            ts(R("KP"), R("R256"), C("l"), A.is_equal, 32768.0, A.mult)
+
+    def search(t):
+        for c, d in PARTS:
+            blocks(0, range(c, d))
+            tt(R("A1", 4 * c, 4 * d), counted(0, c, d), R("OC", 4 * c, 4 * d), A.add)
+            lin(R("A1", 16 + 4 * c, 16 + 4 * d), R("A1", 4 * c, 4 * d), 1.0, 1.0, EN["A1"])
         codes(1)
         masks(1)
-        scans(1, range(N))
-        def H(b, u, k=1):
-            return (b, PARTS[u] // k, PARTS[u + 1] // k)
+        scans(1)
+        for (c, d), pb in zip(PARTS, ("P0", "P7", "P0", "P7")):
+            blocks(1, range(c, d))
+            counts(1, range(c, d))
+            l, f = (4 * c, 4 * d), (64 * c, 64 * d)
+            mm((R(pb, *f), R("IDN"), R("MKS", *f), True, False))
+            for i, (o, x) in enumerate((("O1", "I2"), ("O2", "XP"))):
+                tt(R(o, *l), counted(1, c, d), R("A1", 16 * i + l[0], 16 * i + l[1]), A.add)
+                tt(R(x, *f), (R("W3S", 0, min(256 * d + 16, 1088)), R(o, *l)), R("sR", *f), A.is_le)
+                mm((R(pb, *f), R("BO"), R(x, *f), False, i == 1))
+            ts(R("T3", *l), R("O1", *l), 16.0, A.mult)
+            scan(R("PK", *f), R("KZ", *f), R(pb, *f), 0.0, A.max, A.min)
+            tt(R("O3", *l), R("PK", f[0] + 15, f[1], 16), R("T3", *l), A.add)
 
-        def pick(bank, u):
-            scan(H("PK1", u), H("KP", u), H(bank, u), 0.0, A.max, A.min)
-            return ("PK1", PARTS[u] + 15, PARTS[u + 1], 16)
-
-        def add(bank, u, i, first, last):
-            mm([H(bank, u) + (R("BO"), H(i, u), first, last)])
-
-        b1, b2, b3 = ("P2", "P4", "P4"), ("P1", "P3", "P7"), ("P0", "P2", "P5")
-        for u in range(2):
-            add(b2[u], u, "R256", True, False)
-        def tables(p0, p1, bank):
-            c, d = 16 * p0, 16 * p1
-            mm([(bank, 256 + c, 256 + d, R("BO"), ("SC", 16 * c + 15, 16 * d, 16), True, True)])
-            for b in range(0, 16, 2):
-                mm([("P7", c, d, ("LS", 128 * i, 128 * i + 128), ("SC", 16 * c + i, 16 * d, 16), i == 0, i == 15) for i in (b, b + 1)])
-            scan(R("W1T", c, d), R("KP", c, d), (bank, 256 + c, 256 + d), 0.0, A.max, A.min)
-            for p in range(p0, p1):
-                ts(("I1", 64 * p, 64 * p + 64), R("sB"), ("W1T", 16 * p + 15, 16 * p + 16), A.is_ge, float(p), A.add)
-            act(R("W2S", c, d), ("P7", c, d))
-
-        tables(0, OWN, "P0")
-        for u in range(2):
-            add(b1[u], u, "I1", True, True)
-        counts(1, (0, 1))
-        counts(1, (2,) if len(PARTS) > 3 else (2, 3))
-
-        def search(us):
-            for u in us:
-                pk = pick(b1[u], u)
-                cp(H("O1", u, 16), pk)
-                lin(H("T2", u, 16), pk, 16.0, C("r%d" % u))
-                add(b3[u], u, "R3", True, False)
-            for u in us:
-                tt(H("I2", u), (R("W2S"), H("O1", u, 16)), H("sR", u), A.is_le)
-                add(b2[u], u, "I2", False, True)
-            for u in us:
-                tt(H("O2", u, 16), pick(b2[u], u), H("T2", u, 16), A.add)
-            for u in us:
-                w = 256 * (PARTS[u] // CAP)
-                tt(H("XP", u), (("W3S", w, min(w + 544, 1056)), H("O2", u, 16)), H("sR", u), A.is_le)
-                add(b3[u], u, "XP", False, True)
-                ts(H("T3", u, 16), H("O2", u, 16), 16.0, A.mult, C("r3"), A.add)
-            for u in us:
-                tt(H("O3", u, 16), pick(b3[u], u), H("T3", u, 16), A.add)
-
-        search((0, 1))
-        act(H(send, 0), (("CAND", 0, J + DUM), H("O3", 0, 16)))
-        cp(R(send, PARTS[1], 192), (("CAND", 0, J + DUM), R("O3", PARTS[1] // 16, 12)))
+    def send(t):
+        o, n = 256 * t, str(t)
+        for q, out, c, d in zip(SV, (R("SEND", o, o + 128), R("SEND", o + 128, o + 192), R("LAND", o + 64 * rank, o + 64 * rank + 64)), (0, 8, 12), (8, 12, 16)):
+            (act if q == "S" else cp)(out, (R("CAND"), R("O3", c, d)))
         tr = []
         for i, p in enumerate(owners[:-1]):
             rid, pid = topo.addr(T.cores[p])[:2]
             e = topo.engines(core, T.cores[p])
-            mask = sum(1 << x for x in (e[0::2] + e[1::2])[4 * i:4 * i + 4])
-            tr.append(RemoteDMATransfer(dst_ids=[DstId(rid=rid, pnc=pid)], dma_engine_mask=mask, remote_sem=T.sem["arr%d" % t],
-                                        src=T[send][:, 64 * i:64 * i + 64], dst=T[land][:, 64 * rank:64 * rank + 64]))
-        others = [(land, 64 * p, 64 * p + 64) for p in owners[:-1]]
+            mask = sum(1 << x for x in (e[0::2] + e[1::2])[ENG[i][0]:ENG[i][1]])
+            tr.append(RemoteDMATransfer(dst_ids=[DstId(rid=rid, pnc=pid)], dma_engine_mask=mask, remote_sem=T.sem["arr" + n],
+                                        src=ap(R("SEND", o + 64 * i, o + 64 * i + 64)), dst=ap(R("LAND", o + 64 * rank, o + 64 * rank + 64))))
+        others = [R("LAND", o + 64 * p, o + 64 * p + 64) for p in owners[:-1]]
 
-        def write(t=t, tr=tr, others=others):
-            g.remote_dma_fused(tr, local_sem=T.sem["snt%d" % t])
-            count["snt%d" % t] = count["arr%d" % t] = 12
-            note("G", [], others, ("arr%d" % t, 12), True)
-        later("G", write, [R(send, 0, 192)], others, 100, FLY if t else 2 * FLY)
-        if len(PARTS) > 3:
-            add(b1[2], 2, "I1", True, True)
-            counts(1, (3,))
-            add(b2[2], 2, "R256", True, False)
-            search((2,))
-            act((land, 64 * rank, 64 * rank + 64), (("CAND", 0, J + DUM), R("O3", 12, 16)))
-        else:
-            cp((land, 64 * rank, 64 * rank + 64), (("CAND", 0, J + DUM), R("O3", 12, 16)))
-        hold[:] = [R(*HOLD)]
-        if t == 0:
-            ts(C("wi"), C("l"), 3.5, A.mult, 2.25, A.add)
-            ts(R("MK2"), R("R256"), C("l"), A.not_equal, 9984.0, A.mult)
-            if PAIRS:
-                fill(R("E2"), 2.0)
-            for c in PAIRS:
-                ts(R("MK2", 16 * c + 16), R("MK2", 16 * c + 16), 32.0, A.add)
-            ts(R("MKB"), R("R256"), C("l"), A.not_equal, 2.0 ** 21, A.mult)
-            ts(R("KZ"), R("R256"), 0.0, A.is_equal, ZK + 2.0 ** 20, A.mult)
-            ts(R("I16"), R("I16"), C("l"), A.add)
-            ts(C("cr"), C("l"), 0.0, A.is_equal, -2048.0, A.mult)
-            ts(C("cr1"), C("l"), 1.0, A.is_equal, 0.25 - rank / 4.0, A.mult)
-            ts(R("KZ"), R("KZ"), -2.0 ** 20, A.add)
-            ts(R("TB"), R("I16"), float(TR), A.add)
-            act(R("WB"), R("BO"), scale=C("wi"))
-            act(R("NBO"), R("BO"), scale=-1.0)
-            lin(C("cr"), C("cr"), 1.0, C("cr1"))
-            act(R("CR"), R("ONE256"), scale=C("cr"))
-            do("V", lambda: g.vector.reciprocal(ap(C("rc0")), ap(K("RN", 0))), [K("RN", 0)], [C("rc0")])
-            act(C("s2"), K("RN", 0), scale=1.0 / 2048)
-            fill(K("AC", 2), 256.0)
-            ts(C("aa"), C("rc0"), -2047.5, A.mult)
-            cp(K("AC", 0), C("aa"))
-            tt(K("AC", 1), C("aa"), K("AC", 0), A.subtract)
-        for b, w, c, first in (("P1", "BO", "CR", True), ("P1", "IDN", "MKB", False), ("P4", "BO", "CR", True), ("P3", "NID", "MK2", True)):
-            mm([(b, 0, 256, R(w), R(c), first, False)])
-        lin(C("Told"), C("Told"), 1.0, C("e%d" % t))
-        if t < RO - 1:
-            act(K("RN", 3 + t), C("e%d" % t))
-            anti(t + 1)
-            hold[:] = [R(land)]
-            mm([("P2", 0, 1, R("IDN"), K("AC", i), i == 0, False) for i in range(3)] + [("P0", 0, 1, R("IDN"), K("AC", 2), True, False)])
-            hold[:] = [R(*HOLD)]
-            prepare(t + 1)
-        lin(R("TI"), R("I16"), 1.0, C("Told"))
-        if t:
-            tt(R("UO2"), R("BD"), R("NK"), A.max)
-            for c in range(0, 16, US):
-                cp((("USED", 0, TR + 256), R("UO2", c, c + US)), R("ONE256", 0, 16 * US))
-        if t < RO - 1:
-            shares(t + 1)
-            act(C("TqO"), C("Told"), scale=2.0 ** -12)
-            steps(t + 1)
-            cp(R("RCF"), R("RC", 256 * (t + 1), 256 * (t + 1) + 256))
-            sums(t + 1)
+        wide = [d - c for c, d in ENG]
+        come = sum(wide[order(q).index(rank)] for q in range(N) if q != rank)
+
+        def write(c, d):
+            g.remote_dma_fused(tr[c:d], local_sem=T.sem["snt" + n])
+            count["snt" + n], count["arr" + n] = sum(wide), come
+            note("G", [], others if d == 3 else [], ("arr" + n, come), True)
+        for c, d in CALLS:
+            later("G", lambda c=c, d=d: write(c, d), [R("SEND", o + 64 * c, o + 64 * d)], others if d == 3 else [K("turn", 15)], 100, FLY if t else 2 * FLY)
+            hold[:] = [K("turn", 15)]
         hold[:] = []
-        mm([("P1", 0, 256, R("WB"), R(land), False, True)])
-        mm([("P4", 0, 256, R("WB"), R(land), False, True)])
-        pk = ("PK1", 15, 256, 16)
-        scan(R("PK1"), R("KZ"), ("P1", 0, 256), 0.0, A.max, A.min)
-        ts(R("T16"), pk, M35, A.add, M35 + 4096.0, A.subtract)
-        tt(R("BC"), pk, R("T16"), A.subtract)
-        for c, d in BRC:
-            ts(R("XT", c, d), ("P4", c, d), M35, A.add, M35 + 4096.0, A.subtract)
-            tt(R("BR", c, d), ("P4", c, d), R("XT", c, d), A.subtract)
-        ts(R("NV"), pk, 2.0 ** 19, A.is_ge, 4096.0, A.mult)
-        if PAIRS:
-            lin(R("BI"), R("BC"), 1.0, -0.25)
-        for n in range(16):
-            c = EO[n]
-            k = max(i for i in range(len(EG) - 1) if EG[i] <= c)
-            o = 256 * k + 16 * c
-            if c - 1 in PAIRS:
-                f = 256 * PAIRS.index(c - 1)
-                ts(("E2", f + 16 * c + 16, f + 256), ("BR", 16 * c + 16, 256), K("BI", c), A.is_equal, 2.0, A.add)
-                scan(("E3", f + 16 * c, f + 256), ("E", o, o + 256 - 16 * c), ("E2", f + 16 * c, f + 256), 2.0, A.min, A.add)
-                mm([("P3", 16 * c, 256, R("BO"), ("E3", f + 16 * c, f + 256), False, False)])
-                ts(("E", o, o + 16), ("BR", 16 * c, 16 * c + 16), K("BI", c), A.is_equal)
-            else:
-                ts(("E", o, o + 256 - 16 * c), ("BR", 16 * c, 256), 0.25, A.add, K("BC", c), A.is_equal)
-            if c < 15 and c not in PAIRS and c - 1 not in PAIRS:
-                mm([("P3", 16 * c + 16, 256, R("BO"), ("E", o + 16, o + 256 - 16 * c), False, False)])
-            if c + 1 == EG[k + 1]:
-                mm([("P3", 16 * EG[k], 16 * c + 16, R("SU"), ("E", 256 * k + 16 * EG[k], o + 16), False, n == 15)])
-            if n == 1:
-                tt(R("BD"), R("BC"), R("NV"), A.add)
-            if n == 3:
-                ts(R("UO"), R("BD"), -2048.25, A.add)
-                act(R("UG"), (("USED", 0, TR + 256), R("UO")), scale=-1.0)
-                lin(R("BD"), R("BD"), 1.0, -2048.25)
-        tt(R("XP"), ("P3", 0, 256), R("UG"), A.is_gt)
-        scan(("XS", 16, 272), R("XP"), R("XP"), 0.0, A.add, A.max)
-        sk = ("XS", 31, 272, 16)
-        if t < RO - 1:
-            mm([("P2", 0, 1, R("NBO"), K("XS", 271), False, True)])
-            mm([("P0", 0, 1, R("NBO"), K("XS", 271), False, True)])
-        mm([("P5", 0, 16, R("NBO"), sk, True, False), ("P5", 0, 16, R("UP"), sk, False, False), ("P5", 1, 16, R("NU"), ("XS", 31, 256, 16), False, True)])
-        tt(R("NK"), sk, ("XS", 15, 256, 16), A.subtract)
 
-    tt(R("NK"), R("NK"), R("TB"), A.mult)
-    places()
-    cp((("BANK", 0, TR + 256), R("SO")), R("LAND%d" % (RO - 1)))
-    dma("Y", [(T.y[:, :], T.BANK[:, B:TR])], [("BANK", B, TR)], [], 3000)
+    def mark():
+        tt(R("NK"), R("NE"), R("TB", 16), A.mult)
+        tt(R("UO2"), R("NK"), R("UO"), A.max)
+        for c in range(0, 16, US):
+            cp((R("USED"), R("UO2", c, c + US)), R("ONE", 0, 16 * US))
+
+    def receive(t):
+        land, pk = R("LAND", 256 * t, 256 * t + 256), R("PK", 15, 256, 16)
+        d = R("P3", 0, 256)
+        mm((d, R("WQ"), R("DG"), True, False))
+        for f, a, b in KEYS:
+            a, b, l = R(a, *f), R(b, *f), (f[0] // 16, f[1] // 16)
+            mm((a, R("BO"), R("CK", *f), True, False), (a, R("IDN"), R("MKB", *f), False, False))
+            mm((b, R("BO"), R("CK", *f), True, False))
+            hold[:] = [land]
+            mm((b, R("WB"), R("LAND", 256 * t + f[0], 256 * t + f[1]), False, True))
+            mm((a, R("WB"), R("LAND", 256 * t + f[0], 256 * t + f[1]), False, True))
+            hold[:] = []
+            scan(R("PK", *f), R("KZ", *f), a, 0.0, A.max, A.min)
+            lin(R("HB", *f), b, 1.0, -2048.0)
+            lin(R("T16", *l), R("PK", f[0] + 15, f[1], 16), 1.0, -2048.0, EN["T16"])
+            tt(R("BC", *l), R("PK", f[0] + 15, f[1], 16), R("T16", *l), A.subtract)
+            tt(R("BR", *f), b, R("HB", *f), A.subtract)
+        tt(R("UO"), pk, R("T16"), A.subtract)
+        act(R("UG"), (R("USED"), R("UO")))
+        for n, c in enumerate(EO):
+            o = 256 * (c // EG) + 16 * c
+            ts(R("E", o, o + 256 - 16 * c), R("BR", 16 * c), 0.25, A.add, K("BC", c), A.is_equal)
+            if n == UK:
+                mm((d, R("BO"), R("UG"), False, False))
+            if c < 15:
+                mm((R("P3", 16 * c + 16, 256), R("BO"), R("E", o + 16, o + 256 - 16 * c), False, False))
+            if c % EG == EG - 1:
+                mm((R("P3", 16 * (c + 1 - EG), 16 * c + 16), R("WQ"), R("E", o + 16 - 16 * EG, o + 16), False, n == 15))
+        act(R("D"), d, F.Sign, -1.0, C("e%d" % t))
+        scan(R("XS", 16), R("D"), R("ONE"), 0.0, A.add, A.add)
+        scan(R("C1"), R("KP"), R("XS", 16), 0.0, A.max, A.min)
+        scan(R("C0"), R("KP"), R("XS", 15, 271), 0.0, A.max, A.min)
+        c1, c0 = R("C1", 15, 256, 16), R("C0", 15, 256, 16)
+        tt(R("NE"), c1, c0, A.is_equal)
+        lin(R("PO"), c1, 0.5, C("tm%d" % t) if t else -1.0)
+        tt(R("NK"), R("NE"), R("TB", 0, 16), A.mult)
+        tt(R("SO"), R("PO"), R("NK"), A.max)
+        cp((R("BANK", B), R("SO")), land)
+
+    prepare(0)
+    for t in range(RO):
+        decode(t)
+        if t == 0:
+            common()
+        operands(t)
+        search(t)
+        hold[:] = [R(*HOLD)]
+        if t:
+            mark()
+        else:
+            hold[:] = []
+            arrivals()
+            picks(1)
+            picks(2)
+            hold[:] = [R(*HOLD)]
+        if t < RO - 1:
+            prepare(t + 1)
+        hold[:] = []
+        send(t)
+        receive(t)
+    dma("Y", [(T.y[:, :], ap(R("BANK", B, TR)))], [R("BANK", B, TR)], [], 3000)
     schedule()
     for s in sorted(count):
         g.wait_ge(T.sem[s], count[s])

import math
import numpy as np
from concourse.bass import DstId, RemoteDMATransfer
from concourse.mybir import dt, AluOpType as A, AxisListType, ActivationFunctionType as F

B, J, CAP, RO, Q, N = 3328, 4096, 64, 3, 4096, 4
TR = 4096
DUM = 288
M23 = 8388608.0
M24 = 16777218.0
M27 = 201326592.0
MB = 532480.0
EPS = 2.0 ** -13
NONE = 4096
ZK = 786432.0 + 4095.875

ORDER = ("z:0:64 x:64:128 Xz:0:64 Ymax:64:128 x:128:160 y:128:160 sub:128:160:P5 Yx:0:64 x:160:192 y:160:192 sub:160:192:P6 Zy:64:128 "
         "sum:0:128 abs:128:160:P5 x:192:224 abs:160:192:P6 Zd:128:160 Yadd:192:224 Zd:160:192 x:224:256 y:224:256 first:0 sum:128:192 "
         "Zy:192:224 first:1 first:2 add:224:256:P0 z:224:256 sum:192:224 cut:224:256:P0 sum:224:256 first:3")
COSTS = ((1.56, 3.8, 0, 200, 1.0), (1.3, 3.0, 40, 220, 1.2), (2.0, 4.5, 0, 160, 0.8))
TRIES, SEED, USE, HEAT = 260000, 0, 3, (0.002, 0.0001)
FLY = 1100
BANKT = 6500
DM = 2000
LV = "VSVSVSVS"
SV = "SVV"
EN = dict(al="V", ga="V", th="V", T16="V", X1="SV", CD="SV", W3="VVVVVVVV", A1="V")
PARTS = ((0, 2), (2, 3), (3, 4))
CE = (("P7", "P3", "P7", "P3"), ("P1", "P3", "P1", "P3"))
UK = 11
US = 8
EO = (8, 10, 12, 14, 0, 2, 4, 6, 9, 11, 13, 15, 1, 3, 5, 7)
HOLD = ("KI", 128)
START = (0, 1)
ORDER0 = ORDER.replace("z:0:64 ", "z:0:64 Z:224:256 ", 1).replace(" z:224:256", "")
DIRECT = 0
EG = 2
FIX = "VS"
ENG, CALLS = ((0, 2), (2, 4), (4, 6)), ((0, 3),)
CN = ("SSSS", "SSSS")
KEYS = (((128, 256), "P1", "P4"), ((0, 128), "P2", "P5"))
INP = (1, 1)
FS = 40
PASSES, WIDE = 16, 120
DBG = []
ISSUE = []

BUF = dict(bfloat16=dict(BANK=TR + 256, USED=TR + 256, CAND=J + DUM, TX=J, TY=J, TZ=J, JK=2048, JS=2048, R64=256, AL=256, SG=256, GM=128, LT=1024, X1=512, OB=256,
                         CD=256, FM=1024, SC=1024, W3S=1088, I1=256, I2=256, XP=256, SEND=768, LAND=768, HB=256, T16=16, E=2048, UG=256, D=256,
                         XS=272, C1=256, C0=256, LX=128, GR=128, LR=128, TM=128, BO=128, NU=128, IDN=128, NID=128, WQ=128, WB=128, JL=128,
                         IOC=256, WT=32, S32=128, SK=384, ONE=256, R16=256, MKS=256, sR=256, KP=256, MKB=256, DG=256, CK=256, UB=256, RST=48),
           float32=dict(ZT=256, JC=128, XT=256, YT=256, RCF=256, T2=16, T3=16, PK=256, BC=16, NK=16, PO=16, RN=48, T8=48, PB=48, CF=16, SEL=128, ACC=32, A1=32, OC=16, SV=4, IC0=256,
                        NIC=256, ONF=128, TRI=128, KZ=256, I48=48, REP=48, E7=48, MV=48, MK=144, XW=64, I16=16, TB=32, NE=16, QR=16, QS=16, cols=96, turn=208),
           int32=dict(RA=768, RB=768, RC=768, KI=256, WI=4, ip=12, NI=4, UI=256),
           uint16=dict(XO=256, YO=256, ZO=256, O1=16, O2=16, O3=16, UO=16, SO=16, UO2=16, BR=256))
PLACE, SCRATCH = {}, {}
for _d in BUF:
    _at = 0
    for _n, _w in BUF[_d].items():
        if _w > 1000:
            SCRATCH[_n] = ("sbuf", [128, _w], _d)
            PLACE[_n] = (_n, 0, _w, _d)
        else:
            PLACE[_n] = ("pool_" + _d, _at, _w, _d)
            _at += -(-_w // 16) * 16
    SCRATCH["pool_" + _d] = ("sbuf", [128, _at], _d)
for _b in range(8):
    SCRATCH["P%d" % _b] = ("psum", [128, 512], "float32")
    PLACE["P%d" % _b] = ("P%d" % _b, 0, 512, "float32")

SEMAPHORES = ["cV", "cS", "cP", "cG"] + ["d%d" % i for i in range(16)] + [x + str(i) for x in ("arr", "snt") for i in range(RO)]


def rank_program(g, core, T, topo):
    rank = T.rank_of(core)
    if rank is None:
        return
    def order(q):
        return sorted(range(N), key=lambda p: (p == q, topo.die(T.cores[p]) == topo.die(T.cores[q])))

    owners = order(rank)
    queue = {"V": g.vector, "S": g.scalar, "P": g.tensor, "G": g, "Y": g.sync}
    count, snap, recs, names, nd, calls = {}, {}, {}, {}, [0], []
    known = {q: {} for q in queue}
    hold = []

    def R(b, lo=0, hi=None, step=1, p=(0, 128)):
        return (b, lo, PLACE[b][2] if hi is None else hi, step) + p

    def K(b, i, p=(0, 128)):
        return R(b, i, i + 1, 1, p)

    def C(name, p=(0, 128)):
        return K("cols", names.setdefault(name, len(names)), p)

    def ap(r):
        b, at = PLACE[r[0]][:2]
        return T[b][r[4]:r[5], at + r[1]:at + r[2]:r[3]] if r[3] > 1 else T[b][r[4]:r[5], at + r[1]:at + r[2]]

    def pair(x):
        return isinstance(x, tuple) and isinstance(x[0], tuple)

    def regs(*xs):
        return [r for x in xs if isinstance(x, tuple) for r in (x if pair(x) else [x])]

    def view(x):
        return ap(x[0]).indirect(ap(x[1])) if pair(x) else ap(x) if isinstance(x, tuple) else x

    def psum(b):
        return b[0] == "P" and b[1:].isdigit()

    def meet(r, s):
        return r[1] < s[2] and s[1] < r[2] and r[4] < s[5] and s[4] < r[5]

    def inside(r, s):
        return s[3] == 1 and r[1] >= s[1] and r[2] <= s[2] and r[4] >= s[4] and r[5] <= s[5]

    def size(r):
        return 16 * size(r[1]) if pair(r) else len(range(r[1], r[2], r[3]))

    def short(*rs):
        return all(PLACE[r[0]][3] in ("bfloat16", "uint16") for r in rs)

    def deps(q, reads, writes):
        need = {}
        for lst, w in ((reads, False), (writes, True)):
            for x in lst:
                for r, wrote, tok, q2 in recs.get(x[0], []):
                    clash = meet(r, x) and (w or wrote)
                    if (q2 != q or clash and q != "P") if psum(x[0]) else clash:
                        need[tok[0]] = max(need.get(tok[0], 0), tok[1])
        for s, v in need.items():
            if known[q].get(s, 0) < v:
                queue[q].wait_ge(T.sem[s], v)
                known[q][s] = v
        for s, v in need.items():
            for s2, v2 in snap.get((s, v), {}).items():
                known[q][s2] = max(known[q].get(s2, 0), v2)

    def note(q, reads, writes, tok, remote=False):
        snap[tok] = {} if remote else dict(known[q])
        for x in writes:
            recs[x[0]] = [r for r in recs.get(x[0], []) if not inside(r[0], x)] + [(x, True, tok, q)]
        for x in reads:
            recs[x[0]] = [r for r in recs.get(x[0], []) if r[1] or r[3] != q or not inside(r[0], x)] + [(x, False, tok, q)]

    def later(q, issue, reads, writes, busy, more=0):
        calls.append((q, issue, reads, writes, busy if isinstance(busy, tuple) else (busy, 0, 0), more, list(hold)))

    def do(q, fn, reads, writes, busy):
        def issue():
            s = "c" + q
            count[s] = count.get(s, 0) + 1
            fn().then_inc(T.sem[s], 1)
            note(q, reads, writes, (s, count[s]))
        later(q, issue, reads, writes, busy)

    def mm(*lst):
        reads, writes = [x[1] for x in lst] + [x[2] for x in lst], [x[0] for x in lst]

        def issue():
            last = [g.tensor.matmul(ap(o), ap(lh), ap(rh), st, sp) for o, lh, rh, st, sp in lst][-1]
            count["cP"] = count.get("cP", 0) + 1
            last.then_inc(T.sem["cP"], 1)
            note("P", reads, writes, ("cP", count["cP"]))
        later("P", issue, reads, writes, sum(max(min(64, size(x[1])), size(x[2])) * (1 if short(x[1]) else 4) for x in lst))

    def dma(q, pairs, reads, writes, more):
        def issue():
            sem = "d%d" % nd[0]
            nd[0] += 1
            for out, in_ in pairs:
                queue[q].dma_start(out, in_).then_inc(T.sem[sem], 16)
            count[sem] = 16 * len(pairs)
            note(q, reads, writes, (sem, count[sem]))
        later(q, issue, reads, writes, 64 * len(pairs), more)

    def cycles(out, in0, fast):
        return (0, 0, size(out)) if pair(out) else (0, size(in0), 0) if pair(in0) else size(in0) * fast

    def schedule():
        seen, pre = {}, []
        for i, (q, _, reads, writes, _, _, held) in enumerate(calls):
            e = {}
            for lst, w in ((reads + held, False), (writes, True)):
                for x in lst:
                    for r, wrote, j, q2 in seen.get(x[0], []):
                        if meet(r, x) and (w or wrote) or psum(x[0]) and (q2 != q or q == "P"):
                            e[j] = not (q2 == q == "P" and psum(x[0]) or x[0] == "turn") or e.get(j, False)
            for lst, w in ((writes, True), (reads, False)):
                for x in lst:
                    seen[x[0]] = [r for r in seen.get(x[0], []) if not (w and inside(r[0], x))] + [(x, w, i, q)]
            pre.append(e)
        every, who = range(len(calls)), [c[0] for c in calls]
        post = [[] for _ in every]
        for i in every:
            for j in pre[i]:
                post[j].append(i)
        sinks = [i for i in every if not post[i]]

        def priced(ga, sc, fixed, hop, far):
            busy = [c[4][0] if c[0] not in "VS" or c[5] else 60 + ga * c[4][1] + sc * c[4][2] if c[4][1] + c[4][2] else
                    (c[4][0] + fixed if fixed else max(64, c[4][0])) + FS * (c[0] == "S") for c in calls]
            return busy, [[(j, hop + far * calls[j][5] if w else 0) for j, w in e.items()] for e in pre], [far * c[5] for c in calls]

        def fit(order, busy, before, head):
            taken, end = {q: [] for q in queue}, [0.0] * len(calls)
            for i in order:
                at, l = max([end[j] + gap for j, gap in before[i]] + [head[i]]), taken[who[i]]
                k = len(l)
                while k and l[k - 1][1] > at:
                    k -= 1
                while k < len(l) and l[k][0] < at + busy[i]:
                    at = max(at, l[k][1])
                    k += 1
                l.insert(k, (at, at + busy[i]))
                end[i] = at + busy[i]
            return end

        def first(busy, before, more):
            after = [[(j, dict(before[j])[i]) for j in post[i]] for i in every]
            tail = more[:]
            for i in reversed(every):
                tail[i] = busy[i] + max([tail[i]] + [tail[j] + gap for j, gap in after[i]])
            end = fit(sorted(every, key=lambda i: (-tail[i], i)) if START[0] else every, busy, before, [0] * len(calls))
            for _ in range(START[1]):
                back = fit(sorted(every, key=lambda i: (-end[i], -i)), busy, after, more)
                end = fit(sorted(every, key=lambda i: (-back[i], i)), busy, before, [0] * len(calls))
            return sorted(every, key=lambda i: (end[i] - busy[i], i))

        def sweep(order, busy, links, end, free):
            for i in order:
                at = free[who[i]]
                for j, gap in links[i]:
                    if end[j] + gap > at:
                        at = end[j] + gap
                end[i] = free[who[i]] = at + busy[i]

        def frame(order, a, b, price):
            busy, before, more = price
            end, tail, out, free, next_ = [0.0] * len(calls), [0.0] * len(calls), more[:], dict.fromkeys(queue, 0.0), dict.fromkeys(queue, 0.0)
            sweep(order[:a], busy, before, end, free)
            for i in reversed(order[b:]):
                tail[i] = next_[who[i]] = busy[i] + max(out[i], next_[who[i]])
                for j, gap in before[i]:
                    out[j] = max(out[j], gap + tail[i])
            return busy, before, end, free, out, next_, max([end[i] + out[i] for i in order[:a]] + [0.0])

        def run(part, f):
            busy, before, end, free, out, next_, rest = f
            end, free = end[:], dict(free)
            sweep(part, busy, before, end, free)
            return max(rest, max([end[i] + out[i] for i in part]), max([free[q] + next_[q] for q in free])), end

        def path(part, f, got):
            busy, before, _, _, out, next_, _ = f
            (total, end), last, prev, pairs = got, {}, {}, []
            for i in part:
                prev[i], last[who[i]] = last.get(who[i]), i
            w = [i for i in part if end[i] + out[i] >= total - 1e-6] + [i for q, i in last.items() if end[i] + next_[q] >= total - 1e-6]
            while w and w[0] in prev:
                i = w[0]
                at = end[i] - busy[i] - 1e-6
                w = [j for j, gap in before[i] if end[j] + gap >= at]
                if not w and prev[i] is not None and end[prev[i]] >= at:
                    pairs.append((prev[i], i))
                    w = [prev[i]]
            return pairs

        def move(part, j, i, far, ahead):
            a, b = part.index(j), part.index(i)
            if ahead:
                a = ([a] + [x for x in range(a - 1, max(a - 40, -1), -1) if who[part[x]] == who[i]])[:far + 1][-1]
                need = {i}
                for x in reversed(part[a:b + 1]):
                    if not need.isdisjoint(post[x]):
                        need.add(x)
            else:
                b = ([b] + [x for x in range(b + 1, min(b + 40, len(part))) if who[part[x]] == who[i]])[:far + 1][-1]
                need = {j}
                for x in part[a:b + 1]:
                    if not need.isdisjoint(pre[x]):
                        need.add(x)
            if part[a if ahead else b] not in need:
                return part[:a] + sorted(part[a:b + 1], key=lambda x: (x in need) != ahead) + part[b + 1:]

        if not ISSUE:
            prices, rng = [priced(*c) for c in COSTS[:USE]], np.random.default_rng(SEED)
            def length(order):
                return [run(order, frame(order, 0, len(order), p))[0] for p in prices]
            order = min((first(*p) for p in prices), key=lambda o: sum(length(o)))
            unit, best = length(order), 1.0
            ISSUE.extend(order)
            starts = [a for n in range(PASSES) for a in range(-(n % 2) * WIDE // 4, len(calls) - WIDE // 2, WIDE // 2)]
            for n, a in enumerate(starts):
                a, b, heat = max(a, 0), a + WIDE, HEAT[0] * (HEAT[1] / HEAT[0]) ** (n / len(starts))
                part, frames = order[a:b], [frame(order, a, b, p) for p in prices]
                got = [run(part, f) for f in frames]
                paths, now = [path(part, f, x) for f, x in zip(frames, got)], sum(x[0] / u for x, u in zip(got, unit)) / USE
                for d0, d1, d2, d3, d4 in rng.random((TRIES // len(starts), 5)).tolist():
                    pairs = paths[int(d4 * USE)]
                    new = pairs and move(part, *pairs[int(d0 * len(pairs))], (0, 0, 1, 2, 4)[int(d1 * 5)], d2 < 0.5)
                    if new:
                        got = [run(new, f) for f in frames]
                        mean = sum(x[0] / u for x, u in zip(got, unit)) / USE
                        if mean <= now - heat * math.log(1 - d3):
                            part, now, paths = new, mean, [path(new, f, x) for f, x in zip(frames, got)]
                            if mean < best:
                                best = mean
                                ISSUE[:] = order[:a] + part + order[b:]
                order = order[:a] + part + order[b:]
            DBG.extend([unit, best])
        for i in ISSUE:
            deps(calls[i][0], calls[i][2], calls[i][3])
            calls[i][1]()

    def ts(out, in0, s1, op0, s2=None, op1=None):
        n = cycles(out, in0, 0.5 if short(*regs(out, in0)) else 1)
        if op1 is None:
            do("V", lambda: g.vector.tensor_scalar(ap(out), view(in0), view(s1), None, op0), regs(in0, s1), [out], n)
        else:
            do("V", lambda: g.vector.tensor_scalar(ap(out), view(in0), view(s1), view(s2), op0, op1), regs(in0, s1, s2), [out], n)

    def tt(out, in0, in1, op):
        n = cycles(out, in0, 1 if pair(in0) or psum(in0[0]) or psum(in1[0]) else 2)
        do("V", lambda: g.vector.tensor_tensor(ap(out), view(in0), view(in1), op), regs(in0, in1), [out], n)

    def cp(out, in0):
        if pair(out):
            do("V", lambda: g.vector.tensor_copy(view(out), ap(in0)), [in0, out[1]], [out[0]], cycles(out, in0, 1))
        else:
            do("V", lambda: g.vector.tensor_copy(ap(out), view(in0)), regs(in0), [out], cycles(out, in0, 0.5 if short(*regs(out, in0)) else 1))

    def scan(out, d0, d1, init, op0, op1):
        do("V", lambda: g.vector.tensor_tensor_scan(ap(out), ap(d0), ap(d1), view(init), op0, op1), regs(d0, d1, init), [out],
           cycles(out, d0, 0.5 if short(out, d0, d1) else 1))

    def fill(r, c):
        do("V", lambda: g.vector.memset(ap(r), c), [], [r], cycles(r, r, 0.5 if short(r) else 1))

    def act(out, in0, func=F.Copy, scale=1.0, acc=None, bias=0.0):
        n = cycles(out, in0, 1)
        do("S", lambda: g.scalar.activation(ap(out), view(in0), func, bias=view(bias), scale=view(scale), accum_out=view(acc)),
           regs(in0, scale, bias), regs(out, acc), max(n, 64) + 24 if acc else n)

    def lin(out, in0, scale, bias, q="S"):
        if q == "S":
            act(out, in0, F.Identity, scale, None, bias)
        else:
            ts(out, in0, scale, A.mult, bias, A.add)

    def iota(r, pattern, base=0, cm=0):
        if PLACE[r[0]][3] == "int32":
            do("G", lambda: g.iota(ap(r), pattern, base, cm), [], [r], 160 + 2 * size(r))
        else:
            do("G", lambda: g.iota(ap(r), pattern, base, cm, allow_small_or_imprecise_dtypes=True), [], [r], 160 + 2 * size(r))

    def sel(out, in0, pattern, op, fl, base, cm):
        do("G", lambda: g.affine_select(ap(out), ap(in0), pattern, op, fl, base, cm), [in0], [out], 200 + 2 * size(out))

    p32, ni = (0, 32), PLACE["NI"][1]
    dma("Y", [(T.pool_int32[0:32, ni:ni + 1], T.ncl[:, :])], [], [K("NI", 0)], DM)
    for b, n, more in (("RC", 256, DM + 900), ("BANK", B, BANKT), ("RA", 256, BANKT + 800), ("RB", 256, BANKT + 1600)):
        calls[-1][3].append(K("turn", len(calls)))
        hold[:] = [K("turn", len(calls))]
        dma("Y", [(ap(R(b, 0, n)), T[b.lower()][:, 0:n])], [], [R(b, 0, n)], more)
    calls[-1][3].append(K("turn", len(calls)))
    hold[:] = [K("turn", len(calls))]
    dma("Y", [(T.pool_int32[i:32:2, ni + 1:ni + 2], T.lim[:, :]) for i in range(2)], [], [K("NI", 1)], BANKT + 900)
    hold[:] = []
    dma("Y", [(ap(R("UI")), T.used[:, :])], [R("BANK", 0, 16)], [R("UI")], 2 * DM)
    dma("Y", [(ap(R(b, 256)), T[b.lower()][:, 256:768]) for b in ("RC", "RA", "RB")], [R("BANK", 0, 16)], [R(b, 256) for b in ("RC", "RA", "RB")], 3 * DM)

    ip = K("ip", 0)
    iota(ip, [[0, 1]], 0, 1)
    iota(R("GR"), [[1, 8], [0, 16]])
    iota(R("I48"), [[0, 6], [1, 8]])
    iota(R("I16"), [[1, 16]])
    iota(R("LR"), [[0, 8], [1, 16]])
    iota(R("IC0"), [[1, 256]])
    iota(R("TM"), [[0, 16], [1, 8]])
    iota(R("ONE"), [[0, 256]], 1)
    cols = (("p", 0, 127), ("g", 4, 7), ("l", 0, 15), ("k", 0, 7), ("r", 3, 1), ("q", 0, 1), ("g4", 2, 7), ("i4", 0, 3), ("kd", 1, 1))
    for i, (c, sh, m) in enumerate(cols):
        C(c)
        ts(K("ip", i + 1), ip, sh, A.logical_shift_right, m, A.bitwise_and)
    cp(R("cols", 0, len(cols)), R("ip", 1, len(cols) + 1))
    ts(R("SEL", p=p32), R("GR", p=p32), C("g4", p32), A.is_equal)
    ts(R("REP", p=p32), R("I48", p=p32), C("i4", p32), A.is_equal)
    ts(R("E7"), R("I48"), 7.0, A.is_equal)
    ts(R("RST"), R("I48"), 0.0, A.not_equal)
    cp(C("nf", p32), K("NI", 0, p32))
    ts(R("MV", p=p32), R("REP", p=p32), C("nf", p32), A.mult)
    mm((R("P0", 0, 48), R("SEL", p=p32), R("MV", p=p32), True, True))
    tt(R("RN"), R("P0", 0, 48), R("E7"), A.add)
    ts(R("BO"), R("GR"), C("g"), A.is_equal)
    lin(C("r0"), C("r"), -1.0, 1.0)
    lin(C("sg"), C("r"), 2.0, -1.0)
    ts(C("k0"), C("k"), 0.0, A.is_equal)
    ts(C("k6"), C("k"), 6.0, A.is_equal)
    ts(C("k1"), C("k"), 1.0, A.is_equal)
    lin(C("on"), C("k0"), 1.0, C("k6"))
    act(C("k0r"), C("k0"), scale=C("r"))
    ts(C("f"), C("k"), 0.5, A.is_ge, C("k0r"), A.add)
    ts(C("f6"), C("k"), 5.5, A.is_lt, C("f"), A.mult)
    act(C("sg8"), C("sg"), scale=-8.0)
    lin(C("gm"), C("on"), -2048.0, 2048.0)
    act(C("gm"), C("gm"), scale=C("sg"))
    lin(C("cm"), C("on"), -16.0, -2032.0)
    act(C("cm"), C("cm"), scale=C("sg"))
    lin(C("b1"), C("on"), -10000.0, -M24)
    act(C("c6"), C("k6"), scale=C("r"))
    act(C("c6"), C("c6"), scale=EPS)
    lin(C("cs"), C("k0r"), -1920.5, C("c6"))
    lin(C("cy"), C("k1"), -1.0, C("k0r"))
    act(C("rc"), C("r"), scale=1.0 / 128)
    ts(R("MK", 0, 8), R("I48", 0, 8), C("k"), A.is_equal, C("f6"), A.mult)
    ts(R("MK", 24, 32), R("I48", 0, 8), C("k"), A.subtract, -1.0, A.is_equal)
    tt(R("MK", 16, 24), R("MK", 0, 8), R("MK", 24, 32), A.subtract)
    act(K("MK", 31), C("cs"))
    ts(R("XW", 0, 16), R("I16"), C("k"), A.add, 7.0, A.is_equal)
    ts(R("XW", 0, 16), R("XW", 0, 16), C("f6"), A.mult)
    act(R("XW", 16, 32), R("XW", 0, 16), scale=2.0 ** -12)
    tt(R("XW", 33, 48), R("XW", 1, 16), R("XW", 0, 15), A.subtract)
    lin(R("XW", 48, 64), R("XW", 0, 16), -1.0, C("k0r"))

    def picks(t):
        o, m = 48 * t, 4 - t
        if t:
            act(R("MK", o, o + 32), R("MK", 0, 32))
            ts(K("MK", o + 23), C("k"), 3.0 + t, A.is_equal, 128.0, A.mult)
            act(C("ux%d" % t), K("MK", o + 23), scale=2.0 ** -20)
        act(R("MK", o + 8, o + 16), R("XW", 16 + m, 24 + m))
        act(K("MK", o + 32), K("XW", m))
        act(R("MK", o + 33, o + 39), R("XW", 33 + m, 39 + m))
        act(K("MK", o + 39), C("cy"), scale=128.0 if t else 0.0)
        act(R("MK", o + 40, o + 47), R("XW", 48 + m, 55 + m))
        act(K("MK", o + 47), C("cs"))

    picks(0)
    act(R("ONF"), R("BO"), scale=C("r"))
    ts(R("TRI"), R("TM"), C("k"), A.is_gt, 2.0, A.mult)
    tt(R("TRI"), R("TRI"), R("ONF"), A.mult)
    lin(R("IOC"), R("IC0"), 1.0 / 128, C("rc"))
    lin(R("NIC"), R("IC0"), -1.0 / 128, -2.0 ** -19)
    lin(R("JL"), R("LR"), C("sg"), 64.0)
    tt(R("JL"), R("JL"), R("BO"), A.mult)
    ts(R("JL"), R("JL"), -64.0, A.add)
    iota(R("IDN"), [[0, 128]], 1)
    sel(R("IDN"), R("IDN"), [[-1, 128]], A.is_equal, 0.0, 0, 1)

    def common():
        act(R("NID"), R("IDN"), scale=-1.0)
        lin(C("s4"), C("q"), -0.5, 0.25)
        ts(R("WT", 0, 8), R("I48", 0, 8), C("g"), A.is_equal)
        act(R("WT", 8, 16), R("WT", 0, 8), scale=-1.0)
        act(R("WT", 16, 24), R("WT", 0, 8), scale=C("s4"))
        lin(C("ks"), C("kd"), 2.0, -1.0)
        lin(C("qs"), C("q"), -2.0, 1.0)
        ts(C("lv", p32), K("NI", 1, p32), C("ks", p32), A.mult, 0.5, A.add)
        ts(C("lh", p32), C("lv", p32), M27, A.add, M27, A.subtract)
        ts(C("lh", p32), C("lh", p32), C("qs", p32), A.mult)
        ts(C("lv", p32), C("lv", p32), C("q", p32), A.mult, C("lh", p32), A.add)
        act(R("LX", p=p32), R("ONE", 0, 128, 1, p32), scale=C("lv", p32))
        lin(C("kd0"), C("kd"), -1.0, 1.0)
        for i, c in enumerate((C("kd0", p32), C("kd", p32), 0.0)):
            act(R("SK", 128 * i, 128 * i + 128, 1, p32), R("SEL", p=p32), scale=c)
        iota(R("R16"), [[0, 16], [1, 16]])
        iota(R("CAND", J, J + DUM), [[0, DUM]], NONE)
        iota(R("W3S", 1024), [[0, 64]])
        iota(R("sR"), [[0, 4], [1, 64]])
        iota(R("TB"), [[B, 2], [16, 16]], TR - B)
        iota(R("XS", 0, 16), [[0, 16]])
        zero = R("BANK", B, TR + 256)
        iota(zero, [[0, 1024]])
        dma("Y", [(ap(R("USED", c, c + 1024)), ap(zero)) for c in range(0, Q, 1024)], [zero, R("RB", 256)], [R("USED", 0, Q)], 2 * DM)
        iota(R("USED", TR, TR + 256), [[0, 256]], 1)
        for p in range(N):
            iota(R("OC", 4 * p, 4 * p + 4), [[0, 4]], 256 * p + 64 * (CN[0][p] + CN[1][p]).count("S"))
        iota(R("R64"), [[0, 256]], 1)
        sel(R("R64"), R("R64"), [[0, 4], [1, 64]], A.not_equal, 0.0, 0, 0)
        iota(R("SV"), [[16, 4]])
        sel(R("NU"), R("BO"), [[-1, 128]], A.is_gt, 0.0, 0, 1)
        act(R("NU"), R("NU"), scale=-1.0)
        ts(R("KP"), R("R16"), C("l"), A.is_equal, 32768.0, A.mult)
        ts(R("SV"), R("SV"), C("l"), A.add, 0.5, A.add)
        iota(R("KZ"), [[0, 256]], -2 ** 20)
        sel(R("KZ"), R("KZ"), [[0, 16], [1, 16]], A.not_equal, ZK, 0, 0)
        for p in range(N):
            lin(R("MKS", 64 * p, 64 * p + 64), R("KP", 0, 64), -64.0 - p / 8.0, 2.0 ** 21)
        hold[:] = []

    def arrivals():
        lin(R("MKB"), R("KP"), -64.0, 2.0 ** 21)
        act(R("DG"), R("KP"), scale=-2.0 ** -14)
        lin(R("TB"), R("TB"), 1.0, C("l"))
        lin(C("wi"), C("l"), 3.5, 2.25)
        act(R("WB"), R("BO"), scale=C("wi"))
        ts(C("ck"), C("l"), 0.0, A.is_equal, MB, A.mult)
        ts(C("ck1"), C("l"), 1.0, A.is_equal, 0.25 - rank / 4.0, A.mult)
        lin(C("ck"), C("ck"), 1.0, C("ck1"))
        act(R("CK"), R("ONE"), scale=C("ck"))
        ts(R("QR"), R("I16"), C("l"), A.is_le, -0.75, A.mult)
        lin(R("QR"), R("QR"), 1.0, 1.0)
        scan(R("QS"), R("QR"), R("ONE", 0, 16), 1.0, A.mult, A.mult)
        act(R("WQ"), R("BO"), scale=K("QS", 15))
        act(C("uy"), C("cy"), scale=EPS)
        act(C("s1"), K("RN", 0), scale=2.0 ** -12)
        lin(C("b0"), K("RN", 0), 2.0 ** -4, -1.0 + 2.0 ** -12)
        act(R("UB"), R("UI")) if EN.get("UB") else cp(R("UB"), R("UI"))
        dma("Y", [(T.USED[0:128:16, 0:Q], ap(R("UB")))], [R("UB")], [R("USED", 0, Q)], DM)

    def prepare(t):
        tt(R("T8"), R("RN"), R("MK", 48 * t, 48 * t + 48), A.mult)
        scan(R("PB"), R("RST"), R("T8"), 0.0, A.mult, A.add)
        ts(K("WI", 0), K("PB", 7), K("PB", 15), A.mult, -1024.5 + EPS, A.add)
        ts(C("wp"), K("WI", 0), 1024.0, A.add)
        mm((K("P6", 0), R("ONF"), C("wp"), True, True), (K("P6", 1), R("TRI"), C("wp"), True, True))
        ts(R("CF", 0, 4), R("PB", 23, 48, 8), M27, A.add, M27, A.subtract)
        tt(R("CF", 4, 8), R("PB", 23, 48, 8), R("CF", 0, 4), A.subtract)
        act(R("CF", 0, 8, 2), R("CF", 0, 8, 2), scale=2.0 ** -12)
        if t:
            lin(C("i0"), K("P6", 0), 1.0, -M24)
            lin(C("i1"), K("P6", 1), 1.0, C("b1"))
            cp(R("RCF"), R("RC", 256 * t, 256 * t + 256))
        else:
            cp(C("ct"), K("P6", 0))
            ts(C("c2"), K("P6", 1), C("b1"), A.add, M24, A.add)

    def decode(t):
        ct, c2 = C("ct"), C("c2")
        cf = [K("CF", i) for i in range(8)]
        if t:
            e = C("e%d" % (t - 1))
            lin(C("w2"), e, C("s1"), C("b0"))
            ts(ct, C("w2"), M24, A.add, C("i0"), A.add)
            ts(c2, C("w2"), M24, A.add, C("i1"), A.add)
            lin(C("tq"), e, EPS, C("tq0") if t > 1 else (B + 128) / 4096.0)
            lin(K("CF", 8), e, C("ux%d" % t), cf[4])
            lin(K("CF", 9), e, C("uy"), cf[6])
            cf[4], cf[6] = K("CF", 8), K("CF", 9)
            lin(R("ZT"), R("RCF"), C("tq"), C("zc"))
        else:
            lin(C("zc"), C("r"), 0.0, -1920.5 + EPS)
            ts(R("ZT"), R("RC", 0, 256), B / 4096.0, A.mult, -1920.5 + EPS, A.add)
        ts(R("ZO"), R("ZT"), M23 + 1920.0, A.add, M23, A.subtract)
        act(R("SG"), R("NIC"), F.Sign, ct, C("cnt"), c2)
        lin(C("al"), ct, C("sg8"), 0.0, EN["al"])
        lin(C("ga"), c2, C("gm"), C("r0"), EN["ga"])
        lin(C("ga"), ct, C("cm"), C("ga"), EN["ga"])
        ts(R("AL"), R("IOC"), ct, A.mult, c2, A.is_ge)
        lin(C("th"), C("cnt"), C("al"), C("ga"), EN["th"])
        if DIRECT:
            lin(R("JC"), R("JL"), ct, 0.0, EN.get("JC", "V"))
        ts(R("GM"), R("JL"), ct, A.mult, C("th"), A.is_ge)
        for n in range(4):
            pa, pb = R(("P1", "P2")[n // 2], 0, 256), R(("P3", "P4")[n // 2], 0, 256)
            inp, xt = INP[n // 2], R(("XT", "YT")[n // 2])
            if n % 2 == 0 and inp:
                mm((pb, R("IDN"), R("ONE"), True, False))
            for u in range(2):
                lt = R("LT", 256 * n + 128 * u, 256 * n + 128 * u + 128)
                if 2 * n + u < DIRECT:
                    ts(lt, R("JC"), C("th"), A.is_ge, cf[n + 4 * u], A.mult)
                else:
                    lin(lt, R("GM"), cf[n + 4 * u], 0.0, LV[2 * n + u])
                mm((pb, lt, R("AL"), u == 0 and not inp, u == 1) if n % 2 else (pa, lt, R("AL"), u == 0, u == 1))
            if n % 2 == 0:
                tt(pb if inp else xt, pa, R(("RA", "RB")[n // 2], 256 * t, 256 * t + 256), A.mult)
            else:
                if not inp:
                    tt(xt, pb, xt, A.add)
                ts(R(("XO", "YO")[n // 2]), pb if inp else xt, M23 + 1920.0, A.add, M23, A.subtract)
        if t == 1:
            e = C("e0")
            lin(C("n4"), e, 0.5, 128.0)
            act(R("RN", 4, 48, 8), R("ONE", 0, 6), scale=C("n4"))
            lin(C("tq0"), e, EPS, (B + 256) / 4096.0)
            lin(C("tm1"), e, 0.5, 127.0)
            lin(C("tm"), e, 0.5, 255.0)
        if t == 2:
            lin(C("tm2"), C("e1"), 0.5, C("tm"))

    def codes(h):
        pb, pc, a = "P%d" % (1 + h), R("P%d" % (3 + h), 0, 128), (128 * h, 128 * h + 128)
        ts(R("KI", *a), R(pb, 256, 384), 0.125, A.add)
        tt(R("OB", *a), R(pb, 256, 384), R("KI", *a), A.subtract)
        if EN["X1"][h] == "S":
            act(R("X1", 256 * h, 256 * h + 256), R(pb, 0, 256), F.Sign)
        else:
            ts(R("X1", 256 * h, 256 * h + 256), R(pb, 0, 256), 0.0, A.is_gt, 2.0, A.mult)
        mm((pc, R("OB", *a), R("IDN"), True, False))
        mm(*[(pc, R("X1", 256 * h + 128 * i, 256 * h + 128 * i + 128), R("NID"), False, i == 1) for i in range(2)])
        if EN["CD"][h] == "S":
            act(R("CD", *a), pc)

    def part(h):
        return [(256 * p + 128 * h, 256 * p + 128 * h + 128) for p in range(N)]

    def masks(h):
        for p, f in enumerate(part(h)):
            ts(R("FM", *f), R("CD", 128 * h, 128 * h + 128) if EN["CD"][h] == "S" else R("P%d" % (3 + h), 0, 128),
               (0.0, 0.25, -0.5, -0.25)[owners[p]] - (2.0 if EN["X1"][h] == "S" else 4.0), A.is_equal)

    def scans(h):
        for f in part(h):
            scan(R("SC", *f), R("FM", *f), R("FM", *f), K("SC", f[0] - 1) if h else 0.0, A.add, A.max)

    def counts(h, ps=range(N)):
        q = [(R("P%d" % (5 + p // 2), 256 * (p % 2) + 128 * h, 256 * (p % 2) + 128 * h + 128), part(h)[p]) for p in ps]
        for pb, f in q:
            mm((pb, R("BO"), R("SC", *f), True, False), (pb, R("NU"), R("FM", *f), False, True))
        for p, (pb, f) in zip(ps, q):
            (act if EN["W3"][4 * h + p] == "S" else cp)(R("W3S", *f), pb)

    def blocks(h, ps):
        for p in ps:
            ce, o = R(CE[h][p], 64 * p, 64 * p + 64), 1024 * h + 256 * p
            mm((ce, R("BO"), R("SC", part(h)[p][0] + 1, part(h)[p][1], 2), True, True))
            for m in range(4):
                jk = R("JK", o + 64 * m, o + 64 * m + 64)
                if CN[h][p] == "S":
                    act(jk, ce, F.Sign, -1.0, K("ACC", 16 * h + 4 * p + m), K("SV", m))
                else:
                    ts(jk, ce, K("SV", m), A.is_lt, 2.0, A.mult)
            if CN[h][p] == "V":
                scan(R("JS", o, o + 256), R("R64"), R("JK", o, o + 256), 0.0, A.mult, A.add)

    def counted(h, c, d):
        return R("ACC", 16 * h + 4 * c, 16 * h + 4 * d) if CN[h][c] == "S" else R("JS", 1024 * h + 256 * c + 63, 1024 * h + 256 * d, 64)

    def operands(t):
        def gath(o, c, d):
            old = o == "XO" and d <= J // 2 or o == "YO" and c >= J // 2
            return (R("BANK", 0, B if old else B + N * CAP * t), R(o, c // 16, d // 16))

        for h in range(2):
            mm((R("P%d" % (1 + h), 0, 384), R("LX", p=p32), R("SK", p=p32), True, False))
        mark = len(calls)
        steps(t, gath)
        for q in FIX:
            mine = [c for c in calls[mark:] if c[0] == q and (c[4][1] or c[4][0] >= 256)]
            for i, (a, b) in enumerate(zip(mine, mine[1:])):
                a[3].append(K("turn", 16 + 32 * (2 * t + "VS".index(q)) + i))
                b[6].append(a[3][-1])

    def steps(t, gath):
        for step in (ORDER if t or not ORDER0 else ORDER0).split():
            what, c, d, pb = (step.split(":") + [""] * 3)[:4]
            c, d = 16 * int(c or 0), 16 * int(d or 0)
            if what == "Z":
                cp(R("TZ", c, d), gath("ZO", c, d))
            elif what in "xyz":
                act(R("T" + what.upper(), c, d), gath(what.upper() + "O", c, d))
            elif what in ("sub", "add"):
                mm((R(pb, 0, d - c), R("IDN"), R("TX", c, d), True, False), (R(pb, 0, d - c), R("NID" if what == "sub" else "IDN"), R("TY", c, d), False, True))
            elif what == "abs":
                act(R("TZ", c, d), R(pb, 0, d - c) if pb else R("TY", c, d), F.Abs)
            elif what == "cut":
                tt(R("CAND", c, d), R(pb, 0, d - c), R("TZ", c, d), A.min)
            elif what == "sum":
                rows = (c % 2048 // 16, (d - 1) % 2048 // 16 + 1)
                for m in range(0, 16, 8):
                    mm(*[(R("P%d" % (1 + c // 2048), l, 384, 16, rows), R("CAND", c + l, d, 16), R("WT", 0, 24), False, l == 15) for l in range(m, m + 8)])
            elif what == "first":
                (codes, masks, scans, counts)[c // 16](0)
            else:
                o, w, op = {"Xz": ("TX", "TZ", A.min), "Yx": ("CAND", "TX", A.min), "Ymax": ("TY", "TX", A.max), "Yadd": ("TY", "TX", A.add),
                            "Ysub": ("TY", "TX", A.subtract), "Ymin": ("TY", "TX", A.min), "Xadd": ("TX", "TY", A.add), "Zx": ("CAND", "TX", A.min), "Zy": ("CAND", "TY", A.min), "Zd": ("CAND", "TZ", A.min)}[what]
                tt(R(o, c, d), gath(what[0] + "O", c, d), R(w, c, d), op)

    def search(t):
        for c, d in PARTS:
            blocks(0, range(c, d))
            tt(R("A1", 4 * c, 4 * d), counted(0, c, d), R("OC", 4 * c, 4 * d), A.add)
            lin(R("A1", 16 + 4 * c, 16 + 4 * d), R("A1", 4 * c, 4 * d), 1.0, 1.0, EN["A1"])
        codes(1)
        masks(1)
        scans(1)
        for (c, d), pb in zip(PARTS, ("P0", "P7", "P0", "P7")):
            blocks(1, range(c, d))
            counts(1, range(c, d))
            l, f = (4 * c, 4 * d), (64 * c, 64 * d)
            mm((R(pb, *f), R("IDN"), R("MKS", *f), True, False))
            for i, (o, x) in enumerate((("O1", "I2"), ("O2", "XP"))):
                tt(R(o, *l), counted(1, c, d), R("A1", 16 * i + l[0], 16 * i + l[1]), A.add)
                tt(R(x, *f), (R("W3S", 0, min(256 * d + 16, 1088)), R(o, *l)), R("sR", *f), A.is_le)
                mm((R(pb, *f), R("BO"), R(x, *f), False, i == 1))
            ts(R("T3", *l), R("O1", *l), 16.0, A.mult)
            scan(R("PK", *f), R("KZ", *f), R(pb, *f), 0.0, A.max, A.min)
            tt(R("O3", *l), R("PK", f[0] + 15, f[1], 16), R("T3", *l), A.add)

    def send(t):
        o, n = 256 * t, str(t)
        for q, out, c, d in zip(SV, (R("SEND", o, o + 128), R("SEND", o + 128, o + 192), R("LAND", o + 64 * rank, o + 64 * rank + 64)), (0, 8, 12), (8, 12, 16)):
            (act if q == "S" else cp)(out, (R("CAND"), R("O3", c, d)))
        tr = []
        for i, p in enumerate(owners[:-1]):
            rid, pid = topo.addr(T.cores[p])[:2]
            e = topo.engines(core, T.cores[p])
            mask = sum(1 << x for x in (e[0::2] + e[1::2])[ENG[i][0]:ENG[i][1]])
            tr.append(RemoteDMATransfer(dst_ids=[DstId(rid=rid, pnc=pid)], dma_engine_mask=mask, remote_sem=T.sem["arr" + n],
                                        src=ap(R("SEND", o + 64 * i, o + 64 * i + 64)), dst=ap(R("LAND", o + 64 * rank, o + 64 * rank + 64))))
        others = [R("LAND", o + 64 * p, o + 64 * p + 64) for p in owners[:-1]]

        wide = [d - c for c, d in ENG]
        come = sum(wide[order(q).index(rank)] for q in range(N) if q != rank)

        def write(c, d):
            g.remote_dma_fused(tr[c:d], local_sem=T.sem["snt" + n])
            count["snt" + n], count["arr" + n] = sum(wide), come
            note("G", [], others if d == 3 else [], ("arr" + n, come), True)
        for c, d in CALLS:
            later("G", lambda c=c, d=d: write(c, d), [R("SEND", o + 64 * c, o + 64 * d)], others if d == 3 else [K("turn", 15)], 100, FLY if t else 2 * FLY)
            hold[:] = [K("turn", 15)]
        hold[:] = []

    def mark():
        tt(R("NK"), R("NE"), R("TB", 16), A.mult)
        tt(R("UO2"), R("NK"), R("UO"), A.max)
        for c in range(0, 16, US):
            cp((R("USED"), R("UO2", c, c + US)), R("ONE", 0, 16 * US))

    def receive(t):
        land, pk = R("LAND", 256 * t, 256 * t + 256), R("PK", 15, 256, 16)
        d = R("P3", 0, 256)
        mm((d, R("WQ"), R("DG"), True, False))
        for f, a, b in KEYS:
            a, b, l = R(a, *f), R(b, *f), (f[0] // 16, f[1] // 16)
            mm((a, R("BO"), R("CK", *f), True, False), (a, R("IDN"), R("MKB", *f), False, False))
            mm((b, R("BO"), R("CK", *f), True, False))
            hold[:] = [land]
            mm((b, R("WB"), R("LAND", 256 * t + f[0], 256 * t + f[1]), False, True))
            mm((a, R("WB"), R("LAND", 256 * t + f[0], 256 * t + f[1]), False, True))
            hold[:] = []
            scan(R("PK", *f), R("KZ", *f), a, 0.0, A.max, A.min)
            lin(R("HB", *f), b, 1.0, -2048.0)
            lin(R("T16", *l), R("PK", f[0] + 15, f[1], 16), 1.0, -2048.0, EN["T16"])
            tt(R("BC", *l), R("PK", f[0] + 15, f[1], 16), R("T16", *l), A.subtract)
            tt(R("BR", *f), b, R("HB", *f), A.subtract)
        tt(R("UO"), pk, R("T16"), A.subtract)
        act(R("UG"), (R("USED"), R("UO")))
        for n, c in enumerate(EO):
            o = 256 * (c // EG) + 16 * c
            ts(R("E", o, o + 256 - 16 * c), R("BR", 16 * c), 0.25, A.add, K("BC", c), A.is_equal)
            if n == UK:
                mm((d, R("BO"), R("UG"), False, False))
            if c < 15:
                mm((R("P3", 16 * c + 16, 256), R("BO"), R("E", o + 16, o + 256 - 16 * c), False, False))
            if c % EG == EG - 1:
                mm((R("P3", 16 * (c + 1 - EG), 16 * c + 16), R("WQ"), R("E", o + 16 - 16 * EG, o + 16), False, n == 15))
        act(R("D"), d, F.Sign, -1.0, C("e%d" % t))
        scan(R("XS", 16), R("D"), R("ONE"), 0.0, A.add, A.add)
        scan(R("C1"), R("KP"), R("XS", 16), 0.0, A.max, A.min)
        scan(R("C0"), R("KP"), R("XS", 15, 271), 0.0, A.max, A.min)
        c1, c0 = R("C1", 15, 256, 16), R("C0", 15, 256, 16)
        tt(R("NE"), c1, c0, A.is_equal)
        lin(R("PO"), c1, 0.5, C("tm%d" % t) if t else -1.0)
        tt(R("NK"), R("NE"), R("TB", 0, 16), A.mult)
        tt(R("SO"), R("PO"), R("NK"), A.max)
        cp((R("BANK", B), R("SO")), land)

    prepare(0)
    for t in range(RO):
        decode(t)
        if t == 0:
            common()
        operands(t)
        search(t)
        hold[:] = [R(*HOLD)]
        if t:
            mark()
        else:
            hold[:] = []
            arrivals()
            picks(1)
            picks(2)
            hold[:] = [R(*HOLD)]
        if t < RO - 1:
            prepare(t + 1)
        hold[:] = []
        send(t)
        receive(t)
    dma("Y", [(T.y[:, :], ap(R("BANK", B, TR)))], [R("BANK", B, TR)], [], 3000)
    schedule()
    for s in sorted(count):
        g.wait_ge(T.sem[s], count[s])
